import numpy as np
import ml_dtypes


def mxq(x, axis, fmt="e4m3"):
    dtype, down = {"e4m3": (ml_dtypes.float8_e4m3fn, 7), "e5m2": (ml_dtypes.float8_e5m2, 14)}[fmt]
    v = np.moveaxis(np.asarray(x, np.float32).astype(ml_dtypes.bfloat16).astype(np.float64), axis, -1)
    blocks = v.reshape(v.shape[:-1] + (-1, 32))
    amax = np.abs(blocks).max(-1, keepdims=True)
    byte = np.maximum(np.where(amax > 0, np.frexp(amax)[1] - 1 + 127, 0) - down, 1)
    scale = np.exp2(byte - 127.0)
    codes = (blocks / scale).astype(np.float32).astype(dtype).astype(np.float64)
    return np.moveaxis((codes * scale).reshape(v.shape), -1, axis)


WIDE = False


def mx_kscale(k):
    if not WIDE:
        return np.ones(k)
    levels = np.array([10, -10, 5, -5, 0])
    if k % 512:
        return np.exp2(np.random.permutation(np.resize(levels, k // 32))).repeat(32)
    a = np.empty((k // 512, 16))
    for p in range(k // 512):
        a[p, :8] = np.random.permutation(np.resize(levels, 8))
        for g in range(8):
            far = levels[np.abs(levels - a[p, g]) >= 10]
            a[p, g + 8] = far[np.random.randint(len(far))]
    return np.exp2(a.ravel()).repeat(32)


def f64(x):
    return np.asarray(x).astype(np.float64)


def striped(idx):
    return np.tile(idx.reshape(-1, 16).T, (8, 1)).astype(np.uint16)


def unstriped(offs):
    return offs[:16].T.reshape(-1).astype(np.int64)


E2M1 = np.array([0.0, 0.5, 1.0, 1.5, 2.0, 3.0, 4.0, 6.0, -0.0, -0.5, -1.0, -1.5, -2.0, -3.0, -4.0, -6.0])


def pack_weight(w, fmt):
    k, n = w.shape
    w = f64(np.asarray(w, np.float32).astype(ml_dtypes.bfloat16)).reshape(k // 32, 32, n)
    amax = np.abs(w).max(1)
    if fmt == "e4m3":
        byte = np.frexp(amax)[1] - 1 + 127 - 7
    else:
        mant, ex = np.frexp(amax / 6.0)
        byte = np.where(mant > 0.5, ex, ex - 1) + 127
    byte = np.clip(np.where(amax > 0, byte, 1), 1, 254)
    scaled = (w * np.exp2(127.0 - byte)[:, None, :]).reshape(k, n).astype(np.float32)
    by_word = np.ascontiguousarray(scaled.reshape(k // 512, 128, 4, n).transpose(0, 1, 3, 2))
    if fmt == "e4m3":
        words = by_word.astype(ml_dtypes.float8_e4m3fn).view(np.uint8)
    else:
        c = by_word.astype(ml_dtypes.float4_e2m1fn).view(np.uint8) & 0xF
        words = (c[..., 0::2] | (c[..., 1::2] << 4)).reshape(k // 512, 128, 2 * n)
    return np.ascontiguousarray(words), np.ascontiguousarray(byte.astype(np.uint8).reshape(k // 512, 16, n))


def unpack_weight(words, scales, fmt):
    g, _, n = scales.shape
    words = np.ascontiguousarray(words).reshape(g, 128, n, -1)
    if fmt == "e4m3":
        vals = words.view(ml_dtypes.float8_e4m3fn).astype(np.float64)
    else:
        nib = np.empty((g, 128, n, 4), np.uint8)
        nib[..., 0::2] = words & 0xF
        nib[..., 1::2] = words >> 4
        vals = E2M1[nib]
    vals = vals * np.repeat(np.exp2(scales.astype(np.float64) - 127.0), 8, axis=1)[..., None]
    return vals.transpose(0, 1, 3, 2).reshape(g * 512, n)


def relu(v):
    return np.maximum(v, 0.0)


K, T, E, C, H, N = 1536, 768, 6, 256, 512, 128


def by_expert(wq, xq):
    return np.concatenate([wq[e].T @ xq[:, e * C:(e + 1) * C] for e in range(E)], axis=1)


def setup_inputs():
    n = np.random.standard_normal
    s = mx_kscale(K)
    u = mx_kscale(H)
    first = np.random.permutation(np.repeat(np.arange(E), T // E))
    second = (first + 1 + np.random.permutation(np.repeat(np.arange(E - 1), -(-T // (E - 1)))[:T])) % E
    while np.bincount(second, minlength=E).max() != T // E:
        load = np.bincount(second, minlength=E); hi, lo = int(load.argmax()), int(load.argmin())
        t = np.flatnonzero((second == hi) & (first != lo))[0]; second[t] = lo
    slot_token = np.empty(E * C, np.int64); pos = np.empty((2, T), np.int64); fill = np.zeros(E, np.int64)
    place = np.stack([np.random.permutation(C) for _ in range(E)])
    for r, deal in enumerate((first, second)):
        for t in np.random.permutation(T):
            e = deal[t]; j = e * C + place[e, fill[e]]; fill[e] += 1; slot_token[j] = t; pos[r, t] = j
    g = np.random.uniform(0.2, 0.8, T)
    x = pack_weight(n((K, T)) * s[:, None], "e4m3")
    w1 = [pack_weight(m, "e2m1") for m in n((E, K, H)) / np.sqrt(K) / s[None, :, None] * u]
    w2 = pack_weight(n((H, N)) / np.sqrt(H) / u[:, None], "e4m3")
    return {
        "x_words": x[0],
        "x_scales": x[1],
        "w1_words": np.stack([m[0] for m in w1]),
        "w1_scales": np.stack([m[1] for m in w1]),
        "w2_words": w2[0],
        "w2_scales": w2[1],
        "gate": np.stack([np.tile(g, (128, 1)), np.tile(1.0 - g, (128, 1))]).astype(np.float32),
        "offs": striped(slot_token),
        "pos1": striped(pos[0]),
        "pos2": striped(pos[1]),
    }


def reference(x_words, x_scales, w1_words, w1_scales, w2_words, w2_scales, gate, offs, pos1, pos2):
    w1 = np.stack([unpack_weight(w1_words[e], w1_scales[e], "e2m1") for e in range(E)])
    w2 = unpack_weight(w2_words, w2_scales, "e4m3")
    idx = unstriped(offs)
    xq = unpack_weight(x_words, x_scales, "e4m3")[:, idx]
    h = relu(by_expert(w1, xq))
    c = sum(f64(gate[r, :1]) * h[:, unstriped(p)] for r, p in enumerate((pos1, pos2)))
    return w2.T @ mxq(c, 0, "e4m3")

@@ -1,0 +1,180 @@
+from contextlib import ExitStack
+
+import concourse.mybir as mybir
+from concourse.masks import make_identity
+
+K, T, E, C, H, N = 1536, 768, 6, 256, 512, 128
+S = E * C
+FLOPS = 2 * K * H * S + 2 * H * N * T
+
+F32 = mybir.dt.float32
+BF16 = mybir.dt.bfloat16
+I32 = mybir.dt.int32
+U32 = mybir.dt.uint32
+U16 = mybir.dt.uint16
+U8 = mybir.dt.uint8
+FP8X4 = mybir.dt.float8_e4m3fn_x4
+FP4X4 = mybir.dt.float4_e2m1fn_x4
+MULT = mybir.AluOpType.mult
+RELU = mybir.ActivationFunctionType.Relu
+
+P = 128
+PASSES = K // 512
+PLANES = H // P
+SCALE_WINDOW = 2048
+SLOT_CHUNKS = [(0, 512), (512, 512), (1024, 256), (1280, 256)]
+TOKEN_CHUNKS = [(0, 256), (256, 256), (512, 128), (640, 128)]
+
+
+def tile_moe_sdn_lin_relu_kernel(
+    tc, x_words, x_scales, w1_words, w1_scales, w2_words, w2_scales, gate, offs, pos1, pos2, out
+):
+    nc = tc.nc
+    with ExitStack() as ctx:
+        lists = ctx.enter_context(tc.tile_pool(name="lists", bufs=1))
+        keep = ctx.enter_context(tc.tile_pool(name="keep", bufs=1))
+        psum = ctx.enter_context(tc.psum_pool(name="psum", bufs=1))
+
+        offs_sb = lists.tile([P, S // 16], U16, name="offs_sb")
+        pos_sb = [lists.tile([P, T // 16], U16, name="pos%d_sb" % r) for r in range(2)]
+
+        x_scale_win = keep.tile([P, SCALE_WINDOW], U8, name="x_scale_win", align_bytes=64)
+        w1_scale = keep.tile([P, E * PASSES, H], U8, name="w1_scale", align_bytes=64)
+        w2_scale = keep.tile([P, N], U8, name="w2_scale", align_bytes=64)
+        slot_scale = [keep.tile([P, S], U8, name="slot_scale%d" % s, align_bytes=64) for s in range(PASSES)]
+        win_i = x_scale_win[:].bitcast(I32)
+        nc.gpsimd.memset(win_i[:, : T // 4], 0)
+        nc.gpsimd.memset(w1_scale[:].rearrange("p g n -> p (g n)").bitcast(I32), 0)
+        nc.vector.memset(win_i[:, T // 4 :], 0)
+        nc.vector.memset(w2_scale[:].bitcast(I32), 0)
+        for s in range(1, PASSES):
+            nc.vector.memset(slot_scale[s][96:, :].bitcast(I32), 0)
+
+        nc.sync.dma_start(offs_sb[:], offs)
+        x_win = keep.tile([P, PASSES, T], I32, name="x_win", align_bytes=64)
+        x_words_i = x_words.rearrange("s p t d -> p s (t d)").bitcast(I32)
+        nc.sync.dma_start(x_win[:, :1, :], x_words_i[:, :1, :])
+        nc.sync.dma_start(x_win[:, 1:, :], x_words_i[:, 1:, :])
+
+        x_scales_i = x_scales.bitcast(I32)
+        for q in range(4):
+            nc.scalar.dma_start(win_i[32 * q : 32 * q + 4 * PASSES, : T // 4], x_scales_i[:, 4 * q : 4 * q + 4, :])
+
+        w1_sb = keep.tile([P, E * PASSES, 2 * H], U8, name="w1_sb", align_bytes=64)
+        nc.sync.dma_start(w1_sb[:].bitcast(I32), w1_words.bitcast(I32).rearrange("e s p n -> p (e s) n"))
+        for r, pos in enumerate((pos1, pos2)):
+            nc.sync.dma_start(pos_sb[r][:], pos)
+
+        w1_scales_i = w1_scales.bitcast(I32).rearrange("e s b n -> b (e s) n")
+        for q in range(4):
+            nc.gpsimd.dma_start(w1_scale[32 * q : 32 * q + 4, :, :].bitcast(I32), w1_scales_i[4 * q : 4 * q + 4])
+        gate_sb = keep.tile([P, 2, T], F32, name="gate_sb")
+        nc.gpsimd.dma_start(gate_sb[:], gate.rearrange("r p t -> p r t"))
+        w2_sb = keep.tile([P, N], I32, name="w2_sb", align_bytes=64)
+        nc.gpsimd.dma_start(w2_sb[:], w2_words[0].rearrange("p n d -> p (n d)").bitcast(I32))
+        w2_scales_i = w2_scales.bitcast(I32)
+        for q in range(4):
+            nc.gpsimd.dma_start(w2_scale[32 * q : 32 * q + 4, :].bitcast(I32), w2_scales_i[0, 4 * q : 4 * q + 4, :])
+
+        ident = keep.tile([P, P], F32, name="ident")
+        make_identity(nc, ident[:])
+
+        slot_words = {}
+
+        def gather_words(c, s):
+            first, n = SLOT_CHUNKS[c]
+            g = keep.tile([P, n], U32, name="slot_words%d_%d" % (c, s), align_bytes=64)
+            offsets = offs_sb[:, first // 16 : (first + n) // 16]
+            nc.vector.tensor_copy(g[:], x_win[:, s, :].bitcast(U32).indirect(offsets))
+            slot_words[c, s] = g
+
+        gather_words(0, 0)
+        gather_words(0, 1)
+        nc.vector.tensor_copy(slot_scale[0][:], x_scale_win[:].indirect(offs_sb[:]))
+        for s in range(1, PASSES):
+            nc.scalar.dma_start(
+                slot_scale[s][:112, :].bitcast(I32), slot_scale[0][4 * s : 4 * s + 112, :].bitcast(I32)
+            )
+        gather_words(0, 2)
+        for c in range(1, len(SLOT_CHUNKS)):
+            for s in range(PASSES):
+                gather_words(c, s)
+
+        hidden = [keep.tile([P, S], F32, name="hidden%d" % j) for j in range(PLANES)]
+        early = [(0, 0), (0, 1), (0, 2), (0, 3), (1, 0), (1, 1), (0, 4), (1, 2), (0, 5)]
+        order = early + [(j, e) for j in range(PLANES) for e in range(E) if (j, e) not in early]
+        for j, e in order:
+            if True:
+                acc = psum.tile([P, C], F32, name="acc", tag="acc%d" % (j % 2), bufs=2)
+                c = [i for i, (first, n) in enumerate(SLOT_CHUNKS) if first <= e * C < first + n][0]
+                for half in range(C // P):
+                    slot = e * C + half * P
+                    col = slot - SLOT_CHUNKS[c][0]
+                    for s in range(PASSES):
+                        nc.tensor.matmul_mx(
+                            out=acc[:, half * P : (half + 1) * P],
+                            lhsT=w1_sb[:, e * PASSES + s, 2 * P * j : 2 * P * (j + 1)].bitcast(FP4X4),
+                            lhsT_scale=w1_scale[:, e * PASSES + s, P * j : P * (j + 1)],
+                            rhs=slot_words[c, s][:, col : col + P].bitcast(FP8X4),
+                            rhs_scale=slot_scale[s][:, slot : slot + P],
+                            start=(s == 0),
+                            stop=(s == PASSES - 1),
+                        )
+                nc.scalar.activation(hidden[j][:, e * C : (e + 1) * C], acc[:], RELU)
+
+        c_tok = keep.tile([P, T // P, H], BF16, name="c_tok", align_bytes=64)
+
+        def gather_products(j, first, n):
+            prods = []
+            for r in range(2):
+                prod = keep.tile([P, n], F32, name="prod%d_%d_%d" % (j, first, r))
+                offsets = pos_sb[r][:, first // 16 : (first + n) // 16]
+                nc.vector.tensor_tensor(prod[:], hidden[j][:].indirect(offsets), gate_sb[:, r, first : first + n], MULT)
+                prods.append(prod)
+            return prods
+
+        def add_turned(j, prods, col, first_block, blocks):
+            bank = psum.tile([P, blocks, P], F32, name="turned", tag="turned", bufs=2)
+            for b in range(blocks):
+                cols = slice(col + b * P, col + (b + 1) * P)
+                for r in range(2):
+                    nc.tensor.matmul(
+                        bank[:, b, :], prods[r][:, cols], ident[:], start=(r == 0), stop=(r == 1), is_transpose=True
+                    )
+            nc.scalar.copy(c_tok[:, first_block : first_block + blocks, P * j : P * (j + 1)], bank[:])
+
+        for j in range(PLANES - 1):
+            prods = gather_products(j, 0, T)
+            for first_block in (0, 3):
+                add_turned(j, prods, first_block * P, first_block, 3)
+
+        last_prods = [gather_products(PLANES - 1, first, n) for first, n in TOKEN_CHUNKS]
+        for (first, n), prods in zip(TOKEN_CHUNKS, last_prods):
+            blocks = n // P
+            add_turned(PLANES - 1, prods, 0, first // P, blocks)
+            back = psum.tile([P, blocks, 2, P], F32, name="back", tag="back", bufs=1)
+            for b in range(blocks):
+                pairs = c_tok[:, first // P + b, :].bitcast(F32)
+                for u in range(2):
+                    nc.tensor.transpose(back[:, b, u, :], pairs[:, u : H // 2 : 2], ident[:])
+            grouped = keep.tile([P, 4 * n], BF16, name="grouped%d" % first, align_bytes=64)
+            nc.scalar.copy(
+                grouped[:].bitcast(F32).rearrange("p (b t u) -> p b t u", b=blocks, u=2),
+                back[:].rearrange("p b u t -> p b t u"),
+            )
+            c_words = keep.tile([P, n], U32, name="c_words%d" % first, align_bytes=64)
+            c_scale = keep.tile([P, n], U8, name="c_scale%d" % first, align_bytes=64)
+            nc.vector.quantize_mx(out=c_words[:].bitcast(FP8X4), scales=c_scale[:], in_=grouped[:])
+            res_ps = psum.tile([P, n], F32, name="res_ps", tag="res_ps", bufs=1)
+            nc.tensor.matmul_mx(
+                out=res_ps[:],
+                lhsT=w2_sb[:].bitcast(FP8X4),
+                lhsT_scale=w2_scale[:],
+                rhs=c_words[:].bitcast(FP8X4),
+                rhs_scale=c_scale[:],
+                start=True,
+                stop=True,
+            )
+            res = keep.tile([P, n], F32, name="res%d" % first)
+            nc.scalar.copy(res[:], res_ps[:])
+            nc.sync.dma_start(out[:, first : first + n], res[:])

@@ -22,8 +22,11 @@ P = 128
 PASSES = K // 512
 PLANES = H // P
 SCALE_WINDOW = 2048
-SLOT_CHUNKS = [(0, 512), (512, 512), (1024, 256), (1280, 256)]
-TOKEN_CHUNKS = [(0, 256), (256, 256), (512, 128), (640, 128)]
+FIRST_GATHER = (0, 0, 512)
+LATER_GATHERS = [
+    (1, 0, 512), (2, 0, 512), (0, 512, 512), (1, 512, 512), (2, 512, 512),
+    (0, 1024, 512), (1, 1024, 512), (2, 1024, 256), (2, 1280, 256),
+]
 
 
 def tile_moe_sdn_lin_relu_kernel(
@@ -38,143 +41,174 @@ def tile_moe_sdn_lin_relu_kernel(
         offs_sb = lists.tile([P, S // 16], U16, name="offs_sb")
         pos_sb = [lists.tile([P, T // 16], U16, name="pos%d_sb" % r) for r in range(2)]
 
-        x_scale_win = keep.tile([P, SCALE_WINDOW], U8, name="x_scale_win", align_bytes=64)
+        x_scale_win = keep.tile([P, SCALE_WINDOW], U8, name="x_scale_win", tag="x_scale_win", align_bytes=64)
         w1_scale = keep.tile([P, E * PASSES, H], U8, name="w1_scale", align_bytes=64)
-        w2_scale = keep.tile([P, N], U8, name="w2_scale", align_bytes=64)
         slot_scale = [keep.tile([P, S], U8, name="slot_scale%d" % s, align_bytes=64) for s in range(PASSES)]
         win_i = x_scale_win[:].bitcast(I32)
         nc.gpsimd.memset(win_i[:, : T // 4], 0)
-        nc.gpsimd.memset(w1_scale[:].rearrange("p g n -> p (g n)").bitcast(I32), 0)
+        nc.vector.memset(w1_scale[:].rearrange("p g n -> p (g n)").bitcast(I32), 0)
         nc.vector.memset(win_i[:, T // 4 :], 0)
-        nc.vector.memset(w2_scale[:].bitcast(I32), 0)
         for s in range(1, PASSES):
             nc.vector.memset(slot_scale[s][96:, :].bitcast(I32), 0)
 
         nc.sync.dma_start(offs_sb[:], offs)
-        x_win = keep.tile([P, PASSES, T], I32, name="x_win", align_bytes=64)
         x_words_i = x_words.rearrange("s p t d -> p s (t d)").bitcast(I32)
-        nc.sync.dma_start(x_win[:, :1, :], x_words_i[:, :1, :])
-        nc.sync.dma_start(x_win[:, 1:, :], x_words_i[:, 1:, :])
-
+        x_first = keep.tile([P, T], I32, name="x_first", tag="reused0", align_bytes=64)
+        nc.sync.dma_start(x_first[:], x_words_i[:, 0, :])
         x_scales_i = x_scales.bitcast(I32)
         for q in range(4):
-            nc.scalar.dma_start(win_i[32 * q : 32 * q + 4 * PASSES, : T // 4], x_scales_i[:, 4 * q : 4 * q + 4, :])
-
-        w1_sb = keep.tile([P, E * PASSES, 2 * H], U8, name="w1_sb", align_bytes=64)
-        nc.sync.dma_start(w1_sb[:].bitcast(I32), w1_words.bitcast(I32).rearrange("e s p n -> p (e s) n"))
+            queue = nc.sync if q < 2 else nc.scalar
+            queue.dma_start(win_i[32 * q : 32 * q + 4 * PASSES, : T // 4], x_scales_i[:, 4 * q : 4 * q + 4, :])
+        x_rest = keep.tile([P, PASSES - 1, T], I32, name="x_rest", tag="reused1", align_bytes=64)
+        nc.sync.dma_start(x_rest[:], x_words_i[:, 1:, :])
+        x_win = [x_first[:]] + [x_rest[:, s, :] for s in range(PASSES - 1)]
         for r, pos in enumerate((pos1, pos2)):
             nc.sync.dma_start(pos_sb[r][:], pos)
+        w1_sb = keep.tile([P, E * PASSES, 2 * H], U8, name="w1_sb", align_bytes=64)
+        w1_words_i = w1_words.bitcast(I32).rearrange("e s p n -> p (e s) n")
+        for groups in (slice(0, 2 * PASSES), slice(2 * PASSES, E * PASSES)):
+            nc.sync.dma_start(w1_sb[:, groups, :].bitcast(I32), w1_words_i[:, groups, :])
+        gate_sb = keep.tile([P, 2, T], F32, name="gate_sb")
+        nc.sync.dma_start(gate_sb[:], gate.rearrange("r p t -> p r t"))
 
         w1_scales_i = w1_scales.bitcast(I32).rearrange("e s b n -> b (e s) n")
         for q in range(4):
-            nc.gpsimd.dma_start(w1_scale[32 * q : 32 * q + 4, :, :].bitcast(I32), w1_scales_i[4 * q : 4 * q + 4])
-        gate_sb = keep.tile([P, 2, T], F32, name="gate_sb")
-        nc.gpsimd.dma_start(gate_sb[:], gate.rearrange("r p t -> p r t"))
-        w2_sb = keep.tile([P, N], I32, name="w2_sb", align_bytes=64)
-        nc.gpsimd.dma_start(w2_sb[:], w2_words[0].rearrange("p n d -> p (n d)").bitcast(I32))
-        w2_scales_i = w2_scales.bitcast(I32)
-        for q in range(4):
-            nc.gpsimd.dma_start(w2_scale[32 * q : 32 * q + 4, :].bitcast(I32), w2_scales_i[0, 4 * q : 4 * q + 4, :])
+            nc.scalar.dma_start(w1_scale[32 * q : 32 * q + 4, :, :].bitcast(I32), w1_scales_i[4 * q : 4 * q + 4])
 
         ident = keep.tile([P, P], F32, name="ident")
         make_identity(nc, ident[:])
 
         slot_words = {}
 
-        def gather_words(c, s):
-            first, n = SLOT_CHUNKS[c]
-            g = keep.tile([P, n], U32, name="slot_words%d_%d" % (c, s), align_bytes=64)
+        def gather_words(g, s, first, n):
             offsets = offs_sb[:, first // 16 : (first + n) // 16]
-            nc.vector.tensor_copy(g[:], x_win[:, s, :].bitcast(U32).indirect(offsets))
-            slot_words[c, s] = g
+            nc.vector.tensor_copy(g, x_win[s].bitcast(U32).indirect(offsets))
+            for col in range(0, n, P):
+                slot_words[s, first + col] = g[:, col : col + P]
 
-        gather_words(0, 0)
-        gather_words(0, 1)
+        first_words = keep.tile([P, FIRST_GATHER[2]], U32, name="first_words", align_bytes=64)
+        gather_words(first_words[:], *FIRST_GATHER)
         nc.vector.tensor_copy(slot_scale[0][:], x_scale_win[:].indirect(offs_sb[:]))
         for s in range(1, PASSES):
             nc.scalar.dma_start(
                 slot_scale[s][:112, :].bitcast(I32), slot_scale[0][4 * s : 4 * s + 112, :].bitcast(I32)
             )
-        gather_words(0, 2)
-        for c in range(1, len(SLOT_CHUNKS)):
-            for s in range(PASSES):
-                gather_words(c, s)
+        later_words = keep.tile(
+            [P, PASSES * S - FIRST_GATHER[2]], U32, name="later_words", tag="x_scale_win", align_bytes=64
+        )
+        col = 0
+        for s, first, n in LATER_GATHERS:
+            gather_words(later_words[:, col : col + n], s, first, n)
+            col += n
+
+        w2_scale = keep.tile([P, N], U8, name="w2_scale", tag="reused1", align_bytes=64)
+        nc.vector.memset(w2_scale[:].bitcast(I32), 0)
+        w2_scales_i = w2_scales.bitcast(I32)
+        for q in range(4):
+            nc.sync.dma_start(w2_scale[32 * q : 32 * q + 4, :].bitcast(I32), w2_scales_i[0, 4 * q : 4 * q + 4, :])
+        w2_sb = keep.tile([P, N], I32, name="w2_sb", tag="reused0", align_bytes=64)
+        nc.sync.dma_start(w2_sb[:], w2_words[0].rearrange("p n d -> p (n d)").bitcast(I32))
 
         hidden = [keep.tile([P, S], F32, name="hidden%d" % j) for j in range(PLANES)]
-        early = [(0, 0), (0, 1), (0, 2), (0, 3), (1, 0), (1, 1), (0, 4), (1, 2), (0, 5)]
+        early = [(0, 0), (0, 1), (1, 0), (1, 1), (2, 0), (0, 2), (0, 3), (1, 2), (1, 3), (0, 4), (0, 5)]
         order = early + [(j, e) for j in range(PLANES) for e in range(E) if (j, e) not in early]
         for j, e in order:
-            if True:
-                acc = psum.tile([P, C], F32, name="acc", tag="acc%d" % (j % 2), bufs=2)
-                c = [i for i, (first, n) in enumerate(SLOT_CHUNKS) if first <= e * C < first + n][0]
-                for half in range(C // P):
-                    slot = e * C + half * P
-                    col = slot - SLOT_CHUNKS[c][0]
-                    for s in range(PASSES):
-                        nc.tensor.matmul_mx(
-                            out=acc[:, half * P : (half + 1) * P],
-                            lhsT=w1_sb[:, e * PASSES + s, 2 * P * j : 2 * P * (j + 1)].bitcast(FP4X4),
-                            lhsT_scale=w1_scale[:, e * PASSES + s, P * j : P * (j + 1)],
-                            rhs=slot_words[c, s][:, col : col + P].bitcast(FP8X4),
-                            rhs_scale=slot_scale[s][:, slot : slot + P],
-                            start=(s == 0),
-                            stop=(s == PASSES - 1),
-                        )
-                nc.scalar.activation(hidden[j][:, e * C : (e + 1) * C], acc[:], RELU)
+            acc = psum.tile([P, C], F32, name="acc", tag="work", bufs=4)
+            for half in range(C // P):
+                slot = e * C + half * P
+                for s in range(PASSES):
+                    nc.tensor.matmul_mx(
+                        out=acc[:, half * P : (half + 1) * P],
+                        lhsT=w1_sb[:, e * PASSES + s, 2 * P * j : 2 * P * (j + 1)].bitcast(FP4X4),
+                        lhsT_scale=w1_scale[:, e * PASSES + s, P * j : P * (j + 1)],
+                        rhs=slot_words[s, slot].bitcast(FP8X4),
+                        rhs_scale=slot_scale[s][:, slot : slot + P],
+                        start=(s == 0),
+                        stop=(s == PASSES - 1),
+                    )
+            nc.scalar.activation(hidden[j][:, e * C : (e + 1) * C], acc[:], RELU)
 
         c_tok = keep.tile([P, T // P, H], BF16, name="c_tok", align_bytes=64)
+        grouped = keep.tile([P, 4 * T], BF16, name="grouped", align_bytes=64)
+        c_words = keep.tile([P, T], U32, name="c_words", align_bytes=64)
+        c_scale = keep.tile([P, T], U8, name="c_scale", align_bytes=64)
+        res = keep.tile([P, T], F32, name="res")
+        prods = [[keep.tile([P, T], F32, name="prod%d_%d" % (j, r)) for r in range(2)] for j in range(PLANES)]
 
         def gather_products(j, first, n):
-            prods = []
             for r in range(2):
-                prod = keep.tile([P, n], F32, name="prod%d_%d_%d" % (j, first, r))
                 offsets = pos_sb[r][:, first // 16 : (first + n) // 16]
-                nc.vector.tensor_tensor(prod[:], hidden[j][:].indirect(offsets), gate_sb[:, r, first : first + n], MULT)
-                prods.append(prod)
-            return prods
+                cols = slice(first, first + n)
+                nc.vector.tensor_tensor(prods[j][r][:, cols], hidden[j][:].indirect(offsets), gate_sb[:, r, cols], MULT)
 
-        def add_turned(j, prods, col, first_block, blocks):
-            bank = psum.tile([P, blocks, P], F32, name="turned", tag="turned", bufs=2)
-            for b in range(blocks):
-                cols = slice(col + b * P, col + (b + 1) * P)
+        def add_turned(j, first, n, copy):
+            bank = psum.tile([P, n // P, P], F32, name="turned", tag="work", bufs=4)
+            for b in range(n // P):
+                cols = slice(first + b * P, first + (b + 1) * P)
                 for r in range(2):
                     nc.tensor.matmul(
-                        bank[:, b, :], prods[r][:, cols], ident[:], start=(r == 0), stop=(r == 1), is_transpose=True
+                        bank[:, b, :], prods[j][r][:, cols], ident[:], start=(r == 0), stop=(r == 1), is_transpose=True
                     )
-            nc.scalar.copy(c_tok[:, first_block : first_block + blocks, P * j : P * (j + 1)], bank[:])
+            copy(c_tok[:, first // P : (first + n) // P, P * j : P * (j + 1)], bank[:])
 
-        for j in range(PLANES - 1):
-            prods = gather_products(j, 0, T)
-            for first_block in (0, 3):
-                add_turned(j, prods, first_block * P, first_block, 3)
-
-        last_prods = [gather_products(PLANES - 1, first, n) for first, n in TOKEN_CHUNKS]
-        for (first, n), prods in zip(TOKEN_CHUNKS, last_prods):
-            blocks = n // P
-            add_turned(PLANES - 1, prods, 0, first // P, blocks)
-            back = psum.tile([P, blocks, 2, P], F32, name="back", tag="back", bufs=1)
-            for b in range(blocks):
+        def turn_back(first, n, copy):
+            bank = psum.tile([P, n // P, 2, P], F32, name="back", tag="work", bufs=4)
+            for b in range(n // P):
                 pairs = c_tok[:, first // P + b, :].bitcast(F32)
                 for u in range(2):
-                    nc.tensor.transpose(back[:, b, u, :], pairs[:, u : H // 2 : 2], ident[:])
-            grouped = keep.tile([P, 4 * n], BF16, name="grouped%d" % first, align_bytes=64)
-            nc.scalar.copy(
-                grouped[:].bitcast(F32).rearrange("p (b t u) -> p b t u", b=blocks, u=2),
-                back[:].rearrange("p b u t -> p b t u"),
+                    nc.tensor.transpose(bank[:, b, u, :], pairs[:, u : H // 2 : 2], ident[:])
+            copy(
+                grouped[:, 4 * first : 4 * (first + n)].bitcast(F32).rearrange("p (b t u) -> p b t u", t=P, u=2),
+                bank[:].rearrange("p b u t -> p b t u"),
             )
-            c_words = keep.tile([P, n], U32, name="c_words%d" % first, align_bytes=64)
-            c_scale = keep.tile([P, n], U8, name="c_scale%d" % first, align_bytes=64)
-            nc.vector.quantize_mx(out=c_words[:].bitcast(FP8X4), scales=c_scale[:], in_=grouped[:])
-            res_ps = psum.tile([P, n], F32, name="res_ps", tag="res_ps", bufs=1)
+
+        def quantize(first, n):
+            cols = slice(first, first + n)
+            nc.vector.quantize_mx(
+                out=c_words[:, cols].bitcast(FP8X4), scales=c_scale[:, cols], in_=grouped[:, 4 * first : 4 * (first + n)]
+            )
+
+        def project(first, n, copy):
+            cols = slice(first, first + n)
+            bank = psum.tile([P, n], F32, name="projected", tag="projected", bufs=3)
             nc.tensor.matmul_mx(
-                out=res_ps[:],
+                out=bank[:],
                 lhsT=w2_sb[:].bitcast(FP8X4),
                 lhsT_scale=w2_scale[:],
-                rhs=c_words[:].bitcast(FP8X4),
-                rhs_scale=c_scale[:],
+                rhs=c_words[:, cols].bitcast(FP8X4),
+                rhs_scale=c_scale[:, cols],
                 start=True,
                 stop=True,
             )
-            res = keep.tile([P, n], F32, name="res%d" % first)
-            nc.scalar.copy(res[:], res_ps[:])
-            nc.sync.dma_start(out[:, first : first + n], res[:])
+            copy(res[:, cols], bank[:])
+            nc.sync.dma_start(out[:, cols], res[:, cols])
+
+        on_scalar, on_vector = nc.scalar.copy, nc.vector.tensor_copy
+        chunks = [(0, 256), (256, 256), (512, 128), (640, 128)]
+        for j in range(2):
+            gather_products(j, 0, T)
+        for first, n in chunks:
+            for j in (2, 3):
+                gather_products(j, first, n)
+        for j in range(2):
+            for first in (0, T // 2):
+                add_turned(j, first, T // 2, on_scalar)
+        a, b, c, d = chunks
+        add_turned(2, *a, on_scalar)
+        add_turned(3, *a, on_scalar)
+        add_turned(2, *b, on_scalar)
+        turn_back(*a, on_scalar)
+        add_turned(3, *b, on_scalar)
+        add_turned(2, *c, on_scalar)
+        turn_back(*b, on_scalar)
+        add_turned(3, *c, on_scalar)
+        add_turned(2, *d, on_scalar)
+        turn_back(*c, on_scalar)
+        quantize(0, 512)
+        add_turned(3, *d, on_vector)
+        quantize(*c)
+        turn_back(*d, on_vector)
+        quantize(*d)
+        project(0, 512, on_scalar)
+        project(*c, on_scalar)
+        project(*d, on_vector)

@@ -24,8 +24,8 @@ PLANES = H // P
 SCALE_WINDOW = 2048
 FIRST_GATHER = (0, 0, 512)
 LATER_GATHERS = [
-    (1, 0, 512), (2, 0, 512), (0, 512, 512), (1, 512, 512), (2, 512, 512),
-    (0, 1024, 512), (1, 1024, 512), (2, 1024, 256), (2, 1280, 256),
+    (1, 0, 512), (2, 0, 512), (0, 512, 512), (0, 1024, 512),
+    (1, 512, 512), (2, 512, 512), (1, 1024, 512), (2, 1024, 256), (2, 1280, 256),
 ]
 
 
@@ -36,44 +36,45 @@ def tile_moe_sdn_lin_relu_kernel(
     with ExitStack() as ctx:
         lists = ctx.enter_context(tc.tile_pool(name="lists", bufs=1))
         keep = ctx.enter_context(tc.tile_pool(name="keep", bufs=1))
+        shared = ctx.enter_context(tc.tile_pool(name="shared", bufs=1))
         psum = ctx.enter_context(tc.psum_pool(name="psum", bufs=1))
 
         offs_sb = lists.tile([P, S // 16], U16, name="offs_sb")
         pos_sb = [lists.tile([P, T // 16], U16, name="pos%d_sb" % r) for r in range(2)]
 
-        x_scale_win = keep.tile([P, SCALE_WINDOW], U8, name="x_scale_win", tag="x_scale_win", align_bytes=64)
+        x_scale_win = shared.tile([P, SCALE_WINDOW], U8, name="x_scale_win", align_bytes=64, offset=11264)
         w1_scale = keep.tile([P, E * PASSES, H], U8, name="w1_scale", align_bytes=64)
         slot_scale = [keep.tile([P, S], U8, name="slot_scale%d" % s, align_bytes=64) for s in range(PASSES)]
         win_i = x_scale_win[:].bitcast(I32)
         nc.gpsimd.memset(win_i[:, : T // 4], 0)
-        nc.vector.memset(w1_scale[:].rearrange("p g n -> p (g n)").bitcast(I32), 0)
+        w1_scale_i = w1_scale[:].rearrange("p g n -> p (g n)").bitcast(I32)
+        nc.vector.memset(w1_scale_i[:, : 2 * PASSES * H // 4], 0)
         nc.vector.memset(win_i[:, T // 4 :], 0)
-        for s in range(1, PASSES):
-            nc.vector.memset(slot_scale[s][96:, :].bitcast(I32), 0)
+        nc.vector.memset(w1_scale_i[:, 2 * PASSES * H // 4 :], 0)
 
         nc.sync.dma_start(offs_sb[:], offs)
         x_words_i = x_words.rearrange("s p t d -> p s (t d)").bitcast(I32)
         x_first = keep.tile([P, T], I32, name="x_first", tag="reused0", align_bytes=64)
         nc.sync.dma_start(x_first[:], x_words_i[:, 0, :])
         x_scales_i = x_scales.bitcast(I32)
+        for q in range(2):
+            nc.sync.dma_start(win_i[32 * q : 32 * q + 12, : T // 4], x_scales_i[:, 4 * q : 4 * q + 4, :])
+        for q in range(2, 4):
+            nc.scalar.dma_start(win_i[32 * q : 32 * q + 4, : T // 4], x_scales_i[0, 4 * q : 4 * q + 4, :])
+            nc.scalar.dma_start(win_i[32 * q - 8 : 32 * q, : T // 4], x_scales_i[1:, 4 * q : 4 * q + 4, :])
+        w1_scales_i = w1_scales.bitcast(I32).rearrange("e s b n -> b (e s) n")
         for q in range(4):
-            queue = nc.sync if q < 2 else nc.scalar
-            queue.dma_start(win_i[32 * q : 32 * q + 4 * PASSES, : T // 4], x_scales_i[:, 4 * q : 4 * q + 4, :])
+            nc.scalar.dma_start(
+                w1_scale[32 * q : 32 * q + 4, : 2 * PASSES, :].bitcast(I32), w1_scales_i[4 * q : 4 * q + 4, : 2 * PASSES]
+            )
         x_rest = keep.tile([P, PASSES - 1, T], I32, name="x_rest", tag="reused1", align_bytes=64)
         nc.sync.dma_start(x_rest[:], x_words_i[:, 1:, :])
         x_win = [x_first[:]] + [x_rest[:, s, :] for s in range(PASSES - 1)]
+        w1_words_i = w1_words.bitcast(I32).rearrange("e s p n -> p (e s) n")
+        w1_first = keep.tile([P, 2 * PASSES, 2 * H], U8, name="w1_first", align_bytes=64)
+        nc.sync.dma_start(w1_first[:].bitcast(I32), w1_words_i[:, : 2 * PASSES, :])
         for r, pos in enumerate((pos1, pos2)):
             nc.sync.dma_start(pos_sb[r][:], pos)
-        w1_sb = keep.tile([P, E * PASSES, 2 * H], U8, name="w1_sb", align_bytes=64)
-        w1_words_i = w1_words.bitcast(I32).rearrange("e s p n -> p (e s) n")
-        for groups in (slice(0, 2 * PASSES), slice(2 * PASSES, E * PASSES)):
-            nc.sync.dma_start(w1_sb[:, groups, :].bitcast(I32), w1_words_i[:, groups, :])
-        gate_sb = keep.tile([P, 2, T], F32, name="gate_sb")
-        nc.sync.dma_start(gate_sb[:], gate.rearrange("r p t -> p r t"))
-
-        w1_scales_i = w1_scales.bitcast(I32).rearrange("e s b n -> b (e s) n")
-        for q in range(4):
-            nc.scalar.dma_start(w1_scale[32 * q : 32 * q + 4, :, :].bitcast(I32), w1_scales_i[4 * q : 4 * q + 4])
 
         ident = keep.tile([P, P], F32, name="ident")
         make_identity(nc, ident[:])
@@ -90,36 +91,44 @@ def tile_moe_sdn_lin_relu_kernel(
         gather_words(first_words[:], *FIRST_GATHER)
         nc.vector.tensor_copy(slot_scale[0][:], x_scale_win[:].indirect(offs_sb[:]))
         for s in range(1, PASSES):
+            for row, first in ((0, 4 * s), (64, 52 + 4 * s)):
+                nc.scalar.dma_start(
+                    slot_scale[s][row : row + 64, :].bitcast(I32), slot_scale[0][first : first + 64, :].bitcast(I32)
+                )
+        w1_rest = shared.tile([P, 4 * PASSES, 2 * H], U8, name="w1_rest", align_bytes=64, offset=0)
+        w1_sb = [w1_first[:], w1_rest[:, : 2 * PASSES, :], w1_rest[:, 2 * PASSES :, :]]
+        for pair in (1, 2):
+            groups = slice(2 * PASSES * pair, 2 * PASSES * (pair + 1))
+            nc.scalar.dma_start(w1_sb[pair].bitcast(I32), w1_words_i[:, groups, :])
+        for q in range(4):
             nc.scalar.dma_start(
-                slot_scale[s][:112, :].bitcast(I32), slot_scale[0][4 * s : 4 * s + 112, :].bitcast(I32)
+                w1_scale[32 * q : 32 * q + 4, 2 * PASSES :, :].bitcast(I32), w1_scales_i[4 * q : 4 * q + 4, 2 * PASSES :]
             )
-        later_words = keep.tile(
-            [P, PASSES * S - FIRST_GATHER[2]], U32, name="later_words", tag="x_scale_win", align_bytes=64
+        later_words = shared.tile(
+            [P, PASSES * S - FIRST_GATHER[2]], U32, name="later_words", align_bytes=64, offset=12288
         )
         col = 0
         for s, first, n in LATER_GATHERS:
             gather_words(later_words[:, col : col + n], s, first, n)
             col += n
 
+        gate_sb = keep.tile([P, 2, T], F32, name="gate_sb", tag="reused0", align_bytes=64)
+        nc.gpsimd.dma_start(gate_sb[:], gate.rearrange("r p t -> p r t"))
         w2_scale = keep.tile([P, N], U8, name="w2_scale", tag="reused1", align_bytes=64)
         nc.vector.memset(w2_scale[:].bitcast(I32), 0)
         w2_scales_i = w2_scales.bitcast(I32)
         for q in range(4):
-            nc.sync.dma_start(w2_scale[32 * q : 32 * q + 4, :].bitcast(I32), w2_scales_i[0, 4 * q : 4 * q + 4, :])
-        w2_sb = keep.tile([P, N], I32, name="w2_sb", tag="reused0", align_bytes=64)
-        nc.sync.dma_start(w2_sb[:], w2_words[0].rearrange("p n d -> p (n d)").bitcast(I32))
+            nc.gpsimd.dma_start(w2_scale[32 * q : 32 * q + 4, :].bitcast(I32), w2_scales_i[0, 4 * q : 4 * q + 4, :])
 
         hidden = [keep.tile([P, S], F32, name="hidden%d" % j) for j in range(PLANES)]
-        early = [(0, 0), (0, 1), (1, 0), (1, 1), (2, 0), (0, 2), (0, 3), (1, 2), (1, 3), (0, 4), (0, 5)]
-        order = early + [(j, e) for j in range(PLANES) for e in range(E) if (j, e) not in early]
-        for j, e in order:
+        def expert_plane(j, e):
             acc = psum.tile([P, C], F32, name="acc", tag="work", bufs=4)
             for half in range(C // P):
                 slot = e * C + half * P
                 for s in range(PASSES):
                     nc.tensor.matmul_mx(
                         out=acc[:, half * P : (half + 1) * P],
-                        lhsT=w1_sb[:, e * PASSES + s, 2 * P * j : 2 * P * (j + 1)].bitcast(FP4X4),
+                        lhsT=w1_sb[e // 2][:, (e % 2) * PASSES + s, 2 * P * j : 2 * P * (j + 1)].bitcast(FP4X4),
                         lhsT_scale=w1_scale[:, e * PASSES + s, P * j : P * (j + 1)],
                         rhs=slot_words[s, slot].bitcast(FP8X4),
                         rhs_scale=slot_scale[s][:, slot : slot + P],
@@ -128,7 +137,7 @@ def tile_moe_sdn_lin_relu_kernel(
                     )
             nc.scalar.activation(hidden[j][:, e * C : (e + 1) * C], acc[:], RELU)
 
-        c_tok = keep.tile([P, T // P, H], BF16, name="c_tok", align_bytes=64)
+        c_tok = keep.tile([P, T // P, 2, P, 2], BF16, name="c_tok", align_bytes=64)
         grouped = keep.tile([P, 4 * T], BF16, name="grouped", align_bytes=64)
         c_words = keep.tile([P, T], U32, name="c_words", align_bytes=64)
         c_scale = keep.tile([P, T], U8, name="c_scale", align_bytes=64)
@@ -149,14 +158,18 @@ def tile_moe_sdn_lin_relu_kernel(
                     nc.tensor.matmul(
                         bank[:, b, :], prods[j][r][:, cols], ident[:], start=(r == 0), stop=(r == 1), is_transpose=True
                     )
-            copy(c_tok[:, first // P : (first + n) // P, P * j : P * (j + 1)], bank[:])
+            for b in range(n // P):
+                copy(
+                    c_tok[:, first // P + b, :, 32 * j : 32 * (j + 1), :],
+                    bank[:, b, :].rearrange("p (m u v) -> p u m v", u=2, v=2),
+                )
 
         def turn_back(first, n, copy):
             bank = psum.tile([P, n // P, 2, P], F32, name="back", tag="work", bufs=4)
             for b in range(n // P):
-                pairs = c_tok[:, first // P + b, :].bitcast(F32)
                 for u in range(2):
-                    nc.tensor.transpose(bank[:, b, u, :], pairs[:, u : H // 2 : 2], ident[:])
+                    pairs = c_tok[:, first // P + b, u, :, :].rearrange("p m v -> p (m v)").bitcast(F32)
+                    nc.tensor.transpose(bank[:, b, u, :], pairs, ident[:])
             copy(
                 grouped[:, 4 * first : 4 * (first + n)].bitcast(F32).rearrange("p (b t u) -> p b t u", t=P, u=2),
                 bank[:].rearrange("p b u t -> p b t u"),
@@ -184,31 +197,44 @@ def tile_moe_sdn_lin_relu_kernel(
             nc.sync.dma_start(out[:, cols], res[:, cols])
 
         on_scalar, on_vector = nc.scalar.copy, nc.vector.tensor_copy
-        chunks = [(0, 256), (256, 256), (512, 128), (640, 128)]
-        for j in range(2):
-            gather_products(j, 0, T)
-        for first, n in chunks:
-            for j in (2, 3):
-                gather_products(j, first, n)
-        for j in range(2):
-            for first in (0, T // 2):
-                add_turned(j, first, T // 2, on_scalar)
-        a, b, c, d = chunks
-        add_turned(2, *a, on_scalar)
+        for j, e in [(j, e) for j in range(4) for e in range(2)] + [(0, e) for e in range(2, E)] + [(1, e) for e in range(2, E)]:
+            expert_plane(j, e)
+        most, last = (0, T - P), (T - P, P)
+        gather_products(0, *most)
+        gather_products(1, *most)
+        for e in range(2, E):
+            expert_plane(2, e)
+        add_turned(0, 0, 384, on_scalar)
+        expert_plane(3, 2)
+        expert_plane(3, 3)
+        add_turned(0, 384, 256, on_scalar)
+        for e in range(4, E):
+            expert_plane(3, e)
+        w2_sb = shared.tile([P, N], I32, name="w2_sb", align_bytes=64, offset=0)
+        nc.gpsimd.dma_start(w2_sb[:], w2_words[0].rearrange("p n d -> p (n d)").bitcast(I32))
+        a, b, c = (0, 256), (256, 256), (512, 128)
+        gather_products(2, *most)
+        for chunk in (a, b, c):
+            gather_products(3, *chunk)
+        for j in range(PLANES):
+            gather_products(j, *last)
+        for j in (1, 2):
+            add_turned(j, 0, 384, on_scalar)
+            add_turned(j, 384, 256, on_scalar)
         add_turned(3, *a, on_scalar)
-        add_turned(2, *b, on_scalar)
-        turn_back(*a, on_scalar)
         add_turned(3, *b, on_scalar)
-        add_turned(2, *c, on_scalar)
-        turn_back(*b, on_scalar)
+        turn_back(*a, on_scalar)
         add_turned(3, *c, on_scalar)
-        add_turned(2, *d, on_scalar)
+        turn_back(*b, on_scalar)
+        add_turned(0, *last, on_scalar)
         turn_back(*c, on_scalar)
+        add_turned(1, *last, on_scalar)
+        add_turned(2, *last, on_scalar)
         quantize(0, 512)
-        add_turned(3, *d, on_vector)
+        add_turned(3, *last, on_vector)
         quantize(*c)
-        turn_back(*d, on_vector)
-        quantize(*d)
+        turn_back(*last, on_vector)
+        quantize(*last)
         project(0, 512, on_scalar)
         project(*c, on_scalar)
-        project(*d, on_vector)
+        project(*last, on_vector)

@@ -24,8 +24,8 @@ PLANES = H // P
 SCALE_WINDOW = 2048
 FIRST_GATHER = (0, 0, 512)
 LATER_GATHERS = [
-    (1, 0, 512), (2, 0, 512), (0, 512, 512), (0, 1024, 512),
-    (1, 512, 512), (2, 512, 512), (1, 1024, 512), (2, 1024, 256), (2, 1280, 256),
+    (1, 0, 512), (2, 0, 512), (0, 512, 512), (1, 512, 512), (2, 512, 512),
+    (0, 1024, 512), (1, 1024, 512), (2, 1024, 256), (2, 1280, 256),
 ]
 
 
@@ -47,6 +47,8 @@ def tile_moe_sdn_lin_relu_kernel(
         slot_scale = [keep.tile([P, S], U8, name="slot_scale%d" % s, align_bytes=64) for s in range(PASSES)]
         win_i = x_scale_win[:].bitcast(I32)
         nc.gpsimd.memset(win_i[:, : T // 4], 0)
+        zero_in = keep.tile([P, 1], F32, name="zero_in")
+        nc.gpsimd.memset(zero_in[:], 0.0)
         w1_scale_i = w1_scale[:].rearrange("p g n -> p (g n)").bitcast(I32)
         nc.vector.memset(w1_scale_i[:, : 2 * PASSES * H // 4], 0)
         nc.vector.memset(win_i[:, T // 4 :], 0)
@@ -54,7 +56,7 @@ def tile_moe_sdn_lin_relu_kernel(
 
         nc.sync.dma_start(offs_sb[:], offs)
         x_words_i = x_words.rearrange("s p t d -> p s (t d)").bitcast(I32)
-        x_first = keep.tile([P, T], I32, name="x_first", tag="reused0", align_bytes=64)
+        x_first = keep.tile([P, T], I32, name="x_first", align_bytes=64)
         nc.sync.dma_start(x_first[:], x_words_i[:, 0, :])
         x_scales_i = x_scales.bitcast(I32)
         for q in range(2):
@@ -62,12 +64,14 @@ def tile_moe_sdn_lin_relu_kernel(
         for q in range(2, 4):
             nc.scalar.dma_start(win_i[32 * q : 32 * q + 4, : T // 4], x_scales_i[0, 4 * q : 4 * q + 4, :])
             nc.scalar.dma_start(win_i[32 * q - 8 : 32 * q, : T // 4], x_scales_i[1:, 4 * q : 4 * q + 4, :])
+        zero_bias = keep.tile([P, 1], F32, name="zero_bias")
+        nc.scalar.activation(zero_bias[:], zero_in[:], RELU)
         w1_scales_i = w1_scales.bitcast(I32).rearrange("e s b n -> b (e s) n")
         for q in range(4):
             nc.scalar.dma_start(
                 w1_scale[32 * q : 32 * q + 4, : 2 * PASSES, :].bitcast(I32), w1_scales_i[4 * q : 4 * q + 4, : 2 * PASSES]
             )
-        x_rest = keep.tile([P, PASSES - 1, T], I32, name="x_rest", tag="reused1", align_bytes=64)
+        x_rest = keep.tile([P, PASSES - 1, T], I32, name="x_rest", align_bytes=64)
         nc.sync.dma_start(x_rest[:], x_words_i[:, 1:, :])
         x_win = [x_first[:]] + [x_rest[:, s, :] for s in range(PASSES - 1)]
         w1_words_i = w1_words.bitcast(I32).rearrange("e s p n -> p (e s) n")
@@ -76,8 +80,23 @@ def tile_moe_sdn_lin_relu_kernel(
         for r, pos in enumerate((pos1, pos2)):
             nc.sync.dma_start(pos_sb[r][:], pos)
 
+        for q in range(4):
+            nc.sync.dma_start(
+                w1_scale[32 * q : 32 * q + 4, 2 * PASSES :, :].bitcast(I32), w1_scales_i[4 * q : 4 * q + 4, 2 * PASSES :]
+            )
+
         ident = keep.tile([P, P], F32, name="ident")
         make_identity(nc, ident[:])
+
+        gate_sb = keep.tile([P, 2, T], F32, name="gate_sb")
+        nc.sync.dma_start(gate_sb[:], gate.rearrange("r p t -> p r t"))
+        w2_scale = keep.tile([P, N], U8, name="w2_scale", align_bytes=64)
+        nc.gpsimd.memset(w2_scale[:].bitcast(I32), 0)
+        w2_scales_i = w2_scales.bitcast(I32)
+        for q in range(4):
+            nc.sync.dma_start(w2_scale[32 * q : 32 * q + 4, :].bitcast(I32), w2_scales_i[0, 4 * q : 4 * q + 4, :])
+        w2_sb = keep.tile([P, N], I32, name="w2_sb", align_bytes=64)
+        nc.sync.dma_start(w2_sb[:], w2_words[0].rearrange("p n d -> p (n d)").bitcast(I32))
 
         slot_words = {}
 
@@ -100,10 +119,6 @@ def tile_moe_sdn_lin_relu_kernel(
         for pair in (1, 2):
             groups = slice(2 * PASSES * pair, 2 * PASSES * (pair + 1))
             nc.scalar.dma_start(w1_sb[pair].bitcast(I32), w1_words_i[:, groups, :])
-        for q in range(4):
-            nc.scalar.dma_start(
-                w1_scale[32 * q : 32 * q + 4, 2 * PASSES :, :].bitcast(I32), w1_scales_i[4 * q : 4 * q + 4, 2 * PASSES :]
-            )
         later_words = shared.tile(
             [P, PASSES * S - FIRST_GATHER[2]], U32, name="later_words", align_bytes=64, offset=12288
         )
@@ -111,14 +126,6 @@ def tile_moe_sdn_lin_relu_kernel(
         for s, first, n in LATER_GATHERS:
             gather_words(later_words[:, col : col + n], s, first, n)
             col += n
-
-        gate_sb = keep.tile([P, 2, T], F32, name="gate_sb", tag="reused0", align_bytes=64)
-        nc.gpsimd.dma_start(gate_sb[:], gate.rearrange("r p t -> p r t"))
-        w2_scale = keep.tile([P, N], U8, name="w2_scale", tag="reused1", align_bytes=64)
-        nc.vector.memset(w2_scale[:].bitcast(I32), 0)
-        w2_scales_i = w2_scales.bitcast(I32)
-        for q in range(4):
-            nc.gpsimd.dma_start(w2_scale[32 * q : 32 * q + 4, :].bitcast(I32), w2_scales_i[0, 4 * q : 4 * q + 4, :])
 
         hidden = [keep.tile([P, S], F32, name="hidden%d" % j) for j in range(PLANES)]
         def expert_plane(j, e):
@@ -135,7 +142,7 @@ def tile_moe_sdn_lin_relu_kernel(
                         start=(s == 0),
                         stop=(s == PASSES - 1),
                     )
-            nc.scalar.activation(hidden[j][:, e * C : (e + 1) * C], acc[:], RELU)
+            nc.scalar.activation(hidden[j][:, e * C : (e + 1) * C], acc[:], RELU, bias=zero_bias[:])
 
         c_tok = keep.tile([P, T // P, 2, P, 2], BF16, name="c_tok", align_bytes=64)
         grouped = keep.tile([P, 4 * T], BF16, name="grouped", align_bytes=64)
@@ -205,22 +212,21 @@ def tile_moe_sdn_lin_relu_kernel(
         for e in range(2, E):
             expert_plane(2, e)
         add_turned(0, 0, 384, on_scalar)
+        add_turned(0, 384, 256, on_scalar)
         expert_plane(3, 2)
         expert_plane(3, 3)
-        add_turned(0, 384, 256, on_scalar)
-        for e in range(4, E):
-            expert_plane(3, e)
-        w2_sb = shared.tile([P, N], I32, name="w2_sb", align_bytes=64, offset=0)
-        nc.gpsimd.dma_start(w2_sb[:], w2_words[0].rearrange("p n d -> p (n d)").bitcast(I32))
+        add_turned(1, 0, 384, on_scalar)
+        expert_plane(3, 4)
+        expert_plane(3, 5)
+        add_turned(1, 384, 256, on_scalar)
         a, b, c = (0, 256), (256, 256), (512, 128)
         gather_products(2, *most)
         for chunk in (a, b, c):
             gather_products(3, *chunk)
         for j in range(PLANES):
             gather_products(j, *last)
-        for j in (1, 2):
-            add_turned(j, 0, 384, on_scalar)
-            add_turned(j, 384, 256, on_scalar)
+        add_turned(2, 0, 384, on_scalar)
+        add_turned(2, 384, 256, on_scalar)
         add_turned(3, *a, on_scalar)
         add_turned(3, *b, on_scalar)
         turn_back(*a, on_scalar)
@@ -233,7 +239,7 @@ def tile_moe_sdn_lin_relu_kernel(
         quantize(0, 512)
         add_turned(3, *last, on_vector)
         quantize(*c)
-        turn_back(*last, on_vector)
+        turn_back(*last, on_scalar)
         quantize(*last)
         project(0, 512, on_scalar)
         project(*c, on_scalar)

@@ -25,8 +25,9 @@ SCALE_WINDOW = 2048
 FIRST_GATHER = (0, 0, 512)
 LATER_GATHERS = [
     (1, 0, 512), (2, 0, 512), (0, 512, 512), (1, 512, 512), (2, 512, 512),
-    (0, 1024, 512), (1, 1024, 512), (2, 1024, 256), (2, 1280, 256),
+    (0, 1024, 512), (1, 1024, 512), (2, 1024, 256), (2, 1280, 128), (2, 1408, 128),
 ]
+WORK = 5
 
 
 def tile_moe_sdn_lin_relu_kernel(
@@ -42,61 +43,53 @@ def tile_moe_sdn_lin_relu_kernel(
         offs_sb = lists.tile([P, S // 16], U16, name="offs_sb")
         pos_sb = [lists.tile([P, T // 16], U16, name="pos%d_sb" % r) for r in range(2)]
 
-        x_scale_win = shared.tile([P, SCALE_WINDOW], U8, name="x_scale_win", align_bytes=64, offset=11264)
+        x_scale_win = shared.tile([P, SCALE_WINDOW], U8, name="x_scale_win", align_bytes=64, offset=0)
         w1_scale = keep.tile([P, E * PASSES, H], U8, name="w1_scale", align_bytes=64)
-        slot_scale = [keep.tile([P, S], U8, name="slot_scale%d" % s, align_bytes=64) for s in range(PASSES)]
-        win_i = x_scale_win[:].bitcast(I32)
-        nc.gpsimd.memset(win_i[:, : T // 4], 0)
+        gathered_scale = keep.tile([P, S], U8, name="gathered_scale", align_bytes=64)
+        moved_scale = keep.tile([P, PASSES - 1, S], U8, name="moved_scale", align_bytes=64)
+        slot_scale = [gathered_scale[:]] + [moved_scale[:, s, :] for s in range(PASSES - 1)]
+        w2_scale = keep.tile([P, N], U8, name="w2_scale", align_bytes=64)
         zero_in = keep.tile([P, 1], F32, name="zero_in")
-        nc.gpsimd.memset(zero_in[:], 0.0)
-        w1_scale_i = w1_scale[:].rearrange("p g n -> p (g n)").bitcast(I32)
-        nc.vector.memset(w1_scale_i[:, : 2 * PASSES * H // 4], 0)
+        gate_rows = keep.tile([P, P], F32, name="gate_rows")
+        ident = keep.tile([P, P], F32, name="ident")
+        win_i = x_scale_win[:].bitcast(I32)
+        nc.vector.memset(win_i[:, : T // 4], 0)
+        nc.vector.memset(w1_scale[:].rearrange("p g n -> p (g n)").bitcast(I32), 0)
         nc.vector.memset(win_i[:, T // 4 :], 0)
-        nc.vector.memset(w1_scale_i[:, 2 * PASSES * H // 4 :], 0)
+        nc.gpsimd.memset(zero_in[:], 0.0)
+        nc.gpsimd.memset(gate_rows[:], 0.0)
+        make_identity(nc, ident[:])
+        nc.gpsimd.memset(moved_scale[:].rearrange("p s n -> p (s n)").bitcast(I32), 0)
+        nc.gpsimd.memset(w2_scale[:].bitcast(I32), 0)
+
+        x_words_i = x_words.rearrange("s p t d -> p s (t d)").bitcast(I32)
+        w1_words_i = w1_words.bitcast(I32).rearrange("e s p n -> p (e s) n")
+        x_first = keep.tile([P, T], I32, name="x_first", align_bytes=64)
+        x_rest = keep.tile([P, PASSES - 1, T], I32, name="x_rest", align_bytes=64)
+        w1_first = keep.tile([P, 2 * PASSES, 2 * H], U8, name="w1_first", align_bytes=64)
+        w1_rest = keep.tile([P, 4 * PASSES, 2 * H], U8, name="w1_rest", align_bytes=64)
+        zero_bias = keep.tile([P, 1], F32, name="zero_bias")
+        nc.scalar.dma_start(x_first[:], x_words_i[:, 0, :])
+        nc.scalar.dma_start(x_rest[:], x_words_i[:, 1:, :])
+        nc.scalar.activation(zero_bias[:], zero_in[:], RELU)
+        nc.scalar.dma_start(w1_first[:].bitcast(I32), w1_words_i[:, : 2 * PASSES, :])
+        nc.scalar.dma_start(w1_rest[:].bitcast(I32), w1_words_i[:, 2 * PASSES :, :])
+        x_win = [x_first[:]] + [x_rest[:, s, :] for s in range(PASSES - 1)]
+        w1_sb = [w1_first[:], w1_rest[:, : 2 * PASSES, :], w1_rest[:, 2 * PASSES :, :]]
 
         nc.sync.dma_start(offs_sb[:], offs)
-        x_words_i = x_words.rearrange("s p t d -> p s (t d)").bitcast(I32)
-        x_first = keep.tile([P, T], I32, name="x_first", align_bytes=64)
-        nc.sync.dma_start(x_first[:], x_words_i[:, 0, :])
         x_scales_i = x_scales.bitcast(I32)
-        for q in range(2):
-            nc.sync.dma_start(win_i[32 * q : 32 * q + 12, : T // 4], x_scales_i[:, 4 * q : 4 * q + 4, :])
-        for q in range(2, 4):
-            nc.scalar.dma_start(win_i[32 * q : 32 * q + 4, : T // 4], x_scales_i[0, 4 * q : 4 * q + 4, :])
-            nc.scalar.dma_start(win_i[32 * q - 8 : 32 * q, : T // 4], x_scales_i[1:, 4 * q : 4 * q + 4, :])
-        zero_bias = keep.tile([P, 1], F32, name="zero_bias")
-        nc.scalar.activation(zero_bias[:], zero_in[:], RELU)
-        w1_scales_i = w1_scales.bitcast(I32).rearrange("e s b n -> b (e s) n")
-        for q in range(4):
-            nc.scalar.dma_start(
-                w1_scale[32 * q : 32 * q + 4, : 2 * PASSES, :].bitcast(I32), w1_scales_i[4 * q : 4 * q + 4, : 2 * PASSES]
-            )
-        x_rest = keep.tile([P, PASSES - 1, T], I32, name="x_rest", align_bytes=64)
-        nc.sync.dma_start(x_rest[:], x_words_i[:, 1:, :])
-        x_win = [x_first[:]] + [x_rest[:, s, :] for s in range(PASSES - 1)]
-        w1_words_i = w1_words.bitcast(I32).rearrange("e s p n -> p (e s) n")
-        w1_first = keep.tile([P, 2 * PASSES, 2 * H], U8, name="w1_first", align_bytes=64)
-        nc.sync.dma_start(w1_first[:].bitcast(I32), w1_words_i[:, : 2 * PASSES, :])
-        for r, pos in enumerate((pos1, pos2)):
-            nc.sync.dma_start(pos_sb[r][:], pos)
-
-        for q in range(4):
+        for half in range(2):
             nc.sync.dma_start(
-                w1_scale[32 * q : 32 * q + 4, 2 * PASSES :, :].bitcast(I32), w1_scales_i[4 * q : 4 * q + 4, 2 * PASSES :]
+                win_i[64 * half + 4 : 64 * half + 20, : T // 4],
+                x_scales_i[1:, 8 * half : 8 * half + 8, :].rearrange("s b n -> b s n"),
             )
-
-        ident = keep.tile([P, P], F32, name="ident")
-        make_identity(nc, ident[:])
-
-        gate_sb = keep.tile([P, 2, T], F32, name="gate_sb")
-        nc.sync.dma_start(gate_sb[:], gate.rearrange("r p t -> p r t"))
-        w2_scale = keep.tile([P, N], U8, name="w2_scale", align_bytes=64)
-        nc.gpsimd.memset(w2_scale[:].bitcast(I32), 0)
-        w2_scales_i = w2_scales.bitcast(I32)
         for q in range(4):
-            nc.sync.dma_start(w2_scale[32 * q : 32 * q + 4, :].bitcast(I32), w2_scales_i[0, 4 * q : 4 * q + 4, :])
-        w2_sb = keep.tile([P, N], I32, name="w2_sb", align_bytes=64)
-        nc.sync.dma_start(w2_sb[:], w2_words[0].rearrange("p n d -> p (n d)").bitcast(I32))
+            nc.sync.dma_start(win_i[32 * q : 32 * q + 4, : T // 4], x_scales_i[0, 4 * q : 4 * q + 4, :])
+        nc.sync.dma_start(gate_rows[: 2 * T // P, :], gate[:, 0, :].rearrange("r (b m) -> r b m", m=P))
+        w1_scales_i = w1_scales.bitcast(I32).rearrange("e s (q r) n -> r q (e s) n", r=4)
+        for r in range(4):
+            nc.sync.dma_start(w1_scale[r:P:32, :, :].bitcast(I32), w1_scales_i[r])
 
         slot_words = {}
 
@@ -108,33 +101,47 @@ def tile_moe_sdn_lin_relu_kernel(
 
         first_words = keep.tile([P, FIRST_GATHER[2]], U32, name="first_words", align_bytes=64)
         gather_words(first_words[:], *FIRST_GATHER)
-        nc.vector.tensor_copy(slot_scale[0][:], x_scale_win[:].indirect(offs_sb[:]))
-        for s in range(1, PASSES):
-            for row, first in ((0, 4 * s), (64, 52 + 4 * s)):
-                nc.scalar.dma_start(
-                    slot_scale[s][row : row + 64, :].bitcast(I32), slot_scale[0][first : first + 64, :].bitcast(I32)
-                )
-        w1_rest = shared.tile([P, 4 * PASSES, 2 * H], U8, name="w1_rest", align_bytes=64, offset=0)
-        w1_sb = [w1_first[:], w1_rest[:, : 2 * PASSES, :], w1_rest[:, 2 * PASSES :, :]]
-        for pair in (1, 2):
-            groups = slice(2 * PASSES * pair, 2 * PASSES * (pair + 1))
-            nc.scalar.dma_start(w1_sb[pair].bitcast(I32), w1_words_i[:, groups, :])
-        later_words = shared.tile(
-            [P, PASSES * S - FIRST_GATHER[2]], U32, name="later_words", align_bytes=64, offset=12288
-        )
+        nc.vector.tensor_copy(gathered_scale[:], x_scale_win[:].indirect(offs_sb[:]))
+        for q in (0, 2, 1, 3):
+            first = 64 * (q // 2) + 4 + 8 * (q % 2)
+            nc.sync.dma_start(
+                moved_scale[32 * q : 32 * q + 4, :, :].bitcast(I32), gathered_scale[first : first + 8, :].bitcast(I32)
+            )
+        for r, pos in enumerate((pos1, pos2)):
+            nc.sync.dma_start(pos_sb[r][:], pos)
+        w2_sb = keep.tile([P, N], I32, name="w2_sb", align_bytes=64)
+        nc.sync.dma_start(w2_sb[:], w2_words[0].rearrange("p n d -> p (n d)").bitcast(I32))
+        w2_scales_i = w2_scales.bitcast(I32)
+        for q in range(4):
+            nc.sync.dma_start(w2_scale[32 * q : 32 * q + 4, :].bitcast(I32), w2_scales_i[0, 4 * q : 4 * q + 4, :])
+
+        later_words = shared.tile([P, PASSES * S - FIRST_GATHER[2]], U32, name="later_words", align_bytes=64, offset=0)
         col = 0
         for s, first, n in LATER_GATHERS:
             gather_words(later_words[:, col : col + n], s, first, n)
             col += n
 
+        gate_cols = keep.tile([P, 2 * T // P], F32, name="gate_cols")
+        gate_sb = keep.tile([P, 2 * T], F32, name="gate_sb")
+        bank = psum.tile([P, P], F32, name="gate_turned", tag="work", bufs=WORK)
+        nc.tensor.transpose(bank[:], gate_rows[:], ident[:])
+        nc.scalar.copy(gate_cols[:], bank[:, : 2 * T // P])
+        for first in range(0, 2 * T // P, 4):
+            bank = psum.tile([P, 4, P], F32, name="gate_spread", tag="work", bufs=WORK)
+            for b in range(4):
+                nc.tensor.transpose(bank[:, b, :], gate_cols[:, first + b : first + b + 1].to_broadcast([P, P]), ident[:])
+            nc.scalar.copy(gate_sb[:, first * P : (first + 4) * P], bank[:].rearrange("p b t -> p (b t)"))
+
         hidden = [keep.tile([P, S], F32, name="hidden%d" % j) for j in range(PLANES)]
-        def expert_plane(j, e):
-            acc = psum.tile([P, C], F32, name="acc", tag="work", bufs=4)
-            for half in range(C // P):
-                slot = e * C + half * P
+
+        def unit(j, first, n):
+            e = first // C
+            acc = psum.tile([P, n], F32, name="acc", tag="work", bufs=WORK)
+            for col in range(0, n, P):
+                slot = first + col
                 for s in range(PASSES):
                     nc.tensor.matmul_mx(
-                        out=acc[:, half * P : (half + 1) * P],
+                        out=acc[:, col : col + P],
                         lhsT=w1_sb[e // 2][:, (e % 2) * PASSES + s, 2 * P * j : 2 * P * (j + 1)].bitcast(FP4X4),
                         lhsT_scale=w1_scale[:, e * PASSES + s, P * j : P * (j + 1)],
                         rhs=slot_words[s, slot].bitcast(FP8X4),
@@ -142,7 +149,10 @@ def tile_moe_sdn_lin_relu_kernel(
                         start=(s == 0),
                         stop=(s == PASSES - 1),
                     )
-            nc.scalar.activation(hidden[j][:, e * C : (e + 1) * C], acc[:], RELU, bias=zero_bias[:])
+            nc.scalar.activation(hidden[j][:, first : first + n], acc[:], RELU, bias=zero_bias[:])
+
+        def expert_plane(j, e):
+            unit(j, e * C, C)
 
         c_tok = keep.tile([P, T // P, 2, P, 2], BF16, name="c_tok", align_bytes=64)
         grouped = keep.tile([P, 4 * T], BF16, name="grouped", align_bytes=64)
@@ -155,24 +165,23 @@ def tile_moe_sdn_lin_relu_kernel(
             for r in range(2):
                 offsets = pos_sb[r][:, first // 16 : (first + n) // 16]
                 cols = slice(first, first + n)
-                nc.vector.tensor_tensor(prods[j][r][:, cols], hidden[j][:].indirect(offsets), gate_sb[:, r, cols], MULT)
+                nc.vector.tensor_tensor(prods[j][r][:, cols], hidden[j][:].indirect(offsets), gate_sb[:, r * T + first : r * T + first + n], MULT)
 
         def add_turned(j, first, n, copy):
-            bank = psum.tile([P, n // P, P], F32, name="turned", tag="work", bufs=4)
+            bank = psum.tile([P, n // P, P], F32, name="turned", tag="work", bufs=WORK)
             for b in range(n // P):
                 cols = slice(first + b * P, first + (b + 1) * P)
                 for r in range(2):
                     nc.tensor.matmul(
                         bank[:, b, :], prods[j][r][:, cols], ident[:], start=(r == 0), stop=(r == 1), is_transpose=True
                     )
-            for b in range(n // P):
-                copy(
-                    c_tok[:, first // P + b, :, 32 * j : 32 * (j + 1), :],
-                    bank[:, b, :].rearrange("p (m u v) -> p u m v", u=2, v=2),
-                )
+            copy(
+                c_tok[:, first // P : (first + n) // P, :, 32 * j : 32 * (j + 1), :],
+                bank[:].rearrange("p b (m u v) -> p b u m v", u=2, v=2),
+            )
 
         def turn_back(first, n, copy):
-            bank = psum.tile([P, n // P, 2, P], F32, name="back", tag="work", bufs=4)
+            bank = psum.tile([P, n // P, 2, P], F32, name="back", tag="work", bufs=WORK)
             for b in range(n // P):
                 for u in range(2):
                     pairs = c_tok[:, first // P + b, u, :, :].rearrange("p m v -> p (m v)").bitcast(F32)
@@ -204,29 +213,29 @@ def tile_moe_sdn_lin_relu_kernel(
             nc.sync.dma_start(out[:, cols], res[:, cols])
 
         on_scalar, on_vector = nc.scalar.copy, nc.vector.tensor_copy
-        for j, e in [(j, e) for j in range(4) for e in range(2)] + [(0, e) for e in range(2, E)] + [(1, e) for e in range(2, E)]:
-            expert_plane(j, e)
+        for pair in range(2):
+            for j in range(2):
+                expert_plane(j, 2 * pair)
+                expert_plane(j, 2 * pair + 1)
+        expert_plane(0, 4)
+        unit(0, S - 2 * P, P)
+        unit(0, S - P, P)
+        expert_plane(1, 4)
+        expert_plane(1, 5)
+        for j in (2, 3):
+            for e in range(E):
+                expert_plane(j, e)
         most, last = (0, T - P), (T - P, P)
-        gather_products(0, *most)
-        gather_products(1, *most)
-        for e in range(2, E):
-            expert_plane(2, e)
-        add_turned(0, 0, 384, on_scalar)
-        add_turned(0, 384, 256, on_scalar)
-        expert_plane(3, 2)
-        expert_plane(3, 3)
-        add_turned(1, 0, 384, on_scalar)
-        expert_plane(3, 4)
-        expert_plane(3, 5)
-        add_turned(1, 384, 256, on_scalar)
         a, b, c = (0, 256), (256, 256), (512, 128)
-        gather_products(2, *most)
+        for j in range(3):
+            gather_products(j, *most)
         for chunk in (a, b, c):
             gather_products(3, *chunk)
         for j in range(PLANES):
             gather_products(j, *last)
-        add_turned(2, 0, 384, on_scalar)
-        add_turned(2, 384, 256, on_scalar)
+        for j in range(3):
+            add_turned(j, 0, 384, on_scalar)
+            add_turned(j, 384, 256, on_scalar)
         add_turned(3, *a, on_scalar)
         add_turned(3, *b, on_scalar)
         turn_back(*a, on_scalar)

@@ -24,8 +24,8 @@ PLANES = H // P
 SCALE_WINDOW = 2048
 FIRST_GATHER = (0, 0, 512)
 LATER_GATHERS = [
-    (1, 0, 512), (2, 0, 512), (0, 512, 512), (1, 512, 512), (2, 512, 512),
-    (0, 1024, 512), (1, 1024, 512), (2, 1024, 256), (2, 1280, 128), (2, 1408, 128),
+    (0, 512, 512), (1, 0, 512), (2, 0, 512), (1, 512, 512), (2, 512, 512),
+    (1, 1024, 512), (2, 1024, 512),
 ]
 WORK = 5
 
@@ -40,56 +40,51 @@ def tile_moe_sdn_lin_relu_kernel(
         shared = ctx.enter_context(tc.tile_pool(name="shared", bufs=1))
         psum = ctx.enter_context(tc.psum_pool(name="psum", bufs=1))
 
+        def next_bank(shape, name):
+            return psum.tile(shape, F32, name=name, tag="work", bufs=WORK)
+
         offs_sb = lists.tile([P, S // 16], U16, name="offs_sb")
         pos_sb = [lists.tile([P, T // 16], U16, name="pos%d_sb" % r) for r in range(2)]
 
-        x_scale_win = shared.tile([P, SCALE_WINDOW], U8, name="x_scale_win", align_bytes=64, offset=0)
+        x_scale_win = shared.tile([P, SCALE_WINDOW], U8, name="x_scale_win", align_bytes=64, offset=17408)
         w1_scale = keep.tile([P, E * PASSES, H], U8, name="w1_scale", align_bytes=64)
-        gathered_scale = keep.tile([P, S], U8, name="gathered_scale", align_bytes=64)
-        moved_scale = keep.tile([P, PASSES - 1, S], U8, name="moved_scale", align_bytes=64)
-        slot_scale = [gathered_scale[:]] + [moved_scale[:, s, :] for s in range(PASSES - 1)]
-        w2_scale = keep.tile([P, N], U8, name="w2_scale", align_bytes=64)
+        slot_scale = [keep.tile([P, S], U8, name="slot_scale%d" % s, align_bytes=64) for s in range(PASSES)]
         zero_in = keep.tile([P, 1], F32, name="zero_in")
         gate_rows = keep.tile([P, P], F32, name="gate_rows")
         ident = keep.tile([P, P], F32, name="ident")
         win_i = x_scale_win[:].bitcast(I32)
-        nc.vector.memset(win_i[:, : T // 4], 0)
+        nc.gpsimd.memset(win_i[:, : T // 4], 0)
+        nc.gpsimd.memset(zero_in[:], 0.0)
         nc.vector.memset(w1_scale[:].rearrange("p g n -> p (g n)").bitcast(I32), 0)
         nc.vector.memset(win_i[:, T // 4 :], 0)
-        nc.gpsimd.memset(zero_in[:], 0.0)
         nc.gpsimd.memset(gate_rows[:], 0.0)
         make_identity(nc, ident[:])
-        nc.gpsimd.memset(moved_scale[:].rearrange("p s n -> p (s n)").bitcast(I32), 0)
-        nc.gpsimd.memset(w2_scale[:].bitcast(I32), 0)
 
         x_words_i = x_words.rearrange("s p t d -> p s (t d)").bitcast(I32)
         w1_words_i = w1_words.bitcast(I32).rearrange("e s p n -> p (e s) n")
         x_first = keep.tile([P, T], I32, name="x_first", align_bytes=64)
         x_rest = keep.tile([P, PASSES - 1, T], I32, name="x_rest", align_bytes=64)
-        w1_first = keep.tile([P, 2 * PASSES, 2 * H], U8, name="w1_first", align_bytes=64)
-        w1_rest = keep.tile([P, 4 * PASSES, 2 * H], U8, name="w1_rest", align_bytes=64)
+        w1_first = shared.tile([P, 2 * PASSES, 2 * H], U8, name="w1_first", align_bytes=64, offset=0)
         zero_bias = keep.tile([P, 1], F32, name="zero_bias")
-        nc.scalar.dma_start(x_first[:], x_words_i[:, 0, :])
-        nc.scalar.dma_start(x_rest[:], x_words_i[:, 1:, :])
-        nc.scalar.activation(zero_bias[:], zero_in[:], RELU)
-        nc.scalar.dma_start(w1_first[:].bitcast(I32), w1_words_i[:, : 2 * PASSES, :])
-        nc.scalar.dma_start(w1_rest[:].bitcast(I32), w1_words_i[:, 2 * PASSES :, :])
         x_win = [x_first[:]] + [x_rest[:, s, :] for s in range(PASSES - 1)]
-        w1_sb = [w1_first[:], w1_rest[:, : 2 * PASSES, :], w1_rest[:, 2 * PASSES :, :]]
 
         nc.sync.dma_start(offs_sb[:], offs)
+        nc.sync.dma_start(x_first[:], x_words_i[:, 0, :])
         x_scales_i = x_scales.bitcast(I32)
-        for half in range(2):
-            nc.sync.dma_start(
-                win_i[64 * half + 4 : 64 * half + 20, : T // 4],
-                x_scales_i[1:, 8 * half : 8 * half + 8, :].rearrange("s b n -> b s n"),
-            )
-        for q in range(4):
-            nc.sync.dma_start(win_i[32 * q : 32 * q + 4, : T // 4], x_scales_i[0, 4 * q : 4 * q + 4, :])
-        nc.sync.dma_start(gate_rows[: 2 * T // P, :], gate[:, 0, :].rearrange("r (b m) -> r b m", m=P))
+        for q in range(2):
+            nc.sync.dma_start(win_i[32 * q : 32 * q + 12, : T // 4], x_scales_i[:, 4 * q : 4 * q + 4, :])
+        for q in range(2, 4):
+            nc.scalar.dma_start(win_i[32 * q : 32 * q + 4, : T // 4], x_scales_i[0, 4 * q : 4 * q + 4, :])
+            nc.scalar.dma_start(win_i[32 * q - 8 : 32 * q, : T // 4], x_scales_i[1:, 4 * q : 4 * q + 4, :])
+        nc.scalar.activation(zero_bias[:], zero_in[:], RELU)
         w1_scales_i = w1_scales.bitcast(I32).rearrange("e s (q r) n -> r q (e s) n", r=4)
+        nc.sync.dma_start(x_rest[:], x_words_i[:, 1:, :])
+        nc.sync.dma_start(gate_rows[: 2 * T // P, :], gate[:, 0, :].rearrange("r (b m) -> r b m", m=P))
+        nc.sync.dma_start(w1_first[:].bitcast(I32), w1_words_i[:, : 2 * PASSES, :])
         for r in range(4):
-            nc.sync.dma_start(w1_scale[r:P:32, :, :].bitcast(I32), w1_scales_i[r])
+            nc.sync.dma_start(w1_scale[r:P:32, : 2 * PASSES, :].bitcast(I32), w1_scales_i[r][:, : 2 * PASSES])
+        for r, pos in enumerate((pos1, pos2)):
+            nc.sync.dma_start(pos_sb[r][:], pos)
 
         slot_words = {}
 
@@ -101,53 +96,55 @@ def tile_moe_sdn_lin_relu_kernel(
 
         first_words = keep.tile([P, FIRST_GATHER[2]], U32, name="first_words", align_bytes=64)
         gather_words(first_words[:], *FIRST_GATHER)
-        nc.vector.tensor_copy(gathered_scale[:], x_scale_win[:].indirect(offs_sb[:]))
-        for q in (0, 2, 1, 3):
-            first = 64 * (q // 2) + 4 + 8 * (q % 2)
-            nc.sync.dma_start(
-                moved_scale[32 * q : 32 * q + 4, :, :].bitcast(I32), gathered_scale[first : first + 8, :].bitcast(I32)
-            )
-        for r, pos in enumerate((pos1, pos2)):
-            nc.sync.dma_start(pos_sb[r][:], pos)
-        w2_sb = keep.tile([P, N], I32, name="w2_sb", align_bytes=64)
-        nc.sync.dma_start(w2_sb[:], w2_words[0].rearrange("p n d -> p (n d)").bitcast(I32))
-        w2_scales_i = w2_scales.bitcast(I32)
-        for q in range(4):
-            nc.sync.dma_start(w2_scale[32 * q : 32 * q + 4, :].bitcast(I32), w2_scales_i[0, 4 * q : 4 * q + 4, :])
+        nc.vector.tensor_copy(slot_scale[0][:], x_scale_win[:].indirect(offs_sb[:]))
+        for s in range(1, PASSES):
+            for row, first in ((0, 4 * s), (64, 52 + 4 * s)):
+                nc.sync.dma_start(
+                    slot_scale[s][row : row + 64, :].bitcast(I32), slot_scale[0][first : first + 64, :].bitcast(I32)
+                )
+        for r in range(4):
+            nc.sync.dma_start(w1_scale[r:P:32, 2 * PASSES :, :].bitcast(I32), w1_scales_i[r][:, 2 * PASSES :])
+        w1_rest = shared.tile([P, 4 * PASSES, 2 * H], U8, name="w1_rest", align_bytes=64, offset=6144)
+        w1_sb = [w1_first[:], w1_rest[:, : 2 * PASSES, :], w1_rest[:, 2 * PASSES :, :]]
+        for pair in (1, 2):
+            nc.sync.dma_start(w1_sb[pair].bitcast(I32), w1_words_i[:, 2 * PASSES * pair : 2 * PASSES * (pair + 1), :])
 
-        later_words = shared.tile([P, PASSES * S - FIRST_GATHER[2]], U32, name="later_words", align_bytes=64, offset=0)
+        later_words = shared.tile([P, (PASSES - 1) * S + 512], U32, name="later_words", align_bytes=64, offset=18432)
+        gate_cols = shared.tile([P, 2 * T // P], F32, name="gate_cols", align_bytes=64, offset=32768)
+        gate_sb = keep.tile([P, 2 * T], F32, name="gate_sb")
+        bank = next_bank([P, P], "gate_turned")
+        nc.tensor.transpose(bank[:], gate_rows[:], ident[:])
+        nc.scalar.copy(gate_cols[:], bank[:, : 2 * T // P])
+        for first in range(0, 2 * T // P, 4):
+            bank = next_bank([P, 4, P], "gate_spread")
+            for b in range(4):
+                nc.tensor.transpose(bank[:, b, :], gate_cols[:, first + b : first + b + 1].to_broadcast([P, P]), ident[:])
+            nc.scalar.copy(gate_sb[:, first * P : (first + 4) * P], bank[:].rearrange("p b t -> p (b t)"))
+
+        third_words = shared.tile([P, 512], U32, name="third_words", align_bytes=64, offset=32768)
         col = 0
         for s, first, n in LATER_GATHERS:
             gather_words(later_words[:, col : col + n], s, first, n)
             col += n
-
-        gate_cols = keep.tile([P, 2 * T // P], F32, name="gate_cols")
-        gate_sb = keep.tile([P, 2 * T], F32, name="gate_sb")
-        bank = psum.tile([P, P], F32, name="gate_turned", tag="work", bufs=WORK)
-        nc.tensor.transpose(bank[:], gate_rows[:], ident[:])
-        nc.scalar.copy(gate_cols[:], bank[:, : 2 * T // P])
-        for first in range(0, 2 * T // P, 4):
-            bank = psum.tile([P, 4, P], F32, name="gate_spread", tag="work", bufs=WORK)
-            for b in range(4):
-                nc.tensor.transpose(bank[:, b, :], gate_cols[:, first + b : first + b + 1].to_broadcast([P, P]), ident[:])
-            nc.scalar.copy(gate_sb[:, first * P : (first + 4) * P], bank[:].rearrange("p b t -> p (b t)"))
+        for col, n in ((0, 256), (256, 128), (384, 128)):
+            gather_words(third_words[:, col : col + n], 0, 1024 + col, n)
 
         hidden = [keep.tile([P, S], F32, name="hidden%d" % j) for j in range(PLANES)]
 
         def unit(j, first, n):
             e = first // C
-            acc = psum.tile([P, n], F32, name="acc", tag="work", bufs=WORK)
+            acc = next_bank([P, n], "acc")
             for col in range(0, n, P):
                 slot = first + col
-                for s in range(PASSES):
+                for s in (1, 2, 0):
                     nc.tensor.matmul_mx(
                         out=acc[:, col : col + P],
                         lhsT=w1_sb[e // 2][:, (e % 2) * PASSES + s, 2 * P * j : 2 * P * (j + 1)].bitcast(FP4X4),
                         lhsT_scale=w1_scale[:, e * PASSES + s, P * j : P * (j + 1)],
                         rhs=slot_words[s, slot].bitcast(FP8X4),
                         rhs_scale=slot_scale[s][:, slot : slot + P],
-                        start=(s == 0),
-                        stop=(s == PASSES - 1),
+                        start=(s == 1),
+                        stop=(s == 0),
                     )
             nc.scalar.activation(hidden[j][:, first : first + n], acc[:], RELU, bias=zero_bias[:])
 
@@ -168,7 +165,7 @@ def tile_moe_sdn_lin_relu_kernel(
                 nc.vector.tensor_tensor(prods[j][r][:, cols], hidden[j][:].indirect(offsets), gate_sb[:, r * T + first : r * T + first + n], MULT)
 
         def add_turned(j, first, n, copy):
-            bank = psum.tile([P, n // P, P], F32, name="turned", tag="work", bufs=WORK)
+            bank = next_bank([P, n // P, P], "turned")
             for b in range(n // P):
                 cols = slice(first + b * P, first + (b + 1) * P)
                 for r in range(2):
@@ -181,7 +178,7 @@ def tile_moe_sdn_lin_relu_kernel(
             )
 
         def turn_back(first, n, copy):
-            bank = psum.tile([P, n // P, 2, P], F32, name="back", tag="work", bufs=WORK)
+            bank = next_bank([P, n // P, 2, P], "back")
             for b in range(n // P):
                 for u in range(2):
                     pairs = c_tok[:, first // P + b, u, :, :].rearrange("p m v -> p (m v)").bitcast(F32)
@@ -203,7 +200,7 @@ def tile_moe_sdn_lin_relu_kernel(
             nc.tensor.matmul_mx(
                 out=bank[:],
                 lhsT=w2_sb[:].bitcast(FP8X4),
-                lhsT_scale=w2_scale[:],
+                lhsT_scale=w1_scale[4:P, 0, :N],
                 rhs=c_words[:, cols].bitcast(FP8X4),
                 rhs_scale=c_scale[:, cols],
                 start=True,
@@ -213,8 +210,8 @@ def tile_moe_sdn_lin_relu_kernel(
             nc.sync.dma_start(out[:, cols], res[:, cols])
 
         on_scalar, on_vector = nc.scalar.copy, nc.vector.tensor_copy
-        for pair in range(2):
-            for j in range(2):
+        for pair, planes in ((0, 2), (1, 2)):
+            for j in range(planes):
                 expert_plane(j, 2 * pair)
                 expert_plane(j, 2 * pair + 1)
         expert_plane(0, 4)
@@ -222,18 +219,27 @@ def tile_moe_sdn_lin_relu_kernel(
         unit(0, S - P, P)
         expert_plane(1, 4)
         expert_plane(1, 5)
-        for j in (2, 3):
-            for e in range(E):
-                expert_plane(j, e)
+        for e in range(E):
+            expert_plane(2, e)
+        w2_scales_i = w2_scales.bitcast(I32).rearrange("s (q r) n -> r q (s n)", r=4)
+        for r in range(4):
+            nc.sync.dma_start(w1_scale[4 + r : P : 32, 0, :N].bitcast(I32), w2_scales_i[r])
         most, last = (0, T - P), (T - P, P)
         a, b, c = (0, 256), (256, 256), (512, 128)
-        for j in range(3):
+        gather_products(0, *most)
+        add_turned(0, 0, 384, on_scalar)
+        add_turned(0, 384, 256, on_scalar)
+        for e in range(E):
+            expert_plane(3, e)
+        w2_sb = shared.tile([P, N], I32, name="w2_sb", align_bytes=64, offset=0)
+        nc.sync.dma_start(w2_sb[:], w2_words[0].rearrange("p n d -> p (n d)").bitcast(I32))
+        for j in (1, 2):
             gather_products(j, *most)
         for chunk in (a, b, c):
             gather_products(3, *chunk)
         for j in range(PLANES):
             gather_products(j, *last)
-        for j in range(3):
+        for j in (1, 2):
             add_turned(j, 0, 384, on_scalar)
             add_turned(j, 384, 256, on_scalar)
         add_turned(3, *a, on_scalar)

@@ -15,7 +15,8 @@ U16 = mybir.dt.uint16
 U8 = mybir.dt.uint8
 FP8X4 = mybir.dt.float8_e4m3fn_x4
 FP4X4 = mybir.dt.float4_e2m1fn_x4
-MULT = mybir.AluOpType.mult
+ALU = mybir.AluOpType
+COPY = mybir.ActivationFunctionType.Copy
 RELU = mybir.ActivationFunctionType.Relu
 
 P = 128
@@ -24,10 +25,11 @@ PLANES = H // P
 SCALE_WINDOW = 2048
 FIRST_GATHER = (0, 0, 512)
 LATER_GATHERS = [
-    (0, 512, 512), (1, 0, 512), (2, 0, 512), (1, 512, 512), (2, 512, 512),
-    (1, 1024, 512), (2, 1024, 512),
+    (1, 512, 512), (2, 512, 512), (0, 1024, 512), (1, 1024, 512), (2, 1024, 256), (2, 1280, 128), (2, 1408, 128),
 ]
-WORK = 5
+BANKS = 8
+BLOCKS = T // P
+TINY = 2.0**-60
 
 
 def tile_moe_sdn_lin_relu_kernel(
@@ -40,8 +42,14 @@ def tile_moe_sdn_lin_relu_kernel(
         shared = ctx.enter_context(tc.tile_pool(name="shared", bufs=1))
         psum = ctx.enter_context(tc.psum_pool(name="psum", bufs=1))
 
+        taken = []
+
+        def next_tag():
+            taken.append(len(taken) % BANKS)
+            return "bank%d" % taken[-1]
+
         def next_bank(shape, name):
-            return psum.tile(shape, F32, name=name, tag="work", bufs=WORK)
+            return psum.tile(shape, F32, name=name, tag=next_tag())
 
         offs_sb = lists.tile([P, S // 16], U16, name="offs_sb")
         pos_sb = [lists.tile([P, T // 16], U16, name="pos%d_sb" % r) for r in range(2)]
@@ -65,7 +73,9 @@ def tile_moe_sdn_lin_relu_kernel(
         x_first = keep.tile([P, T], I32, name="x_first", align_bytes=64)
         x_rest = keep.tile([P, PASSES - 1, T], I32, name="x_rest", align_bytes=64)
         w1_first = shared.tile([P, 2 * PASSES, 2 * H], U8, name="w1_first", align_bytes=64, offset=0)
-        zero_bias = keep.tile([P, 1], F32, name="zero_bias")
+        zero_bias = [
+            shared.tile([P, 1], F32, name="zero_bias%d" % k, align_bytes=64, offset=34816 + 4 * T * k) for k in range(2)
+        ]
         x_win = [x_first[:]] + [x_rest[:, s, :] for s in range(PASSES - 1)]
 
         nc.sync.dma_start(offs_sb[:], offs)
@@ -76,10 +86,11 @@ def tile_moe_sdn_lin_relu_kernel(
         for q in range(2, 4):
             nc.scalar.dma_start(win_i[32 * q : 32 * q + 4, : T // 4], x_scales_i[0, 4 * q : 4 * q + 4, :])
             nc.scalar.dma_start(win_i[32 * q - 8 : 32 * q, : T // 4], x_scales_i[1:, 4 * q : 4 * q + 4, :])
-        nc.scalar.activation(zero_bias[:], zero_in[:], RELU)
+        for k in range(2):
+            nc.scalar.activation(zero_bias[k][:], zero_in[:], RELU)
         w1_scales_i = w1_scales.bitcast(I32).rearrange("e s (q r) n -> r q (e s) n", r=4)
+        nc.sync.dma_start(gate_rows[: 2 * BLOCKS, :], gate[:, 0, :].rearrange("r (b m) -> r b m", m=P))
         nc.sync.dma_start(x_rest[:], x_words_i[:, 1:, :])
-        nc.sync.dma_start(gate_rows[: 2 * T // P, :], gate[:, 0, :].rearrange("r (b m) -> r b m", m=P))
         nc.sync.dma_start(w1_first[:].bitcast(I32), w1_words_i[:, : 2 * PASSES, :])
         for r in range(4):
             nc.sync.dma_start(w1_scale[r:P:32, : 2 * PASSES, :].bitcast(I32), w1_scales_i[r][:, : 2 * PASSES])
@@ -109,73 +120,123 @@ def tile_moe_sdn_lin_relu_kernel(
         for pair in (1, 2):
             nc.sync.dma_start(w1_sb[pair].bitcast(I32), w1_words_i[:, 2 * PASSES * pair : 2 * PASSES * (pair + 1), :])
 
-        later_words = shared.tile([P, (PASSES - 1) * S + 512], U32, name="later_words", align_bytes=64, offset=18432)
-        gate_cols = shared.tile([P, 2 * T // P], F32, name="gate_cols", align_bytes=64, offset=32768)
-        gate_sb = keep.tile([P, 2 * T], F32, name="gate_sb")
         bank = next_bank([P, P], "gate_turned")
         nc.tensor.transpose(bank[:], gate_rows[:], ident[:])
-        nc.scalar.copy(gate_cols[:], bank[:, : 2 * T // P])
-        for first in range(0, 2 * T // P, 4):
-            bank = next_bank([P, 4, P], "gate_spread")
-            for b in range(4):
-                nc.tensor.transpose(bank[:, b, :], gate_cols[:, first + b : first + b + 1].to_broadcast([P, P]), ident[:])
-            nc.scalar.copy(gate_sb[:, first * P : (first + 4) * P], bank[:].rearrange("p b t -> p (b t)"))
+        gate_cols = keep.tile([P, 2 * BLOCKS], F32, name="gate_cols")
+        nc.scalar.copy(gate_cols[:], bank[:, : 2 * BLOCKS])
+        g1, g2 = gate_cols[:, :BLOCKS], gate_cols[:, BLOCKS:]
+        square = keep.tile([P, BLOCKS], F32, name="square")
+        lift = keep.tile([P, BLOCKS], F32, name="lift")
+        lifted = shared.tile([P, BLOCKS], F32, name="lifted", align_bytes=64, offset=24576)
+        pivot = keep.tile([P, BLOCKS], F32, name="pivot")
+        inverse = keep.tile([P, BLOCKS], F32, name="inverse")
+        ratio_cols = keep.tile([P, BLOCKS], F32, name="ratio_cols")
+        nc.gpsimd.tensor_tensor(square[:], g2, g2, ALU.mult)
+        nc.gpsimd.tensor_scalar(lift[:], square[:], TINY * TINY, 2 * TINY, ALU.is_lt, ALU.mult)
+        nc.gpsimd.tensor_tensor(lifted[:], g2, lift[:], ALU.add)
+        nc.scalar.copy(pivot[:], lifted[:])
 
-        third_words = shared.tile([P, 512], U32, name="third_words", align_bytes=64, offset=32768)
+        early_words = shared.tile([P, 3 * 512], U32, name="early_words", align_bytes=64, offset=18432)
+        for k, (s, first) in enumerate(((0, 512), (1, 0), (2, 0))):
+            gather_words(early_words[:, 512 * k : 512 * (k + 1)], s, first, 512)
+        nc.vector.reciprocal(inverse[:], lifted[:])
+        for b in range(BLOCKS):
+            nc.scalar.activation(ratio_cols[:, b : b + 1], g1[:, b : b + 1], COPY, scale=inverse[:, b : b + 1])
+        late_words = shared.tile([P, 5 * 512], U32, name="late_words", align_bytes=64, offset=24576)
         col = 0
         for s, first, n in LATER_GATHERS:
-            gather_words(later_words[:, col : col + n], s, first, n)
+            gather_words(late_words[:, col : col + n], s, first, n)
             col += n
-        for col, n in ((0, 256), (256, 128), (384, 128)):
-            gather_words(third_words[:, col : col + n], 0, 1024 + col, n)
 
         hidden = [keep.tile([P, S], F32, name="hidden%d" % j) for j in range(PLANES)]
 
+        def mx_pass(acc, j, slot, s, start, stop):
+            e = slot // C
+            nc.tensor.matmul_mx(
+                out=acc,
+                lhsT=w1_sb[e // 2][:, (e % 2) * PASSES + s, 2 * P * j : 2 * P * (j + 1)].bitcast(FP4X4),
+                lhsT_scale=w1_scale[:, e * PASSES + s, P * j : P * (j + 1)],
+                rhs=slot_words[s, slot].bitcast(FP8X4),
+                rhs_scale=slot_scale[s][:, slot : slot + P],
+                start=start,
+                stop=stop,
+            )
+
+        def relu(j, first, acc):
+            nc.scalar.activation(hidden[j][:, first : first + acc.shape[1]], acc, RELU, bias=zero_bias[j // 2][:])
+
         def unit(j, first, n):
-            e = first // C
             acc = next_bank([P, n], "acc")
             for col in range(0, n, P):
-                slot = first + col
-                for s in (1, 2, 0):
-                    nc.tensor.matmul_mx(
-                        out=acc[:, col : col + P],
-                        lhsT=w1_sb[e // 2][:, (e % 2) * PASSES + s, 2 * P * j : 2 * P * (j + 1)].bitcast(FP4X4),
-                        lhsT_scale=w1_scale[:, e * PASSES + s, P * j : P * (j + 1)],
-                        rhs=slot_words[s, slot].bitcast(FP8X4),
-                        rhs_scale=slot_scale[s][:, slot : slot + P],
-                        start=(s == 1),
-                        stop=(s == 0),
-                    )
-            nc.scalar.activation(hidden[j][:, first : first + n], acc[:], RELU, bias=zero_bias[:])
+                for s in range(PASSES):
+                    mx_pass(acc[:, col : col + P], j, first + col, s, s == 0, s == PASSES - 1)
+            relu(j, first, acc[:])
 
         def expert_plane(j, e):
             unit(j, e * C, C)
 
-        c_tok = keep.tile([P, T // P, 2, P, 2], BF16, name="c_tok", align_bytes=64)
+        opened = [(j, slot, next_bank([P, P], "acc")) for j in range(2) for slot in range(0, 2 * C, P)]
+        for s in range(PASSES):
+            for j, slot, acc in opened:
+                mx_pass(acc[:], j, slot, s, s == 0, s == PASSES - 1)
+        for j, slot, acc in opened:
+            relu(j, slot, acc[:])
+
+        ratio = keep.tile([P, T], F32, name="ratio")
+        for first in range(0, BLOCKS, 3):
+            bank = next_bank([P, 3, P], "spread")
+            for b in range(3):
+                nc.tensor.transpose(bank[:, b, :], ratio_cols[:, first + b : first + b + 1].to_broadcast([P, P]), ident[:])
+            nc.scalar.copy(ratio[:, first * P : (first + 3) * P], bank[:].rearrange("p b t -> p (b t)"))
+
+        for j in range(2):
+            expert_plane(j, 2)
+            expert_plane(j, 3)
+        expert_plane(0, 4)
+        unit(0, S - 2 * P, P)
+        unit(0, S - P, P)
+        expert_plane(1, 4)
+        expert_plane(1, 5)
+        for j in (2, 3):
+            for e in range(E):
+                expert_plane(j, e)
+        w2_scales_i = w2_scales.bitcast(I32).rearrange("s (q r) n -> r q (s n)", r=4)
+        for r in range(4):
+            nc.sync.dma_start(w1_scale[4 + r : P : 32, 0, :N].bitcast(I32), w2_scales_i[r])
+        w2_sb = shared.tile([P, N], I32, name="w2_sb", align_bytes=64, offset=0)
+        nc.sync.dma_start(w2_sb[:], w2_words[0].rearrange("p n d -> p (n d)").bitcast(I32))
+
+        c_tok = keep.tile([P, BLOCKS, 2, P, 2], BF16, name="c_tok", align_bytes=64)
         grouped = keep.tile([P, 4 * T], BF16, name="grouped", align_bytes=64)
         c_words = keep.tile([P, T], U32, name="c_words", align_bytes=64)
         c_scale = keep.tile([P, T], U8, name="c_scale", align_bytes=64)
         res = keep.tile([P, T], F32, name="res")
-        prods = [[keep.tile([P, T], F32, name="prod%d_%d" % (j, r)) for r in range(2)] for j in range(PLANES)]
+        scaled = [keep.tile([P, T], F32, name="scaled%d" % j) for j in range(PLANES)]
+        sums = {j: keep.tile([P, T], F32, name="sum%d" % j) for j in (1, 3)}
+        for j in (0, 2):
+            sums[j] = shared.tile([P, T], F32, name="sum%d" % j, align_bytes=64, offset=34816 + 2 * T * j)
 
-        def gather_products(j, first, n):
-            for r in range(2):
-                offsets = pos_sb[r][:, first // 16 : (first + n) // 16]
-                cols = slice(first, first + n)
-                nc.vector.tensor_tensor(prods[j][r][:, cols], hidden[j][:].indirect(offsets), gate_sb[:, r * T + first : r * T + first + n], MULT)
+        def gather_scaled(j):
+            nc.vector.tensor_tensor(scaled[j][:], hidden[j][:].indirect(pos_sb[0][:]), ratio[:], ALU.mult)
 
-        def add_turned(j, first, n, copy):
-            bank = next_bank([P, n // P, P], "turned")
+        def gather_sum(j, first, n):
+            offsets = pos_sb[1][:, first // 16 : (first + n) // 16]
+            cols = slice(first, first + n)
+            nc.vector.tensor_tensor(sums[j][:, cols], hidden[j][:].indirect(offsets), scaled[j][:, cols], ALU.add)
+
+        def turn(j, first, n, tag):
+            bank = psum.tile([P, n // P, 2, P], F32, name="turned", tag=tag)
+            for k in range(2):
+                for b in range(n // P):
+                    nc.tensor.transpose(bank[:, b, k, :], sums[j + k][:, first + b * P : first + (b + 1) * P], ident[:])
             for b in range(n // P):
-                cols = slice(first + b * P, first + (b + 1) * P)
-                for r in range(2):
-                    nc.tensor.matmul(
-                        bank[:, b, :], prods[j][r][:, cols], ident[:], start=(r == 0), stop=(r == 1), is_transpose=True
-                    )
-            copy(
-                c_tok[:, first // P : (first + n) // P, :, 32 * j : 32 * (j + 1), :],
-                bank[:].rearrange("p b (m u v) -> p b u m v", u=2, v=2),
-            )
+                block = first // P + b
+                nc.scalar.activation(
+                    c_tok[:, block, :, 32 * j : 32 * (j + 2), :],
+                    bank[:, b, :, :].rearrange("p k (m u v) -> p u (k m) v", u=2, v=2),
+                    COPY,
+                    scale=pivot[:, block : block + 1],
+                )
 
         def turn_back(first, n, copy):
             bank = next_bank([P, n // P, 2, P], "back")
@@ -196,7 +257,7 @@ def tile_moe_sdn_lin_relu_kernel(
 
         def project(first, n, copy):
             cols = slice(first, first + n)
-            bank = psum.tile([P, n], F32, name="projected", tag="projected", bufs=3)
+            bank = next_bank([P, n], "projected")
             nc.tensor.matmul_mx(
                 out=bank[:],
                 lhsT=w2_sb[:].bitcast(FP8X4),
@@ -210,52 +271,30 @@ def tile_moe_sdn_lin_relu_kernel(
             nc.sync.dma_start(out[:, cols], res[:, cols])
 
         on_scalar, on_vector = nc.scalar.copy, nc.vector.tensor_copy
-        for pair, planes in ((0, 2), (1, 2)):
-            for j in range(planes):
-                expert_plane(j, 2 * pair)
-                expert_plane(j, 2 * pair + 1)
-        expert_plane(0, 4)
-        unit(0, S - 2 * P, P)
-        unit(0, S - P, P)
-        expert_plane(1, 4)
-        expert_plane(1, 5)
-        for e in range(E):
-            expert_plane(2, e)
-        w2_scales_i = w2_scales.bitcast(I32).rearrange("s (q r) n -> r q (s n)", r=4)
-        for r in range(4):
-            nc.sync.dma_start(w1_scale[4 + r : P : 32, 0, :N].bitcast(I32), w2_scales_i[r])
-        most, last = (0, T - P), (T - P, P)
-        a, b, c = (0, 256), (256, 256), (512, 128)
-        gather_products(0, *most)
-        add_turned(0, 0, 384, on_scalar)
-        add_turned(0, 384, 256, on_scalar)
-        for e in range(E):
-            expert_plane(3, e)
-        w2_sb = shared.tile([P, N], I32, name="w2_sb", align_bytes=64, offset=0)
-        nc.sync.dma_start(w2_sb[:], w2_words[0].rearrange("p n d -> p (n d)").bitcast(I32))
-        for j in (1, 2):
-            gather_products(j, *most)
-        for chunk in (a, b, c):
-            gather_products(3, *chunk)
-        for j in range(PLANES):
-            gather_products(j, *last)
-        for j in (1, 2):
-            add_turned(j, 0, 384, on_scalar)
-            add_turned(j, 384, 256, on_scalar)
-        add_turned(3, *a, on_scalar)
-        add_turned(3, *b, on_scalar)
-        turn_back(*a, on_scalar)
-        add_turned(3, *c, on_scalar)
+        gather_scaled(0)
+        gather_scaled(1)
+        gather_sum(0, 0, T)
+        gather_sum(1, 0, T)
+        gather_scaled(2)
+        gather_scaled(3)
+        for first in range(0, T, 256):
+            turn(0, first, 256, next_tag())
+        a, b, c, last = (0, 256), (256, 256), (512, 128), (640, 128)
+        for chunk in (a, b, c, last):
+            gather_sum(2, *chunk)
+            gather_sum(3, *chunk)
+        tags = [next_tag(), next_tag()]
+        turn(2, *a, tags[0])
+        turn(2, *b, tags[1])
+        turn_back(*a, on_vector)
+        turn(2, *c, tags[0])
+        turn(2, *last, tags[1])
         turn_back(*b, on_scalar)
-        add_turned(0, *last, on_scalar)
-        turn_back(*c, on_scalar)
-        add_turned(1, *last, on_scalar)
-        add_turned(2, *last, on_scalar)
-        quantize(0, 512)
-        add_turned(3, *last, on_vector)
-        quantize(*c)
+        quantize(*a)
+        turn_back(*c, on_vector)
         turn_back(*last, on_scalar)
-        quantize(*last)
-        project(0, 512, on_scalar)
-        project(*c, on_scalar)
-        project(*last, on_vector)
+        quantize(*b)
+        quantize(512, 256)
+        project(*a, on_scalar)
+        project(*b, on_scalar)
+        project(512, 256, on_vector)

@@ -25,11 +25,13 @@ PLANES = H // P
 SCALE_WINDOW = 2048
 FIRST_GATHER = (0, 0, 512)
 LATER_GATHERS = [
-    (1, 512, 512), (2, 512, 512), (0, 1024, 512), (1, 1024, 512), (2, 1024, 256), (2, 1280, 128), (2, 1408, 128),
+    (1, 0, 512), (2, 0, 512), (0, 512, 512), (1, 512, 512), (2, 512, 512),
+    (0, 1024, 512), (1, 1024, 512), (2, 1024, 256), (2, 1280, 128), (2, 1408, 128),
 ]
 BANKS = 8
 BLOCKS = T // P
 TINY = 2.0**-60
+HUGE = 2.0**127
 
 
 def tile_moe_sdn_lin_relu_kernel(
@@ -74,7 +76,8 @@ def tile_moe_sdn_lin_relu_kernel(
         x_rest = keep.tile([P, PASSES - 1, T], I32, name="x_rest", align_bytes=64)
         w1_first = shared.tile([P, 2 * PASSES, 2 * H], U8, name="w1_first", align_bytes=64, offset=0)
         zero_bias = [
-            shared.tile([P, 1], F32, name="zero_bias%d" % k, align_bytes=64, offset=34816 + 4 * T * k) for k in range(2)
+            shared.tile([P, 32], F32, name="zero_bias%d" % k, align_bytes=64, offset=offset)
+            for k, offset in enumerate((34816, 34816 + 8 * T - 64))
         ]
         x_win = [x_first[:]] + [x_rest[:, s, :] for s in range(PASSES - 1)]
 
@@ -87,10 +90,10 @@ def tile_moe_sdn_lin_relu_kernel(
             nc.scalar.dma_start(win_i[32 * q : 32 * q + 4, : T // 4], x_scales_i[0, 4 * q : 4 * q + 4, :])
             nc.scalar.dma_start(win_i[32 * q - 8 : 32 * q, : T // 4], x_scales_i[1:, 4 * q : 4 * q + 4, :])
         for k in range(2):
-            nc.scalar.activation(zero_bias[k][:], zero_in[:], RELU)
+            nc.scalar.activation(zero_bias[k][:, :1], zero_in[:], RELU)
         w1_scales_i = w1_scales.bitcast(I32).rearrange("e s (q r) n -> r q (e s) n", r=4)
-        nc.sync.dma_start(gate_rows[: 2 * BLOCKS, :], gate[:, 0, :].rearrange("r (b m) -> r b m", m=P))
         nc.sync.dma_start(x_rest[:], x_words_i[:, 1:, :])
+        nc.sync.dma_start(gate_rows[: 2 * BLOCKS, :], gate[:, 0, :].rearrange("r (b m) -> r b m", m=P))
         nc.sync.dma_start(w1_first[:].bitcast(I32), w1_words_i[:, : 2 * PASSES, :])
         for r in range(4):
             nc.sync.dma_start(w1_scale[r:P:32, : 2 * PASSES, :].bitcast(I32), w1_scales_i[r][:, : 2 * PASSES])
@@ -120,32 +123,23 @@ def tile_moe_sdn_lin_relu_kernel(
         for pair in (1, 2):
             nc.sync.dma_start(w1_sb[pair].bitcast(I32), w1_words_i[:, 2 * PASSES * pair : 2 * PASSES * (pair + 1), :])
 
-        bank = next_bank([P, P], "gate_turned")
-        nc.tensor.transpose(bank[:], gate_rows[:], ident[:])
-        gate_cols = keep.tile([P, 2 * BLOCKS], F32, name="gate_cols")
-        nc.scalar.copy(gate_cols[:], bank[:, : 2 * BLOCKS])
-        g1, g2 = gate_cols[:, :BLOCKS], gate_cols[:, BLOCKS:]
-        square = keep.tile([P, BLOCKS], F32, name="square")
-        lift = keep.tile([P, BLOCKS], F32, name="lift")
-        lifted = shared.tile([P, BLOCKS], F32, name="lifted", align_bytes=64, offset=24576)
+        gate_cols = next_bank([P, P], "gate_cols")
+        nc.tensor.transpose(gate_cols[:], gate_rows[:], ident[:])
+        g1, g2 = gate_cols[:, :BLOCKS], gate_cols[:, BLOCKS : 2 * BLOCKS]
+        floor = shared.tile([P, BLOCKS], F32, name="floor", align_bytes=64, offset=19456)
         pivot = keep.tile([P, BLOCKS], F32, name="pivot")
         inverse = keep.tile([P, BLOCKS], F32, name="inverse")
         ratio_cols = keep.tile([P, BLOCKS], F32, name="ratio_cols")
-        nc.gpsimd.tensor_tensor(square[:], g2, g2, ALU.mult)
-        nc.gpsimd.tensor_scalar(lift[:], square[:], TINY * TINY, 2 * TINY, ALU.is_lt, ALU.mult)
-        nc.gpsimd.tensor_tensor(lifted[:], g2, lift[:], ALU.add)
-        nc.scalar.copy(pivot[:], lifted[:])
-
-        early_words = shared.tile([P, 3 * 512], U32, name="early_words", align_bytes=64, offset=18432)
-        for k, (s, first) in enumerate(((0, 512), (1, 0), (2, 0))):
-            gather_words(early_words[:, 512 * k : 512 * (k + 1)], s, first, 512)
-        nc.vector.reciprocal(inverse[:], lifted[:])
+        nc.vector.tensor_scalar(floor[:], g2, -TINY, -HUGE, ALU.is_le, ALU.mult)
+        nc.vector.scalar_tensor_tensor(pivot[:], floor[:], TINY, g2, ALU.add, ALU.max)
+        nc.vector.reciprocal(inverse[:], pivot[:])
         for b in range(BLOCKS):
             nc.scalar.activation(ratio_cols[:, b : b + 1], g1[:, b : b + 1], COPY, scale=inverse[:, b : b + 1])
-        late_words = shared.tile([P, 5 * 512], U32, name="late_words", align_bytes=64, offset=24576)
+
+        later_words = shared.tile([P, PASSES * S - FIRST_GATHER[2]], U32, name="later_words", align_bytes=64, offset=18432)
         col = 0
         for s, first, n in LATER_GATHERS:
-            gather_words(late_words[:, col : col + n], s, first, n)
+            gather_words(later_words[:, col : col + n], s, first, n)
             col += n
 
         hidden = [keep.tile([P, S], F32, name="hidden%d" % j) for j in range(PLANES)]
@@ -163,7 +157,7 @@ def tile_moe_sdn_lin_relu_kernel(
             )
 
         def relu(j, first, acc):
-            nc.scalar.activation(hidden[j][:, first : first + acc.shape[1]], acc, RELU, bias=zero_bias[j // 2][:])
+            nc.scalar.activation(hidden[j][:, first : first + acc.shape[1]], acc, RELU, bias=zero_bias[j // 2][:, :1])
 
         def unit(j, first, n):
             acc = next_bank([P, n], "acc")
@@ -175,20 +169,24 @@ def tile_moe_sdn_lin_relu_kernel(
         def expert_plane(j, e):
             unit(j, e * C, C)
 
-        opened = [(j, slot, next_bank([P, P], "acc")) for j in range(2) for slot in range(0, 2 * C, P)]
-        for s in range(PASSES):
-            for j, slot, acc in opened:
-                mx_pass(acc[:], j, slot, s, s == 0, s == PASSES - 1)
+        opened = [(j, slot, next_bank([P, P], "acc")) for slot in range(0, 3 * P, P) for j in range(2)]
         for j, slot, acc in opened:
-            relu(j, slot, acc[:])
-
+            mx_pass(acc[:], j, slot, 0, True, False)
         ratio = keep.tile([P, T], F32, name="ratio")
         for first in range(0, BLOCKS, 3):
             bank = next_bank([P, 3, P], "spread")
             for b in range(3):
                 nc.tensor.transpose(bank[:, b, :], ratio_cols[:, first + b : first + b + 1].to_broadcast([P, P]), ident[:])
             nc.scalar.copy(ratio[:, first * P : (first + 3) * P], bank[:].rearrange("p b t -> p (b t)"))
-
+        for s in range(1, PASSES):
+            for j, slot, acc in opened:
+                mx_pass(acc[:], j, slot, s, False, s == PASSES - 1)
+        for j, slot, acc in opened:
+            relu(j, slot, acc[:])
+        for j in range(2):
+            unit(j, 3 * P, P)
+        expert_plane(2, 0)
+        expert_plane(2, 1)
         for j in range(2):
             expert_plane(j, 2)
             expert_plane(j, 3)
@@ -197,9 +195,10 @@ def tile_moe_sdn_lin_relu_kernel(
         unit(0, S - P, P)
         expert_plane(1, 4)
         expert_plane(1, 5)
-        for j in (2, 3):
-            for e in range(E):
-                expert_plane(j, e)
+        for e in range(2, E):
+            expert_plane(2, e)
+        for e in range(E):
+            expert_plane(3, e)
         w2_scales_i = w2_scales.bitcast(I32).rearrange("s (q r) n -> r q (s n)", r=4)
         for r in range(4):
             nc.sync.dma_start(w1_scale[4 + r : P : 32, 0, :N].bitcast(I32), w2_scales_i[r])
@@ -211,18 +210,23 @@ def tile_moe_sdn_lin_relu_kernel(
         c_words = keep.tile([P, T], U32, name="c_words", align_bytes=64)
         c_scale = keep.tile([P, T], U8, name="c_scale", align_bytes=64)
         res = keep.tile([P, T], F32, name="res")
-        scaled = [keep.tile([P, T], F32, name="scaled%d" % j) for j in range(PLANES)]
+        scaled = {(j, 0): keep.tile([P, T if j < 2 else 512], F32, name="scaled%d" % j) for j in range(PLANES)}
+        scaled[2, 512] = shared.tile([P, 256], F32, name="scaled2_late", align_bytes=64, offset=34816 + 8 * T)
+        scaled[3, 512] = keep.tile([P, 256], F32, name="scaled3_late")
         sums = {j: keep.tile([P, T], F32, name="sum%d" % j) for j in (1, 3)}
         for j in (0, 2):
             sums[j] = shared.tile([P, T], F32, name="sum%d" % j, align_bytes=64, offset=34816 + 2 * T * j)
 
-        def gather_scaled(j):
-            nc.vector.tensor_tensor(scaled[j][:], hidden[j][:].indirect(pos_sb[0][:]), ratio[:], ALU.mult)
+        def gather_scaled(j, first, n):
+            offsets = pos_sb[0][:, first // 16 : (first + n) // 16]
+            nc.vector.tensor_tensor(scaled[j, first][:], hidden[j][:].indirect(offsets), ratio[:, first : first + n], ALU.mult)
 
         def gather_sum(j, first, n):
             offsets = pos_sb[1][:, first // 16 : (first + n) // 16]
             cols = slice(first, first + n)
-            nc.vector.tensor_tensor(sums[j][:, cols], hidden[j][:].indirect(offsets), scaled[j][:, cols], ALU.add)
+            base = 512 if j >= 2 and first >= 512 else 0
+            other = scaled[j, base][:, first - base : first - base + n]
+            nc.vector.tensor_tensor(sums[j][:, cols], hidden[j][:].indirect(offsets), other, ALU.add)
 
         def turn(j, first, n, tag):
             bank = psum.tile([P, n // P, 2, P], F32, name="turned", tag=tag)
@@ -238,8 +242,8 @@ def tile_moe_sdn_lin_relu_kernel(
                     scale=pivot[:, block : block + 1],
                 )
 
-        def turn_back(first, n, copy):
-            bank = next_bank([P, n // P, 2, P], "back")
+        def turn_back(first, n, copy, tag):
+            bank = psum.tile([P, n // P, 2, P], F32, name="back", tag=tag)
             for b in range(n // P):
                 for u in range(2):
                     pairs = c_tok[:, first // P + b, u, :, :].rearrange("p m v -> p (m v)").bitcast(F32)
@@ -271,30 +275,33 @@ def tile_moe_sdn_lin_relu_kernel(
             nc.sync.dma_start(out[:, cols], res[:, cols])
 
         on_scalar, on_vector = nc.scalar.copy, nc.vector.tensor_copy
-        gather_scaled(0)
-        gather_scaled(1)
+        a, b, c, last = (0, 256), (256, 256), (512, 128), (640, 128)
+        gather_scaled(0, 0, T)
+        gather_scaled(1, 0, T)
         gather_sum(0, 0, T)
         gather_sum(1, 0, T)
-        gather_scaled(2)
-        gather_scaled(3)
+        gather_scaled(2, 0, 512)
+        gather_scaled(3, 0, 512)
         for first in range(0, T, 256):
             turn(0, first, 256, next_tag())
-        a, b, c, last = (0, 256), (256, 256), (512, 128), (640, 128)
-        for chunk in (a, b, c, last):
+        for chunk in (a, b):
             gather_sum(2, *chunk)
             gather_sum(3, *chunk)
-        tags = [next_tag(), next_tag()]
+        gather_scaled(2, 512, 256)
+        gather_scaled(3, 512, 256)
+        gather_sum(2, 512, 256)
+        gather_sum(3, *c)
+        gather_sum(3, *last)
+        tags = [next_tag() for k in range(3)]
         turn(2, *a, tags[0])
         turn(2, *b, tags[1])
-        turn_back(*a, on_vector)
-        turn(2, *c, tags[0])
-        turn(2, *last, tags[1])
-        turn_back(*b, on_scalar)
-        quantize(*a)
-        turn_back(*c, on_vector)
-        turn_back(*last, on_scalar)
-        quantize(*b)
+        turn_back(*a, on_scalar, tags[2])
+        turn_back(*b, on_vector, next_tag())
+        turn(2, *c, tags[1])
+        turn(2, *last, tags[2])
+        quantize(0, 512)
+        turn_back(*c, on_scalar, next_tag())
+        turn_back(*last, on_scalar, next_tag())
         quantize(512, 256)
-        project(*a, on_scalar)
-        project(*b, on_scalar)
+        project(0, 512, on_scalar)
         project(512, 256, on_vector)

@@ -85,10 +85,10 @@ def tile_moe_sdn_lin_relu_kernel(
         nc.sync.dma_start(x_first[:], x_words_i[:, 0, :])
         x_scales_i = x_scales.bitcast(I32)
         for q in range(2):
-            nc.sync.dma_start(win_i[32 * q : 32 * q + 12, : T // 4], x_scales_i[:, 4 * q : 4 * q + 4, :])
+            nc.scalar.dma_start(win_i[32 * q : 32 * q + 12, : T // 4], x_scales_i[:, 4 * q : 4 * q + 4, :])
         for q in range(2, 4):
-            nc.scalar.dma_start(win_i[32 * q : 32 * q + 4, : T // 4], x_scales_i[0, 4 * q : 4 * q + 4, :])
-            nc.scalar.dma_start(win_i[32 * q - 8 : 32 * q, : T // 4], x_scales_i[1:, 4 * q : 4 * q + 4, :])
+            nc.sync.dma_start(win_i[32 * q : 32 * q + 4, : T // 4], x_scales_i[0, 4 * q : 4 * q + 4, :])
+            nc.sync.dma_start(win_i[32 * q - 8 : 32 * q, : T // 4], x_scales_i[1:, 4 * q : 4 * q + 4, :])
         for k in range(2):
             nc.scalar.activation(zero_bias[k][:, :1], zero_in[:], RELU)
         w1_scales_i = w1_scales.bitcast(I32).rearrange("e s (q r) n -> r q (e s) n", r=4)
@@ -259,9 +259,9 @@ def tile_moe_sdn_lin_relu_kernel(
                 out=c_words[:, cols].bitcast(FP8X4), scales=c_scale[:, cols], in_=grouped[:, 4 * first : 4 * (first + n)]
             )
 
-        def project(first, n, copy):
+        def project(first, n, copy, tag):
             cols = slice(first, first + n)
-            bank = next_bank([P, n], "projected")
+            bank = psum.tile([P, n], F32, name="projected", tag=tag)
             nc.tensor.matmul_mx(
                 out=bank[:],
                 lhsT=w2_sb[:].bitcast(FP8X4),
@@ -289,19 +289,23 @@ def tile_moe_sdn_lin_relu_kernel(
             gather_sum(3, *chunk)
         gather_scaled(2, 512, 256)
         gather_scaled(3, 512, 256)
-        gather_sum(2, 512, 256)
-        gather_sum(3, *c)
-        gather_sum(3, *last)
-        tags = [next_tag() for k in range(3)]
+        for chunk in (c, last):
+            gather_sum(2, *chunk)
+            gather_sum(3, *chunk)
+        tags = [next_tag() for k in range(5)]
         turn(2, *a, tags[0])
         turn(2, *b, tags[1])
         turn_back(*a, on_scalar, tags[2])
+        quantize(*a)
         turn_back(*b, on_vector, next_tag())
         turn(2, *c, tags[1])
         turn(2, *last, tags[2])
-        quantize(0, 512)
-        turn_back(*c, on_scalar, next_tag())
-        turn_back(*last, on_scalar, next_tag())
-        quantize(512, 256)
-        project(0, 512, on_scalar)
-        project(512, 256, on_vector)
+        turn_back(*c, on_scalar, tags[3])
+        turn_back(*last, on_scalar, tags[4])
+        quantize(*b)
+        quantize(*c)
+        quantize(*last)
+        project(*a, on_scalar, tags[2])
+        project(*b, on_scalar, tags[3])
+        project(*c, on_vector, tags[4])
+        project(*last, on_vector, tags[0])

@@ -85,10 +85,10 @@ def tile_moe_sdn_lin_relu_kernel(
         nc.sync.dma_start(x_first[:], x_words_i[:, 0, :])
         x_scales_i = x_scales.bitcast(I32)
         for q in range(2):
-            nc.scalar.dma_start(win_i[32 * q : 32 * q + 12, : T // 4], x_scales_i[:, 4 * q : 4 * q + 4, :])
+            nc.sync.dma_start(win_i[32 * q : 32 * q + 12, : T // 4], x_scales_i[:, 4 * q : 4 * q + 4, :])
         for q in range(2, 4):
-            nc.sync.dma_start(win_i[32 * q : 32 * q + 4, : T // 4], x_scales_i[0, 4 * q : 4 * q + 4, :])
-            nc.sync.dma_start(win_i[32 * q - 8 : 32 * q, : T // 4], x_scales_i[1:, 4 * q : 4 * q + 4, :])
+            nc.scalar.dma_start(win_i[32 * q : 32 * q + 4, : T // 4], x_scales_i[0, 4 * q : 4 * q + 4, :])
+            nc.scalar.dma_start(win_i[32 * q - 8 : 32 * q, : T // 4], x_scales_i[1:, 4 * q : 4 * q + 4, :])
         for k in range(2):
             nc.scalar.activation(zero_bias[k][:, :1], zero_in[:], RELU)
         w1_scales_i = w1_scales.bitcast(I32).rearrange("e s (q r) n -> r q (e s) n", r=4)
@@ -186,7 +186,6 @@ def tile_moe_sdn_lin_relu_kernel(
         for j in range(2):
             unit(j, 3 * P, P)
         expert_plane(2, 0)
-        expert_plane(2, 1)
         for j in range(2):
             expert_plane(j, 2)
             expert_plane(j, 3)
@@ -195,7 +194,7 @@ def tile_moe_sdn_lin_relu_kernel(
         unit(0, S - P, P)
         expert_plane(1, 4)
         expert_plane(1, 5)
-        for e in range(2, E):
+        for e in range(1, E):
             expert_plane(2, e)
         for e in range(E):
             expert_plane(3, e)

@@ -74,7 +74,10 @@ def tile_moe_sdn_lin_relu_kernel(
         w1_words_i = w1_words.bitcast(I32).rearrange("e s p n -> p (e s) n")
         x_first = keep.tile([P, T], I32, name="x_first", align_bytes=64)
         x_rest = keep.tile([P, PASSES - 1, T], I32, name="x_rest", align_bytes=64)
-        w1_first = shared.tile([P, 2 * PASSES, 2 * H], U8, name="w1_first", align_bytes=64, offset=0)
+        w1_low = [keep.tile([P, 2 * PASSES, H], U8, name="w1_low%d" % pair, align_bytes=64) for pair in range(E // 2)]
+        w1_high = [
+            shared.tile([P, 3 * PASSES, H], U8, name="w1_high%d" % k, align_bytes=64, offset=3 * PASSES * H * k) for k in range(2)
+        ]
         zero_bias = [
             shared.tile([P, 32], F32, name="zero_bias%d" % k, align_bytes=64, offset=offset)
             for k, offset in enumerate((34816, 34816 + 8 * T - 64))
@@ -94,7 +97,7 @@ def tile_moe_sdn_lin_relu_kernel(
         w1_scales_i = w1_scales.bitcast(I32).rearrange("e s (q r) n -> r q (e s) n", r=4)
         nc.sync.dma_start(x_rest[:], x_words_i[:, 1:, :])
         nc.sync.dma_start(gate_rows[: 2 * BLOCKS, :], gate[:, 0, :].rearrange("r (b m) -> r b m", m=P))
-        nc.sync.dma_start(w1_first[:].bitcast(I32), w1_words_i[:, : 2 * PASSES, :])
+        nc.sync.dma_start(w1_low[0][:].bitcast(I32), w1_words_i[:, : 2 * PASSES, : H // 4])
         for r in range(4):
             nc.sync.dma_start(w1_scale[r:P:32, : 2 * PASSES, :].bitcast(I32), w1_scales_i[r][:, : 2 * PASSES])
         for r, pos in enumerate((pos1, pos2)):
@@ -118,10 +121,12 @@ def tile_moe_sdn_lin_relu_kernel(
                 )
         for r in range(4):
             nc.sync.dma_start(w1_scale[r:P:32, 2 * PASSES :, :].bitcast(I32), w1_scales_i[r][:, 2 * PASSES :])
-        w1_rest = shared.tile([P, 4 * PASSES, 2 * H], U8, name="w1_rest", align_bytes=64, offset=6144)
-        w1_sb = [w1_first[:], w1_rest[:, : 2 * PASSES, :], w1_rest[:, 2 * PASSES :, :]]
         for pair in (1, 2):
-            nc.sync.dma_start(w1_sb[pair].bitcast(I32), w1_words_i[:, 2 * PASSES * pair : 2 * PASSES * (pair + 1), :])
+            nc.sync.dma_start(
+                w1_low[pair][:].bitcast(I32), w1_words_i[:, 2 * PASSES * pair : 2 * PASSES * (pair + 1), : H // 4]
+            )
+        for k in range(2):
+            nc.sync.dma_start(w1_high[k][:].bitcast(I32), w1_words_i[:, 3 * PASSES * k : 3 * PASSES * (k + 1), H // 4 :])
 
         gate_cols = next_bank([P, P], "gate_cols")
         nc.tensor.transpose(gate_cols[:], gate_rows[:], ident[:])
@@ -146,9 +151,10 @@ def tile_moe_sdn_lin_relu_kernel(
 
         def mx_pass(acc, j, slot, s, start, stop):
             e = slot // C
+            words = w1_low[e // 2][:, (e % 2) * PASSES + s, :] if j < 2 else w1_high[e // 3][:, (e % 3) * PASSES + s, :]
             nc.tensor.matmul_mx(
                 out=acc,
-                lhsT=w1_sb[e // 2][:, (e % 2) * PASSES + s, 2 * P * j : 2 * P * (j + 1)].bitcast(FP4X4),
+                lhsT=words[:, 2 * P * (j % 2) : 2 * P * (j % 2 + 1)].bitcast(FP4X4),
                 lhsT_scale=w1_scale[:, e * PASSES + s, P * j : P * (j + 1)],
                 rhs=slot_words[s, slot].bitcast(FP8X4),
                 rhs_scale=slot_scale[s][:, slot : slot + P],
@@ -185,7 +191,6 @@ def tile_moe_sdn_lin_relu_kernel(
             relu(j, slot, acc[:])
         for j in range(2):
             unit(j, 3 * P, P)
-        expert_plane(2, 0)
         for j in range(2):
             expert_plane(j, 2)
             expert_plane(j, 3)
@@ -194,10 +199,12 @@ def tile_moe_sdn_lin_relu_kernel(
         unit(0, S - P, P)
         expert_plane(1, 4)
         expert_plane(1, 5)
-        for e in range(1, E):
-            expert_plane(2, e)
         for e in range(E):
+            expert_plane(2, e)
+        for e in range(E - 1):
             expert_plane(3, e)
+        unit(3, S - 2 * P, P)
+        unit(3, S - P, P)
         w2_scales_i = w2_scales.bitcast(I32).rearrange("s (q r) n -> r q (s n)", r=4)
         for r in range(4):
             nc.sync.dma_start(w1_scale[4 + r : P : 32, 0, :N].bitcast(I32), w2_scales_i[r])

@@ -23,12 +23,11 @@ P = 128
 PASSES = K // 512
 PLANES = H // P
 SCALE_WINDOW = 2048
-FIRST_GATHER = (0, 0, 512)
+FIRST_SLOTS = 512
 LATER_GATHERS = [
     (1, 0, 512), (2, 0, 512), (0, 512, 512), (1, 512, 512), (2, 512, 512),
-    (0, 1024, 512), (1, 1024, 512), (2, 1024, 256), (2, 1280, 128), (2, 1408, 128),
+    (0, 1024, 512), (1, 1024, 512), (2, 1024, 256), (2, 1280, 256),
 ]
-BANKS = 8
 BLOCKS = T // P
 TINY = 2.0**-60
 HUGE = 2.0**127
@@ -44,14 +43,8 @@ def tile_moe_sdn_lin_relu_kernel(
         shared = ctx.enter_context(tc.tile_pool(name="shared", bufs=1))
         psum = ctx.enter_context(tc.psum_pool(name="psum", bufs=1))
 
-        taken = []
-
-        def next_tag():
-            taken.append(len(taken) % BANKS)
-            return "bank%d" % taken[-1]
-
-        def next_bank(shape, name):
-            return psum.tile(shape, F32, name=name, tag=next_tag())
+        def bank(k, shape, name):
+            return psum.tile(shape, F32, name=name, tag="bank%d" % k)
 
         offs_sb = lists.tile([P, S // 16], U16, name="offs_sb")
         pos_sb = [lists.tile([P, T // 16], U16, name="pos%d_sb" % r) for r in range(2)]
@@ -74,13 +67,12 @@ def tile_moe_sdn_lin_relu_kernel(
         w1_words_i = w1_words.bitcast(I32).rearrange("e s p n -> p (e s) n")
         x_first = keep.tile([P, T], I32, name="x_first", align_bytes=64)
         x_rest = keep.tile([P, PASSES - 1, T], I32, name="x_rest", align_bytes=64)
-        w1_low = [keep.tile([P, 2 * PASSES, H], U8, name="w1_low%d" % pair, align_bytes=64) for pair in range(E // 2)]
-        w1_high = [
-            shared.tile([P, 3 * PASSES, H], U8, name="w1_high%d" % k, align_bytes=64, offset=3 * PASSES * H * k) for k in range(2)
+        w1_pair = [shared.tile([P, 2 * PASSES, 2 * H], U8, name="w1_pair0", align_bytes=64, offset=0)] + [
+            keep.tile([P, 2 * PASSES, 2 * H], U8, name="w1_pair%d" % pair, align_bytes=64) for pair in range(1, E // 2)
         ]
         zero_bias = [
             shared.tile([P, 32], F32, name="zero_bias%d" % k, align_bytes=64, offset=offset)
-            for k, offset in enumerate((34816, 34816 + 8 * T - 64))
+            for k, offset in enumerate((34816, 35840 + 4 * T - 64))
         ]
         x_win = [x_first[:]] + [x_rest[:, s, :] for s in range(PASSES - 1)]
 
@@ -97,7 +89,7 @@ def tile_moe_sdn_lin_relu_kernel(
         w1_scales_i = w1_scales.bitcast(I32).rearrange("e s (q r) n -> r q (e s) n", r=4)
         nc.sync.dma_start(x_rest[:], x_words_i[:, 1:, :])
         nc.sync.dma_start(gate_rows[: 2 * BLOCKS, :], gate[:, 0, :].rearrange("r (b m) -> r b m", m=P))
-        nc.sync.dma_start(w1_low[0][:].bitcast(I32), w1_words_i[:, : 2 * PASSES, : H // 4])
+        nc.sync.dma_start(w1_pair[0][:].bitcast(I32), w1_words_i[:, : 2 * PASSES, :])
         for r in range(4):
             nc.sync.dma_start(w1_scale[r:P:32, : 2 * PASSES, :].bitcast(I32), w1_scales_i[r][:, : 2 * PASSES])
         for r, pos in enumerate((pos1, pos2)):
@@ -108,11 +100,14 @@ def tile_moe_sdn_lin_relu_kernel(
         def gather_words(g, s, first, n):
             offsets = offs_sb[:, first // 16 : (first + n) // 16]
             nc.vector.tensor_copy(g, x_win[s].bitcast(U32).indirect(offsets))
-            for col in range(0, n, P):
-                slot_words[s, first + col] = g[:, col : col + P]
+            for col in range(0, n, C):
+                slot_words[s, (first + col) // C] = g[:, col : col + C]
 
-        first_words = keep.tile([P, FIRST_GATHER[2]], U32, name="first_words", align_bytes=64)
-        gather_words(first_words[:], *FIRST_GATHER)
+        first_words = [
+            shared.tile([P, C], U32, name="first_words%d" % e, align_bytes=64, offset=6144 + 4 * C * e) for e in range(2)
+        ]
+        for e in range(2):
+            gather_words(first_words[e][:], 0, e * C, C)
         nc.vector.tensor_copy(slot_scale[0][:], x_scale_win[:].indirect(offs_sb[:]))
         for s in range(1, PASSES):
             for row, first in ((0, 4 * s), (64, 52 + 4 * s)):
@@ -122,26 +117,22 @@ def tile_moe_sdn_lin_relu_kernel(
         for r in range(4):
             nc.sync.dma_start(w1_scale[r:P:32, 2 * PASSES :, :].bitcast(I32), w1_scales_i[r][:, 2 * PASSES :])
         for pair in (1, 2):
-            nc.sync.dma_start(
-                w1_low[pair][:].bitcast(I32), w1_words_i[:, 2 * PASSES * pair : 2 * PASSES * (pair + 1), : H // 4]
-            )
-        for k in range(2):
-            nc.sync.dma_start(w1_high[k][:].bitcast(I32), w1_words_i[:, 3 * PASSES * k : 3 * PASSES * (k + 1), H // 4 :])
+            nc.sync.dma_start(w1_pair[pair][:].bitcast(I32), w1_words_i[:, 2 * PASSES * pair : 2 * PASSES * (pair + 1), :])
 
-        gate_cols = next_bank([P, P], "gate_cols")
+        gate_cols = bank(6, [P, P], "gate_cols")
         nc.tensor.transpose(gate_cols[:], gate_rows[:], ident[:])
         g1, g2 = gate_cols[:, :BLOCKS], gate_cols[:, BLOCKS : 2 * BLOCKS]
         floor = shared.tile([P, BLOCKS], F32, name="floor", align_bytes=64, offset=19456)
         pivot = keep.tile([P, BLOCKS], F32, name="pivot")
         inverse = keep.tile([P, BLOCKS], F32, name="inverse")
-        ratio_cols = keep.tile([P, BLOCKS], F32, name="ratio_cols")
+        ratio_cols = shared.tile([P, BLOCKS], F32, name="ratio_cols", align_bytes=64, offset=6144)
         nc.vector.tensor_scalar(floor[:], g2, -TINY, -HUGE, ALU.is_le, ALU.mult)
         nc.vector.scalar_tensor_tensor(pivot[:], floor[:], TINY, g2, ALU.add, ALU.max)
         nc.vector.reciprocal(inverse[:], pivot[:])
         for b in range(BLOCKS):
             nc.scalar.activation(ratio_cols[:, b : b + 1], g1[:, b : b + 1], COPY, scale=inverse[:, b : b + 1])
 
-        later_words = shared.tile([P, PASSES * S - FIRST_GATHER[2]], U32, name="later_words", align_bytes=64, offset=18432)
+        later_words = shared.tile([P, PASSES * S - FIRST_SLOTS], U32, name="later_words", align_bytes=64, offset=18432)
         col = 0
         for s, first, n in LATER_GATHERS:
             gather_words(later_words[:, col : col + n], s, first, n)
@@ -149,169 +140,188 @@ def tile_moe_sdn_lin_relu_kernel(
 
         hidden = [keep.tile([P, S], F32, name="hidden%d" % j) for j in range(PLANES)]
 
-        def mx_pass(acc, j, slot, s, start, stop):
-            e = slot // C
-            words = w1_low[e // 2][:, (e % 2) * PASSES + s, :] if j < 2 else w1_high[e // 3][:, (e % 3) * PASSES + s, :]
+        def mx_pass(acc, j, e, s, start, stop):
             nc.tensor.matmul_mx(
                 out=acc,
-                lhsT=words[:, 2 * P * (j % 2) : 2 * P * (j % 2 + 1)].bitcast(FP4X4),
+                lhsT=w1_pair[e // 2][:, (e % 2) * PASSES + s, 2 * P * j : 2 * P * (j + 1)].bitcast(FP4X4),
                 lhsT_scale=w1_scale[:, e * PASSES + s, P * j : P * (j + 1)],
-                rhs=slot_words[s, slot].bitcast(FP8X4),
-                rhs_scale=slot_scale[s][:, slot : slot + P],
+                rhs=slot_words[s, e].bitcast(FP8X4),
+                rhs_scale=slot_scale[s][:, e * C : (e + 1) * C],
                 start=start,
                 stop=stop,
             )
 
-        def relu(j, first, acc):
-            nc.scalar.activation(hidden[j][:, first : first + acc.shape[1]], acc, RELU, bias=zero_bias[j // 2][:, :1])
+        def relu(j, e, acc):
+            nc.scalar.activation(hidden[j][:, e * C : e * C + acc.shape[1]], acc, RELU, bias=zero_bias[j // 3][:, :1])
 
-        def unit(j, first, n):
-            acc = next_bank([P, n], "acc")
-            for col in range(0, n, P):
+        def pair_plane(j, pair, k):
+            acc = bank(k, [P, 2 * C], "acc")
+            for h in range(2):
                 for s in range(PASSES):
-                    mx_pass(acc[:, col : col + P], j, first + col, s, s == 0, s == PASSES - 1)
-            relu(j, first, acc[:])
+                    mx_pass(acc[:, h * C : (h + 1) * C], j, 2 * pair + h, s, s == 0, s == PASSES - 1)
+            relu(j, 2 * pair, acc[:])
 
-        def expert_plane(j, e):
-            unit(j, e * C, C)
-
-        opened = [(j, slot, next_bank([P, P], "acc")) for slot in range(0, 3 * P, P) for j in range(2)]
-        for j, slot, acc in opened:
-            mx_pass(acc[:], j, slot, 0, True, False)
+        first_acc = [bank(j, [P, 2 * C], "acc") for j in range(PLANES)]
+        for e in range(2):
+            for j in range(PLANES):
+                mx_pass(first_acc[j][:, e * C : (e + 1) * C], j, e, 0, e == 0, False)
         ratio = keep.tile([P, T], F32, name="ratio")
         for first in range(0, BLOCKS, 3):
-            bank = next_bank([P, 3, P], "spread")
+            spread = bank(4 + first // 3, [P, 3, P], "spread")
             for b in range(3):
-                nc.tensor.transpose(bank[:, b, :], ratio_cols[:, first + b : first + b + 1].to_broadcast([P, P]), ident[:])
-            nc.scalar.copy(ratio[:, first * P : (first + 3) * P], bank[:].rearrange("p b t -> p (b t)"))
-        for s in range(1, PASSES):
-            for j, slot, acc in opened:
-                mx_pass(acc[:], j, slot, s, False, s == PASSES - 1)
-        for j, slot, acc in opened:
-            relu(j, slot, acc[:])
-        for j in range(2):
-            unit(j, 3 * P, P)
-        for j in range(2):
-            expert_plane(j, 2)
-            expert_plane(j, 3)
-        expert_plane(0, 4)
-        unit(0, S - 2 * P, P)
-        unit(0, S - P, P)
-        expert_plane(1, 4)
-        expert_plane(1, 5)
-        for e in range(E):
-            expert_plane(2, e)
-        for e in range(E - 1):
-            expert_plane(3, e)
-        unit(3, S - 2 * P, P)
-        unit(3, S - P, P)
+                nc.tensor.transpose(spread[:, b, :], ratio_cols[:, first + b : first + b + 1].to_broadcast([P, P]), ident[:])
+            nc.scalar.copy(ratio[:, first * P : (first + 3) * P], spread[:].rearrange("p b t -> p (b t)"))
+        for j in range(PLANES):
+            for s in range(1, PASSES):
+                for e in range(2):
+                    mx_pass(first_acc[j][:, e * C : (e + 1) * C], j, e, s, False, s == PASSES - 1 and e == 1)
+            relu(j, 0, first_acc[j][:])
+        for j, k in ((0, 7), (1, 6), (2, 4)):
+            pair_plane(j, 1, k)
+        last_acc = {(j, e): bank(k, [P, C], "acc") for j, e, k in ((0, 4, 5), (1, 4, 1), (0, 5, 0), (1, 5, 2))}
+        for s in range(PASSES):
+            for j, e in last_acc:
+                mx_pass(last_acc[j, e][:], j, e, s, s == 0, s == PASSES - 1)
+        relu(0, 4, last_acc[0, 4][:])
+        nc.vector.tensor_scalar_max(hidden[1][:, 4 * C : 5 * C], last_acc[1, 4][:], 0.0)
+        relu(0, 5, last_acc[0, 5][:])
+        relu(1, 5, last_acc[1, 5][:])
+
+        a, b, c, last = (0, 256), (256, 256), (512, 128), (640, 128)
+        scaled = [keep.tile([P, T], F32, name="scaled%d" % j) for j in range(3)]
+        scaled3 = {0: keep.tile([P, 512], F32, name="scaled3_early"), 512: keep.tile([P, 256], F32, name="scaled3_late")}
+        plain0 = keep.tile([P, T], F32, name="plain0")
+        plain1 = shared.tile([P, T], F32, name="plain1", align_bytes=64, offset=35840 + 4 * T)
+        plain2 = shared.tile([P, T], F32, name="plain2", align_bytes=64, offset=35840)
+        sum3 = {first: keep.tile([P, n], F32, name="sum3_%d" % first) for first, n in (a, b, c, last)}
+
+        def gather_scaled(dst, j, first):
+            n = dst.shape[1]
+            offsets = pos_sb[0][:, first // 16 : (first + n) // 16]
+            nc.vector.tensor_tensor(dst, hidden[j][:].indirect(offsets), ratio[:, first : first + n], ALU.mult)
+
+        def gather_plain(dst, j, first):
+            offsets = pos_sb[1][:, first // 16 : (first + dst.shape[1]) // 16]
+            nc.scalar.activation(dst, hidden[j][:].indirect(offsets), COPY)
+
+        def gather_sum(first, n):
+            offsets = pos_sb[1][:, first // 16 : (first + n) // 16]
+            base = 512 * (first // 512)
+            other = scaled3[base][:, first - base : first - base + n]
+            nc.vector.tensor_tensor(sum3[first][:], hidden[3][:].indirect(offsets), other, ALU.add)
+
+        gather_scaled(scaled[0][:], 0, 0)
+        gather_plain(plain0[:], 0, 0)
+        pair_plane(2, 2, 3)
+        pair_plane(3, 1, 5)
+        pair_plane(3, 2, 0)
         w2_scales_i = w2_scales.bitcast(I32).rearrange("s (q r) n -> r q (s n)", r=4)
         for r in range(4):
             nc.sync.dma_start(w1_scale[4 + r : P : 32, 0, :N].bitcast(I32), w2_scales_i[r])
         w2_sb = shared.tile([P, N], I32, name="w2_sb", align_bytes=64, offset=0)
         nc.sync.dma_start(w2_sb[:], w2_words[0].rearrange("p n d -> p (n d)").bitcast(I32))
 
-        c_tok = keep.tile([P, BLOCKS, 2, P, 2], BF16, name="c_tok", align_bytes=64)
-        grouped = keep.tile([P, 4 * T], BF16, name="grouped", align_bytes=64)
-        c_words = keep.tile([P, T], U32, name="c_words", align_bytes=64)
-        c_scale = keep.tile([P, T], U8, name="c_scale", align_bytes=64)
-        res = keep.tile([P, T], F32, name="res")
-        scaled = {(j, 0): keep.tile([P, T if j < 2 else 512], F32, name="scaled%d" % j) for j in range(PLANES)}
-        scaled[2, 512] = shared.tile([P, 256], F32, name="scaled2_late", align_bytes=64, offset=34816 + 8 * T)
-        scaled[3, 512] = keep.tile([P, 256], F32, name="scaled3_late")
-        sums = {j: keep.tile([P, T], F32, name="sum%d" % j) for j in (1, 3)}
-        for j in (0, 2):
-            sums[j] = shared.tile([P, T], F32, name="sum%d" % j, align_bytes=64, offset=34816 + 2 * T * j)
+        gather_scaled(scaled[1][:], 1, 0)
+        gather_scaled(scaled[2][:], 2, 0)
+        gather_plain(plain1[:], 1, 0)
+        for first in range(0, T, 256):
+            gather_plain(plain2[:, first : first + 256], 2, first)
+        for first in scaled3:
+            gather_scaled(scaled3[first][:], 3, first)
+        for chunk in (a, b, c, last):
+            gather_sum(*chunk)
 
-        def gather_scaled(j, first, n):
-            offsets = pos_sb[0][:, first // 16 : (first + n) // 16]
-            nc.vector.tensor_tensor(scaled[j, first][:], hidden[j][:].indirect(offsets), ratio[:, first : first + n], ALU.mult)
+        c_tok = [keep.tile([P, 2, P, 2], BF16, name="c_tok%d" % block, align_bytes=64) for block in range(BLOCKS)]
 
-        def gather_sum(j, first, n):
-            offsets = pos_sb[1][:, first // 16 : (first + n) // 16]
-            cols = slice(first, first + n)
-            base = 512 if j >= 2 and first >= 512 else 0
-            other = scaled[j, base][:, first - base : first - base + n]
-            nc.vector.tensor_tensor(sums[j][:, cols], hidden[j][:].indirect(offsets), other, ALU.add)
+        low = {first: bank(k, [P, 2, 2, P], "low") for first, k in ((0, 7), (256, 6))}
+        high = {first: bank(k, [P, 2, 2, P], "high") for first, k in ((0, 4), (256, 1))}
+        whole = {first: bank(k, [P, PLANES, P], "whole") for first, k in ((512, 2), (640, 3))}
 
-        def turn(j, first, n, tag):
-            bank = psum.tile([P, n // P, 2, P], F32, name="turned", tag=tag)
-            for k in range(2):
-                for b in range(n // P):
-                    nc.tensor.transpose(bank[:, b, k, :], sums[j + k][:, first + b * P : first + (b + 1) * P], ident[:])
-            for b in range(n // P):
-                block = first // P + b
-                nc.scalar.activation(
-                    c_tok[:, block, :, 32 * j : 32 * (j + 2), :],
-                    bank[:, b, :, :].rearrange("p k (m u v) -> p u (k m) v", u=2, v=2),
-                    COPY,
-                    scale=pivot[:, block : block + 1],
-                )
+        def turned(block, j):
+            if block >= 4:
+                return whole[block * P][:, j, :]
+            return (low if j < 2 else high)[256 * (block // 2)][:, block % 2, j % 2, :]
 
-        def turn_back(first, n, copy, tag):
-            bank = psum.tile([P, n // P, 2, P], F32, name="back", tag=tag)
+        def turn(j, block, terms):
+            for k, term in enumerate(terms):
+                nc.tensor.matmul(turned(block, j), term, ident[:], start=k == 0, stop=k == len(terms) - 1, is_transpose=True)
+
+        def cols(tile, block, base=0):
+            return tile[:, block * P - base : (block + 1) * P - base]
+
+        def round_on_scalar(dst, src, block):
+            nc.scalar.activation(dst, src, COPY, scale=pivot[:, block : block + 1])
+
+        def round_on_vector(dst, src, block):
+            nc.vector.tensor_scalar_mul(dst, src, pivot[:, block : block + 1])
+
+        def round_out(src, block, j, engine):
+            planes = src.shape[1]
+            engine(
+                c_tok[block][:, :, 32 * j : 32 * (j + planes), :],
+                src.rearrange("p k (m u v) -> p u (k m) v", u=2, v=2),
+                block,
+            )
+
+        grouped, c_words, c_scale = {}, {}, {}
+
+        def turn_back(first, n, copy, k):
+            back = bank(k, [P, n // P, 2, P], "back")
             for b in range(n // P):
                 for u in range(2):
-                    pairs = c_tok[:, first // P + b, u, :, :].rearrange("p m v -> p (m v)").bitcast(F32)
-                    nc.tensor.transpose(bank[:, b, u, :], pairs, ident[:])
+                    pairs = c_tok[first // P + b][:, u, :, :].rearrange("p m v -> p (m v)").bitcast(F32)
+                    nc.tensor.transpose(back[:, b, u, :], pairs, ident[:])
+            grouped[first] = keep.tile([P, 4 * n], BF16, name="grouped%d" % first, align_bytes=64)
             copy(
-                grouped[:, 4 * first : 4 * (first + n)].bitcast(F32).rearrange("p (b t u) -> p b t u", t=P, u=2),
-                bank[:].rearrange("p b u t -> p b t u"),
+                grouped[first][:].bitcast(F32).rearrange("p (b t u) -> p b t u", t=P, u=2),
+                back[:].rearrange("p b u t -> p b t u"),
             )
 
         def quantize(first, n):
-            cols = slice(first, first + n)
-            nc.vector.quantize_mx(
-                out=c_words[:, cols].bitcast(FP8X4), scales=c_scale[:, cols], in_=grouped[:, 4 * first : 4 * (first + n)]
-            )
+            c_words[first] = keep.tile([P, n], U32, name="c_words%d" % first, align_bytes=64)
+            c_scale[first] = keep.tile([P, n], U8, name="c_scale%d" % first, align_bytes=64)
+            nc.vector.quantize_mx(out=c_words[first][:].bitcast(FP8X4), scales=c_scale[first][:], in_=grouped[first][:])
 
-        def project(first, n, copy, tag):
-            cols = slice(first, first + n)
-            bank = psum.tile([P, n], F32, name="projected", tag=tag)
+        def project(first, n, copy, k):
+            projected = bank(k, [P, n], "projected")
             nc.tensor.matmul_mx(
-                out=bank[:],
+                out=projected[:],
                 lhsT=w2_sb[:].bitcast(FP8X4),
                 lhsT_scale=w1_scale[4:P, 0, :N],
-                rhs=c_words[:, cols].bitcast(FP8X4),
-                rhs_scale=c_scale[:, cols],
+                rhs=c_words[first][:].bitcast(FP8X4),
+                rhs_scale=c_scale[first][:],
                 start=True,
                 stop=True,
             )
-            copy(res[:, cols], bank[:])
-            nc.sync.dma_start(out[:, cols], res[:, cols])
+            res = keep.tile([P, n], F32, name="res%d" % first)
+            copy(res[:], projected[:])
+            nc.sync.dma_start(out[:, first : first + n], res[:])
 
         on_scalar, on_vector = nc.scalar.copy, nc.vector.tensor_copy
-        a, b, c, last = (0, 256), (256, 256), (512, 128), (640, 128)
-        gather_scaled(0, 0, T)
-        gather_scaled(1, 0, T)
-        gather_sum(0, 0, T)
-        gather_sum(1, 0, T)
-        gather_scaled(2, 0, 512)
-        gather_scaled(3, 0, 512)
-        for first in range(0, T, 256):
-            turn(0, first, 256, next_tag())
-        for chunk in (a, b):
-            gather_sum(2, *chunk)
-            gather_sum(3, *chunk)
-        gather_scaled(2, 512, 256)
-        gather_scaled(3, 512, 256)
-        for chunk in (c, last):
-            gather_sum(2, *chunk)
-            gather_sum(3, *chunk)
-        tags = [next_tag() for k in range(5)]
-        turn(2, *a, tags[0])
-        turn(2, *b, tags[1])
-        turn_back(*a, on_scalar, tags[2])
+        for block in range(BLOCKS):
+            turn(0, block, [cols(scaled[0], block), cols(plain0, block)])
+        for block in range(BLOCKS):
+            turn(1, block, [cols(scaled[1], block), cols(plain1, block)])
+        for block in range(4):
+            round_out(low[256 * (block // 2)][:, block % 2, :, :], block, 0, round_on_scalar)
+        for first, n in (a, b, c, last):
+            for block in range(first // P, (first + n) // P):
+                turn(2, block, [cols(scaled[2], block), cols(plain2, block)])
+            for block in range(first // P, (first + n) // P):
+                turn(3, block, [cols(sum3[first], block, first)])
+        for block in range(4):
+            round_out(high[256 * (block // 2)][:, block % 2, :, :], block, 2, round_on_scalar if block < 2 else round_on_vector)
+        turn_back(*a, on_vector, 5)
+        round_out(whole[512][:], 4, 0, round_on_scalar)
+        round_out(whole[640][:], 5, 0, round_on_scalar)
+        turn_back(*b, on_vector, 0)
         quantize(*a)
-        turn_back(*b, on_vector, next_tag())
-        turn(2, *c, tags[1])
-        turn(2, *last, tags[2])
-        turn_back(*c, on_scalar, tags[3])
-        turn_back(*last, on_scalar, tags[4])
+        turn_back(*c, on_scalar, 7)
+        turn_back(*last, on_scalar, 6)
         quantize(*b)
         quantize(*c)
         quantize(*last)
-        project(*a, on_scalar, tags[2])
-        project(*b, on_scalar, tags[3])
-        project(*c, on_vector, tags[4])
-        project(*last, on_vector, tags[0])
+        project(*a, on_scalar, 4)
+        project(*b, on_scalar, 1)
+        project(*c, on_vector, 2)
+        project(*last, on_vector, 3)

@@ -18,6 +18,8 @@ FP4X4 = mybir.dt.float4_e2m1fn_x4
 ALU = mybir.AluOpType
 COPY = mybir.ActivationFunctionType.Copy
 RELU = mybir.ActivationFunctionType.Relu
+SIGN = mybir.ActivationFunctionType.Sign
+IDENTITY = mybir.ActivationFunctionType.Identity
 
 P = 128
 PASSES = K // 512
@@ -25,12 +27,11 @@ PLANES = H // P
 SCALE_WINDOW = 2048
 FIRST_SLOTS = 512
 LATER_GATHERS = [
-    (1, 0, 512), (2, 0, 512), (0, 512, 512), (1, 512, 512), (2, 512, 512),
+    (2, 0, 512), (0, 512, 512), (1, 512, 512), (2, 512, 512),
     (0, 1024, 512), (1, 1024, 512), (2, 1024, 256), (2, 1280, 256),
 ]
 BLOCKS = T // P
 TINY = 2.0**-60
-HUGE = 2.0**127
 
 
 def tile_moe_sdn_lin_relu_kernel(
@@ -121,18 +122,22 @@ def tile_moe_sdn_lin_relu_kernel(
 
         gate_cols = bank(6, [P, P], "gate_cols")
         nc.tensor.transpose(gate_cols[:], gate_rows[:], ident[:])
-        g1, g2 = gate_cols[:, :BLOCKS], gate_cols[:, BLOCKS : 2 * BLOCKS]
-        floor = shared.tile([P, BLOCKS], F32, name="floor", align_bytes=64, offset=19456)
+        gates = keep.tile([P, 2, BLOCKS], F32, name="gates")
+        side = shared.tile([P, BLOCKS], F32, name="side", align_bytes=64, offset=19456)
         pivot = keep.tile([P, BLOCKS], F32, name="pivot")
         inverse = keep.tile([P, BLOCKS], F32, name="inverse")
         ratio_cols = shared.tile([P, BLOCKS], F32, name="ratio_cols", align_bytes=64, offset=6144)
-        nc.vector.tensor_scalar(floor[:], g2, -TINY, -HUGE, ALU.is_le, ALU.mult)
-        nc.vector.scalar_tensor_tensor(pivot[:], floor[:], TINY, g2, ALU.add, ALU.max)
+        nc.scalar.copy(gates[:].rearrange("p r b -> p (r b)"), gate_cols[:, : 2 * BLOCKS])
+        nc.scalar.activation(side[:], gate_cols[:, BLOCKS : 2 * BLOCKS], SIGN, bias=TINY / 2)
+        for b in range(BLOCKS):
+            nc.scalar.activation(pivot[:, b : b + 1], side[:, b : b + 1], IDENTITY, bias=gates[:, 1, b : b + 1], scale=TINY)
+        second_words = shared.tile([P, FIRST_SLOTS], U32, name="second_words", align_bytes=64, offset=15360 + 1024)
+        gather_words(second_words[:], 1, 0, FIRST_SLOTS)
         nc.vector.reciprocal(inverse[:], pivot[:])
         for b in range(BLOCKS):
-            nc.scalar.activation(ratio_cols[:, b : b + 1], g1[:, b : b + 1], COPY, scale=inverse[:, b : b + 1])
+            nc.scalar.activation(ratio_cols[:, b : b + 1], gates[:, 0, b : b + 1], COPY, scale=inverse[:, b : b + 1])
 
-        later_words = shared.tile([P, PASSES * S - FIRST_SLOTS], U32, name="later_words", align_bytes=64, offset=18432)
+        later_words = shared.tile([P, PASSES * S - 2 * FIRST_SLOTS], U32, name="later_words", align_bytes=64, offset=18432)
         col = 0
         for s, first, n in LATER_GATHERS:
             gather_words(later_words[:, col : col + n], s, first, n)
@@ -176,9 +181,9 @@ def tile_moe_sdn_lin_relu_kernel(
                 for e in range(2):
                     mx_pass(first_acc[j][:, e * C : (e + 1) * C], j, e, s, False, s == PASSES - 1 and e == 1)
             relu(j, 0, first_acc[j][:])
-        for j, k in ((0, 7), (1, 6), (2, 4)):
+        for j, k in ((0, 7), (1, 6)):
             pair_plane(j, 1, k)
-        last_acc = {(j, e): bank(k, [P, C], "acc") for j, e, k in ((0, 4, 5), (1, 4, 1), (0, 5, 0), (1, 5, 2))}
+        last_acc = {(j, e): bank(k, [P, C], "acc") for j, e, k in ((0, 4, 4), (1, 4, 5), (0, 5, 0), (1, 5, 1))}
         for s in range(PASSES):
             for j, e in last_acc:
                 mx_pass(last_acc[j, e][:], j, e, s, s == 0, s == PASSES - 1)
@@ -191,9 +196,10 @@ def tile_moe_sdn_lin_relu_kernel(
         scaled = [keep.tile([P, T], F32, name="scaled%d" % j) for j in range(3)]
         scaled3 = {0: keep.tile([P, 512], F32, name="scaled3_early"), 512: keep.tile([P, 256], F32, name="scaled3_late")}
         plain0 = keep.tile([P, T], F32, name="plain0")
-        plain1 = shared.tile([P, T], F32, name="plain1", align_bytes=64, offset=35840 + 4 * T)
-        plain2 = shared.tile([P, T], F32, name="plain2", align_bytes=64, offset=35840)
-        sum3 = {first: keep.tile([P, n], F32, name="sum3_%d" % first) for first, n in (a, b, c, last)}
+        late_plain = shared.tile([P, T + 256], F32, name="late_plain", align_bytes=64, offset=35840 + 4 * T)
+        plain1, plain2 = late_plain[:, :T], late_plain[:, T:]
+        sum2 = shared.tile([P, T], F32, name="sum2", align_bytes=64, offset=35840)
+        sum3 = keep.tile([P, T], F32, name="sum3")
 
         def gather_scaled(dst, j, first):
             n = dst.shape[1]
@@ -204,17 +210,16 @@ def tile_moe_sdn_lin_relu_kernel(
             offsets = pos_sb[1][:, first // 16 : (first + dst.shape[1]) // 16]
             nc.scalar.activation(dst, hidden[j][:].indirect(offsets), COPY)
 
-        def gather_sum(first, n):
-            offsets = pos_sb[1][:, first // 16 : (first + n) // 16]
-            base = 512 * (first // 512)
-            other = scaled3[base][:, first - base : first - base + n]
-            nc.vector.tensor_tensor(sum3[first][:], hidden[3][:].indirect(offsets), other, ALU.add)
+        def gather_sum(dst, j, first, other):
+            offsets = pos_sb[1][:, first // 16 : (first + other.shape[1]) // 16]
+            nc.vector.tensor_tensor(dst[:, first : first + other.shape[1]], hidden[j][:].indirect(offsets), other, ALU.add)
 
         gather_scaled(scaled[0][:], 0, 0)
         gather_plain(plain0[:], 0, 0)
-        pair_plane(2, 2, 3)
-        pair_plane(3, 1, 5)
-        pair_plane(3, 2, 0)
+        pair_plane(2, 1, 4)
+        pair_plane(2, 2, 5)
+        pair_plane(3, 1, 0)
+        pair_plane(3, 2, 1)
         w2_scales_i = w2_scales.bitcast(I32).rearrange("s (q r) n -> r q (s n)", r=4)
         for r in range(4):
             nc.sync.dma_start(w1_scale[4 + r : P : 32, 0, :N].bitcast(I32), w2_scales_i[r])
@@ -223,44 +228,40 @@ def tile_moe_sdn_lin_relu_kernel(
 
         gather_scaled(scaled[1][:], 1, 0)
         gather_scaled(scaled[2][:], 2, 0)
-        gather_plain(plain1[:], 1, 0)
-        for first in range(0, T, 256):
-            gather_plain(plain2[:, first : first + 256], 2, first)
-        for first in scaled3:
-            gather_scaled(scaled3[first][:], 3, first)
-        for chunk in (a, b, c, last):
-            gather_sum(*chunk)
+        gather_plain(plain1, 1, 0)
+        gather_plain(plain2, 2, 0)
+        gather_scaled(scaled3[0][:], 3, 0)
+        gather_sum(sum2, 2, 256, scaled[2][:, 256:512])
+        gather_sum(sum3, 3, 0, scaled3[0][:, :256])
+        gather_sum(sum3, 3, 256, scaled3[0][:, 256:])
+        gather_scaled(scaled3[512][:], 3, 512)
+        gather_sum(sum2, 2, 512, scaled[2][:, 512:])
+        gather_sum(sum3, 3, 512, scaled3[512][:, :P])
+        gather_sum(sum3, 3, 640, scaled3[512][:, P:])
 
         c_tok = [keep.tile([P, 2, P, 2], BF16, name="c_tok%d" % block, align_bytes=64) for block in range(BLOCKS)]
 
-        low = {first: bank(k, [P, 2, 2, P], "low") for first, k in ((0, 7), (256, 6))}
-        high = {first: bank(k, [P, 2, 2, P], "high") for first, k in ((0, 4), (256, 1))}
-        whole = {first: bank(k, [P, PLANES, P], "whole") for first, k in ((512, 2), (640, 3))}
+        low = [bank(k, [P, 2, 2, P], "low") for k in (7, 6, 2)]
+        high = [bank(k, [P, n // P, 2, P], "high") for k, (first, n) in zip((3, 4, 5, 0), (a, b, c, last))]
 
-        def turned(block, j):
-            if block >= 4:
-                return whole[block * P][:, j, :]
-            return (low if j < 2 else high)[256 * (block // 2)][:, block % 2, j % 2, :]
+        def pair_of_planes(block, j):
+            if j < 2:
+                return low[block // 2][:, block % 2, :, :]
+            return high[block // 2][:, block % 2, :, :] if block < 4 else high[block - 2][:, 0, :, :]
 
         def turn(j, block, terms):
             for k, term in enumerate(terms):
-                nc.tensor.matmul(turned(block, j), term, ident[:], start=k == 0, stop=k == len(terms) - 1, is_transpose=True)
+                nc.tensor.matmul(pair_of_planes(block, j)[:, j % 2, :], term, ident[:], start=k == 0, stop=k == len(terms) - 1, is_transpose=True)
 
         def cols(tile, block, base=0):
             return tile[:, block * P - base : (block + 1) * P - base]
 
-        def round_on_scalar(dst, src, block):
-            nc.scalar.activation(dst, src, COPY, scale=pivot[:, block : block + 1])
-
-        def round_on_vector(dst, src, block):
-            nc.vector.tensor_scalar_mul(dst, src, pivot[:, block : block + 1])
-
-        def round_out(src, block, j, engine):
-            planes = src.shape[1]
-            engine(
-                c_tok[block][:, :, 32 * j : 32 * (j + planes), :],
-                src.rearrange("p k (m u v) -> p u (k m) v", u=2, v=2),
-                block,
+        def round_out(block, j):
+            nc.scalar.activation(
+                c_tok[block][:, :, 32 * j : 32 * (j + 2), :],
+                pair_of_planes(block, j).rearrange("p k (m u v) -> p u (k m) v", u=2, v=2),
+                COPY,
+                scale=pivot[:, block : block + 1],
             )
 
         grouped, c_words, c_scale = {}, {}, {}
@@ -302,26 +303,30 @@ def tile_moe_sdn_lin_relu_kernel(
             turn(0, block, [cols(scaled[0], block), cols(plain0, block)])
         for block in range(BLOCKS):
             turn(1, block, [cols(scaled[1], block), cols(plain1, block)])
+        for block in range(BLOCKS):
+            round_out(block, 0)
+        for block in range(2):
+            turn(2, block, [cols(scaled[2], block), cols(plain2, block)])
+        for block in range(2, 4):
+            turn(2, block, [cols(sum2, block)])
         for block in range(4):
-            round_out(low[256 * (block // 2)][:, block % 2, :, :], block, 0, round_on_scalar)
-        for first, n in (a, b, c, last):
-            for block in range(first // P, (first + n) // P):
-                turn(2, block, [cols(scaled[2], block), cols(plain2, block)])
-            for block in range(first // P, (first + n) // P):
-                turn(3, block, [cols(sum3[first], block, first)])
+            turn(3, block, [cols(sum3, block)])
         for block in range(4):
-            round_out(high[256 * (block // 2)][:, block % 2, :, :], block, 2, round_on_scalar if block < 2 else round_on_vector)
-        turn_back(*a, on_vector, 5)
-        round_out(whole[512][:], 4, 0, round_on_scalar)
-        round_out(whole[640][:], 5, 0, round_on_scalar)
-        turn_back(*b, on_vector, 0)
+            round_out(block, 2)
+        turn_back(*a, on_scalar, 1)
+        for j, block in ((2, 4), (2, 5), (3, 4)):
+            turn(j, block, [cols(sum2 if j == 2 else sum3, block)])
+        turn_back(*b, on_vector, 7)
+        turn(3, 5, [cols(sum3, 5)])
+        round_out(4, 2)
+        round_out(5, 2)
         quantize(*a)
-        turn_back(*c, on_scalar, 7)
-        turn_back(*last, on_scalar, 6)
         quantize(*b)
+        turn_back(*c, on_scalar, 6)
+        turn_back(*last, on_scalar, 2)
         quantize(*c)
         quantize(*last)
-        project(*a, on_scalar, 4)
-        project(*b, on_scalar, 1)
-        project(*c, on_vector, 2)
-        project(*last, on_vector, 3)
+        project(*a, on_scalar, 3)
+        project(*b, on_scalar, 4)
+        project(*c, on_vector, 5)
+        project(*last, on_vector, 0)

@@ -68,13 +68,11 @@ def tile_moe_sdn_lin_relu_kernel(
         w1_words_i = w1_words.bitcast(I32).rearrange("e s p n -> p (e s) n")
         x_first = keep.tile([P, T], I32, name="x_first", align_bytes=64)
         x_rest = keep.tile([P, PASSES - 1, T], I32, name="x_rest", align_bytes=64)
-        w1_pair = [shared.tile([P, 2 * PASSES, 2 * H], U8, name="w1_pair0", align_bytes=64, offset=0)] + [
-            keep.tile([P, 2 * PASSES, 2 * H], U8, name="w1_pair%d" % pair, align_bytes=64) for pair in range(1, E // 2)
+        w1_pair = [
+            shared.tile([P, 2 * PASSES, 2 * H], U8, name="w1_pair%d" % pair, align_bytes=64, offset=offset)
+            for pair, offset in enumerate((0, 34816, 40960))
         ]
-        zero_bias = [
-            shared.tile([P, 32], F32, name="zero_bias%d" % k, align_bytes=64, offset=offset)
-            for k, offset in enumerate((34816, 35840 + 4 * T - 64))
-        ]
+        zero_bias = keep.tile([P, 1], F32, name="zero_bias")
         x_win = [x_first[:]] + [x_rest[:, s, :] for s in range(PASSES - 1)]
 
         nc.sync.dma_start(offs_sb[:], offs)
@@ -85,8 +83,7 @@ def tile_moe_sdn_lin_relu_kernel(
         for q in range(2, 4):
             nc.scalar.dma_start(win_i[32 * q : 32 * q + 4, : T // 4], x_scales_i[0, 4 * q : 4 * q + 4, :])
             nc.scalar.dma_start(win_i[32 * q - 8 : 32 * q, : T // 4], x_scales_i[1:, 4 * q : 4 * q + 4, :])
-        for k in range(2):
-            nc.scalar.activation(zero_bias[k][:, :1], zero_in[:], RELU)
+        nc.scalar.activation(zero_bias[:], zero_in[:], RELU)
         w1_scales_i = w1_scales.bitcast(I32).rearrange("e s (q r) n -> r q (e s) n", r=4)
         nc.sync.dma_start(x_rest[:], x_words_i[:, 1:, :])
         nc.sync.dma_start(gate_rows[: 2 * BLOCKS, :], gate[:, 0, :].rearrange("r (b m) -> r b m", m=P))
@@ -131,7 +128,7 @@ def tile_moe_sdn_lin_relu_kernel(
         nc.scalar.activation(side[:], gate_cols[:, BLOCKS : 2 * BLOCKS], SIGN, bias=TINY / 2)
         for b in range(BLOCKS):
             nc.scalar.activation(pivot[:, b : b + 1], side[:, b : b + 1], IDENTITY, bias=gates[:, 1, b : b + 1], scale=TINY)
-        second_words = shared.tile([P, FIRST_SLOTS], U32, name="second_words", align_bytes=64, offset=15360 + 1024)
+        second_words = keep.tile([P, FIRST_SLOTS], U32, name="second_words", align_bytes=64)
         gather_words(second_words[:], 1, 0, FIRST_SLOTS)
         nc.vector.reciprocal(inverse[:], pivot[:])
         for b in range(BLOCKS):
@@ -157,13 +154,14 @@ def tile_moe_sdn_lin_relu_kernel(
             )
 
         def relu(j, e, acc):
-            nc.scalar.activation(hidden[j][:, e * C : e * C + acc.shape[1]], acc, RELU, bias=zero_bias[j // 3][:, :1])
+            nc.scalar.activation(hidden[j][:, e * C : e * C + acc.shape[1]], acc, RELU, bias=zero_bias[:])
 
-        def pair_plane(j, pair, k):
+        def pair_plane(j, pair, k, between=lambda: None):
             acc = bank(k, [P, 2 * C], "acc")
             for h in range(2):
                 for s in range(PASSES):
                     mx_pass(acc[:, h * C : (h + 1) * C], j, 2 * pair + h, s, s == 0, s == PASSES - 1)
+            between()
             relu(j, 2 * pair, acc[:])
 
         first_acc = [bank(j, [P, 2 * C], "acc") for j in range(PLANES)]
@@ -187,18 +185,21 @@ def tile_moe_sdn_lin_relu_kernel(
         for s in range(PASSES):
             for j, e in last_acc:
                 mx_pass(last_acc[j, e][:], j, e, s, s == 0, s == PASSES - 1)
-        relu(0, 4, last_acc[0, 4][:])
-        nc.vector.tensor_scalar_max(hidden[1][:, 4 * C : 5 * C], last_acc[1, 4][:], 0.0)
-        relu(0, 5, last_acc[0, 5][:])
-        relu(1, 5, last_acc[1, 5][:])
+        for e in (4, 5):
+            relu(0, e, last_acc[0, e][:])
+            nc.vector.tensor_scalar_max(hidden[1][:, e * C : (e + 1) * C], last_acc[1, e][:], 0.0)
 
         a, b, c, last = (0, 256), (256, 256), (512, 128), (640, 128)
-        scaled = [keep.tile([P, T], F32, name="scaled%d" % j) for j in range(3)]
-        scaled3 = {0: keep.tile([P, 512], F32, name="scaled3_early"), 512: keep.tile([P, 256], F32, name="scaled3_late")}
-        plain0 = keep.tile([P, T], F32, name="plain0")
-        late_plain = shared.tile([P, T + 256], F32, name="late_plain", align_bytes=64, offset=35840 + 4 * T)
-        plain1, plain2 = late_plain[:, :T], late_plain[:, T:]
-        sum2 = shared.tile([P, T], F32, name="sum2", align_bytes=64, offset=35840)
+        scaled = {(j, 0): keep.tile([P, T], F32, name="scaled%d" % j) for j in range(2)}
+        for j in (2, 3):
+            for first, n in ((0, 512), (512, 256)):
+                scaled[j, first] = keep.tile([P, n], F32, name="scaled%d_%d" % (j, first))
+        plain = [
+            keep.tile([P, T], F32, name="plain0"),
+            shared.tile([P, T], F32, name="plain1", align_bytes=64, offset=34816),
+            shared.tile([P, 512], F32, name="plain2", align_bytes=64, offset=40960),
+        ]
+        sum2 = keep.tile([P, T], F32, name="sum2")
         sum3 = keep.tile([P, T], F32, name="sum3")
 
         def gather_scaled(dst, j, first):
@@ -214,35 +215,22 @@ def tile_moe_sdn_lin_relu_kernel(
             offsets = pos_sb[1][:, first // 16 : (first + other.shape[1]) // 16]
             nc.vector.tensor_tensor(dst[:, first : first + other.shape[1]], hidden[j][:].indirect(offsets), other, ALU.add)
 
-        gather_scaled(scaled[0][:], 0, 0)
-        gather_plain(plain0[:], 0, 0)
+        gather_scaled(scaled[0, 0][:], 0, 0)
+        gather_plain(plain[0][:], 0, 0)
         pair_plane(2, 1, 4)
         pair_plane(2, 2, 5)
-        pair_plane(3, 1, 0)
-        pair_plane(3, 2, 1)
+        gather_scaled(scaled[1, 0][:], 1, 0)
+        pair_plane(3, 1, 0, between=lambda: gather_plain(plain[1][:], 1, 0))
         w2_scales_i = w2_scales.bitcast(I32).rearrange("s (q r) n -> r q (s n)", r=4)
         for r in range(4):
             nc.sync.dma_start(w1_scale[4 + r : P : 32, 0, :N].bitcast(I32), w2_scales_i[r])
         w2_sb = shared.tile([P, N], I32, name="w2_sb", align_bytes=64, offset=0)
         nc.sync.dma_start(w2_sb[:], w2_words[0].rearrange("p n d -> p (n d)").bitcast(I32))
 
-        gather_scaled(scaled[1][:], 1, 0)
-        gather_scaled(scaled[2][:], 2, 0)
-        gather_plain(plain1, 1, 0)
-        gather_plain(plain2, 2, 0)
-        gather_scaled(scaled3[0][:], 3, 0)
-        gather_sum(sum2, 2, 256, scaled[2][:, 256:512])
-        gather_sum(sum3, 3, 0, scaled3[0][:, :256])
-        gather_sum(sum3, 3, 256, scaled3[0][:, 256:])
-        gather_scaled(scaled3[512][:], 3, 512)
-        gather_sum(sum2, 2, 512, scaled[2][:, 512:])
-        gather_sum(sum3, 3, 512, scaled3[512][:, :P])
-        gather_sum(sum3, 3, 640, scaled3[512][:, P:])
-
         c_tok = [keep.tile([P, 2, P, 2], BF16, name="c_tok%d" % block, align_bytes=64) for block in range(BLOCKS)]
 
         low = [bank(k, [P, 2, 2, P], "low") for k in (7, 6, 2)]
-        high = [bank(k, [P, n // P, 2, P], "high") for k, (first, n) in zip((3, 4, 5, 0), (a, b, c, last))]
+        high = []
 
         def pair_of_planes(block, j):
             if j < 2:
@@ -256,13 +244,13 @@ def tile_moe_sdn_lin_relu_kernel(
         def cols(tile, block, base=0):
             return tile[:, block * P - base : (block + 1) * P - base]
 
-        def round_out(block, j):
-            nc.scalar.activation(
-                c_tok[block][:, :, 32 * j : 32 * (j + 2), :],
-                pair_of_planes(block, j).rearrange("p k (m u v) -> p u (k m) v", u=2, v=2),
-                COPY,
-                scale=pivot[:, block : block + 1],
-            )
+        def round_out(block, j, on_vector=False):
+            dst = c_tok[block][:, :, 32 * j : 32 * (j + 2), :]
+            src = pair_of_planes(block, j).rearrange("p k (m u v) -> p u (k m) v", u=2, v=2)
+            if on_vector:
+                nc.vector.tensor_scalar_mul(dst, src, pivot[:, block : block + 1])
+            else:
+                nc.scalar.activation(dst, src, COPY, scale=pivot[:, block : block + 1])
 
         grouped, c_words, c_scale = {}, {}, {}
 
@@ -300,30 +288,37 @@ def tile_moe_sdn_lin_relu_kernel(
 
         on_scalar, on_vector = nc.scalar.copy, nc.vector.tensor_copy
         for block in range(BLOCKS):
-            turn(0, block, [cols(scaled[0], block), cols(plain0, block)])
+            turn(0, block, [cols(scaled[0, 0], block), cols(plain[0], block)])
+        pair_plane(3, 2, 1)
+        high.extend(bank(k, [P, n // P, 2, P], "high") for k, (first, n) in zip((3, 4, 5, 0), (a, b, c, last)))
+        gather_scaled(scaled[2, 512][:], 2, 512)
+        gather_scaled(scaled[2, 0][:], 2, 0)
+        gather_sum(sum2, 2, 512, scaled[2, 512][:])
+        for first in (0, 256):
+            gather_plain(plain[2][:, first : first + 256], 2, first)
+        gather_scaled(scaled[3, 0][:], 3, 0)
+        gather_scaled(scaled[3, 512][:], 3, 512)
+        for first, n in (a, b, c, last):
+            base = 512 * (first // 512)
+            gather_sum(sum3, 3, first, scaled[3, base][:, first - base : first - base + n])
         for block in range(BLOCKS):
-            turn(1, block, [cols(scaled[1], block), cols(plain1, block)])
-        for block in range(BLOCKS):
-            round_out(block, 0)
-        for block in range(2):
-            turn(2, block, [cols(scaled[2], block), cols(plain2, block)])
-        for block in range(2, 4):
+            turn(1, block, [cols(scaled[1, 0], block), cols(plain[1], block)])
+        for block in (4, 5):
             turn(2, block, [cols(sum2, block)])
         for block in range(4):
+            turn(2, block, [cols(scaled[2, 0], block), cols(plain[2], block)])
+        for block in range(BLOCKS):
+            round_out(block, 0)
+        for block in range(BLOCKS):
             turn(3, block, [cols(sum3, block)])
-        for block in range(4):
-            round_out(block, 2)
-        turn_back(*a, on_scalar, 1)
-        for j, block in ((2, 4), (2, 5), (3, 4)):
-            turn(j, block, [cols(sum2 if j == 2 else sum3, block)])
-        turn_back(*b, on_vector, 7)
-        turn(3, 5, [cols(sum3, 5)])
-        round_out(4, 2)
-        round_out(5, 2)
+        for block in range(BLOCKS):
+            round_out(block, 2, on_vector=block in (2, 3))
+        turn_back(*a, on_vector, 1)
+        turn_back(*b, on_scalar, 7)
         quantize(*a)
-        quantize(*b)
-        turn_back(*c, on_scalar, 6)
+        turn_back(*c, on_vector, 6)
         turn_back(*last, on_scalar, 2)
+        quantize(*b)
         quantize(*c)
         quantize(*last)
         project(*a, on_scalar, 3)

@@ -68,10 +68,21 @@ def tile_moe_sdn_lin_relu_kernel(
         w1_words_i = w1_words.bitcast(I32).rearrange("e s p n -> p (e s) n")
         x_first = keep.tile([P, T], I32, name="x_first", align_bytes=64)
         x_rest = keep.tile([P, PASSES - 1, T], I32, name="x_rest", align_bytes=64)
-        w1_pair = [
-            shared.tile([P, 2 * PASSES, 2 * H], U8, name="w1_pair%d" % pair, align_bytes=64, offset=offset)
-            for pair, offset in enumerate((0, 34816, 40960))
-        ]
+        parts = ((0, 0, 3), (1, 0, 2), (2, 0, 2), (1, 2, 2), (2, 2, 2))
+        w1_part = {}
+        for k, (pair, plane, planes) in enumerate(parts):
+            w1_part[pair, plane] = shared.tile(
+                [P, 2 * PASSES, 2 * P * planes], U8, name="w1_part%d%d" % (pair, plane), align_bytes=64,
+                offset=34816 + 3072 * k if k else 0,
+            )
+
+        w1_last_early = keep.tile([P, 2, 2 * P], U8, name="w1_last_early", align_bytes=64)
+        w1_last_late = [keep.tile([P, PASSES - 1, 2 * P], U8, name="w1_last_late%d" % e, align_bytes=64) for e in range(2)]
+
+        def load_part(pair, plane, planes):
+            src = w1_words_i[:, 2 * PASSES * pair : 2 * PASSES * (pair + 1), 64 * plane : 64 * (plane + planes)]
+            nc.sync.dma_start(w1_part[pair, plane][:].bitcast(I32), src)
+
         zero_bias = keep.tile([P, 1], F32, name="zero_bias")
         x_win = [x_first[:]] + [x_rest[:, s, :] for s in range(PASSES - 1)]
 
@@ -87,7 +98,8 @@ def tile_moe_sdn_lin_relu_kernel(
         w1_scales_i = w1_scales.bitcast(I32).rearrange("e s (q r) n -> r q (e s) n", r=4)
         nc.sync.dma_start(x_rest[:], x_words_i[:, 1:, :])
         nc.sync.dma_start(gate_rows[: 2 * BLOCKS, :], gate[:, 0, :].rearrange("r (b m) -> r b m", m=P))
-        nc.sync.dma_start(w1_pair[0][:].bitcast(I32), w1_words_i[:, : 2 * PASSES, :])
+        load_part(*parts[0])
+        nc.sync.dma_start(w1_last_early[:].bitcast(I32), w1_words_i[:, 0 : 2 * PASSES : PASSES, 192:])
         for r in range(4):
             nc.sync.dma_start(w1_scale[r:P:32, : 2 * PASSES, :].bitcast(I32), w1_scales_i[r][:, : 2 * PASSES])
         for r, pos in enumerate((pos1, pos2)):
@@ -114,8 +126,10 @@ def tile_moe_sdn_lin_relu_kernel(
                 )
         for r in range(4):
             nc.sync.dma_start(w1_scale[r:P:32, 2 * PASSES :, :].bitcast(I32), w1_scales_i[r][:, 2 * PASSES :])
-        for pair in (1, 2):
-            nc.sync.dma_start(w1_pair[pair][:].bitcast(I32), w1_words_i[:, 2 * PASSES * pair : 2 * PASSES * (pair + 1), :])
+        for part in parts[1:]:
+            load_part(*part)
+        for e in range(2):
+            nc.sync.dma_start(w1_last_late[e][:].bitcast(I32), w1_words_i[:, PASSES * e + 1 : PASSES * (e + 1), 192:])
 
         gate_cols = bank(6, [P, P], "gate_cols")
         nc.tensor.transpose(gate_cols[:], gate_rows[:], ident[:])
@@ -143,9 +157,14 @@ def tile_moe_sdn_lin_relu_kernel(
         hidden = [keep.tile([P, S], F32, name="hidden%d" % j) for j in range(PLANES)]
 
         def mx_pass(acc, j, e, s, start, stop):
+            plane = max(first for pair, first in w1_part if pair == e // 2 and first <= j)
+            if e < 2 and j == 3:
+                words = w1_last_late[e][:, s - 1, :] if s else w1_last_early[:, e, :]
+            else:
+                words = w1_part[e // 2, plane][:, (e % 2) * PASSES + s, 2 * P * (j - plane) : 2 * P * (j - plane + 1)]
             nc.tensor.matmul_mx(
                 out=acc,
-                lhsT=w1_pair[e // 2][:, (e % 2) * PASSES + s, 2 * P * j : 2 * P * (j + 1)].bitcast(FP4X4),
+                lhsT=words.bitcast(FP4X4),
                 lhsT_scale=w1_scale[:, e * PASSES + s, P * j : P * (j + 1)],
                 rhs=slot_words[s, e].bitcast(FP8X4),
                 rhs_scale=slot_scale[s][:, e * C : (e + 1) * C],
@@ -155,6 +174,9 @@ def tile_moe_sdn_lin_relu_kernel(
 
         def relu(j, e, acc):
             nc.scalar.activation(hidden[j][:, e * C : e * C + acc.shape[1]], acc, RELU, bias=zero_bias[:])
+
+        def relu_on_vector(j, e, acc):
+            nc.vector.tensor_scalar_max(hidden[j][:, e * C : e * C + acc.shape[1]], acc, 0.0)
 
         def pair_plane(j, pair, k, between=lambda: None):
             acc = bank(k, [P, 2 * C], "acc")
@@ -174,20 +196,25 @@ def tile_moe_sdn_lin_relu_kernel(
             for b in range(3):
                 nc.tensor.transpose(spread[:, b, :], ratio_cols[:, first + b : first + b + 1].to_broadcast([P, P]), ident[:])
             nc.scalar.copy(ratio[:, first * P : (first + 3) * P], spread[:].rearrange("p b t -> p (b t)"))
-        for j in range(PLANES):
+
+        def finish_first(j, empty):
             for s in range(1, PASSES):
                 for e in range(2):
                     mx_pass(first_acc[j][:, e * C : (e + 1) * C], j, e, s, False, s == PASSES - 1 and e == 1)
-            relu(j, 0, first_acc[j][:])
+            empty(j, 0, first_acc[j][:])
+
+        for j in range(3):
+            finish_first(j, relu)
         for j, k in ((0, 7), (1, 6)):
             pair_plane(j, 1, k)
-        last_acc = {(j, e): bank(k, [P, C], "acc") for j, e, k in ((0, 4, 4), (1, 4, 5), (0, 5, 0), (1, 5, 1))}
-        for s in range(PASSES):
-            for j, e in last_acc:
-                mx_pass(last_acc[j, e][:], j, e, s, s == 0, s == PASSES - 1)
+        last_acc = {(j, e): bank(k, [P, C], "acc") for j, e, k in ((0, 4, 4), (1, 4, 0), (0, 5, 5), (1, 5, 1))}
+        for units in (((0, 4), (1, 4), (0, 5)), ((1, 5),)):
+            for s in range(PASSES):
+                for j, e in units:
+                    mx_pass(last_acc[j, e][:], j, e, s, s == 0, s == PASSES - 1)
         for e in (4, 5):
             relu(0, e, last_acc[0, e][:])
-            nc.vector.tensor_scalar_max(hidden[1][:, e * C : (e + 1) * C], last_acc[1, e][:], 0.0)
+            relu_on_vector(1, e, last_acc[1, e][:])
 
         a, b, c, last = (0, 256), (256, 256), (512, 128), (640, 128)
         scaled = {(j, 0): keep.tile([P, T], F32, name="scaled%d" % j) for j in range(2)}
@@ -196,8 +223,8 @@ def tile_moe_sdn_lin_relu_kernel(
                 scaled[j, first] = keep.tile([P, n], F32, name="scaled%d_%d" % (j, first))
         plain = [
             keep.tile([P, T], F32, name="plain0"),
-            shared.tile([P, T], F32, name="plain1", align_bytes=64, offset=34816),
-            shared.tile([P, 512], F32, name="plain2", align_bytes=64, offset=40960),
+            shared.tile([P, T], F32, name="plain1", align_bytes=64, offset=34816 + 3072 * 3),
+            shared.tile([P, 512], F32, name="plain2", align_bytes=64, offset=34816 + 3072 * 4),
         ]
         sum2 = keep.tile([P, T], F32, name="sum2")
         sum3 = keep.tile([P, T], F32, name="sum3")
@@ -217,10 +244,11 @@ def tile_moe_sdn_lin_relu_kernel(
 
         gather_scaled(scaled[0, 0][:], 0, 0)
         gather_plain(plain[0][:], 0, 0)
-        pair_plane(2, 1, 4)
-        pair_plane(2, 2, 5)
+        pair_plane(2, 1, 2)
+        pair_plane(2, 2, 7)
         gather_scaled(scaled[1, 0][:], 1, 0)
-        pair_plane(3, 1, 0, between=lambda: gather_plain(plain[1][:], 1, 0))
+        finish_first(3, relu_on_vector)
+        pair_plane(3, 1, 6, between=lambda: gather_plain(plain[1][:], 1, 0))
         w2_scales_i = w2_scales.bitcast(I32).rearrange("s (q r) n -> r q (s n)", r=4)
         for r in range(4):
             nc.sync.dma_start(w1_scale[4 + r : P : 32, 0, :N].bitcast(I32), w2_scales_i[r])
@@ -229,7 +257,7 @@ def tile_moe_sdn_lin_relu_kernel(
 
         c_tok = [keep.tile([P, 2, P, 2], BF16, name="c_tok%d" % block, align_bytes=64) for block in range(BLOCKS)]
 
-        low = [bank(k, [P, 2, 2, P], "low") for k in (7, 6, 2)]
+        low = [bank(k, [P, 2, 2, P], "low") for k in (5, 0, 1)]
         high = []
 
         def pair_of_planes(block, j):
@@ -289,8 +317,8 @@ def tile_moe_sdn_lin_relu_kernel(
         on_scalar, on_vector = nc.scalar.copy, nc.vector.tensor_copy
         for block in range(BLOCKS):
             turn(0, block, [cols(scaled[0, 0], block), cols(plain[0], block)])
-        pair_plane(3, 2, 1)
-        high.extend(bank(k, [P, n // P, 2, P], "high") for k, (first, n) in zip((3, 4, 5, 0), (a, b, c, last)))
+        pair_plane(3, 2, 4)
+        high.extend(bank(k, [P, n // P, 2, P], "high") for k, (first, n) in zip((2, 7, 3, 6), (a, b, c, last)))
         gather_scaled(scaled[2, 512][:], 2, 512)
         gather_scaled(scaled[2, 0][:], 2, 0)
         gather_sum(sum2, 2, 512, scaled[2, 512][:])
@@ -313,15 +341,15 @@ def tile_moe_sdn_lin_relu_kernel(
             turn(3, block, [cols(sum3, block)])
         for block in range(BLOCKS):
             round_out(block, 2, on_vector=block in (2, 3))
-        turn_back(*a, on_vector, 1)
-        turn_back(*b, on_scalar, 7)
+        turn_back(*a, on_vector, 4)
+        turn_back(*b, on_scalar, 5)
         quantize(*a)
-        turn_back(*c, on_vector, 6)
-        turn_back(*last, on_scalar, 2)
+        turn_back(*c, on_vector, 0)
+        turn_back(*last, on_scalar, 1)
         quantize(*b)
         quantize(*c)
         quantize(*last)
-        project(*a, on_scalar, 3)
-        project(*b, on_scalar, 4)
-        project(*c, on_vector, 5)
-        project(*last, on_vector, 0)
+        project(*a, on_scalar, 2)
+        project(*b, on_scalar, 7)
+        project(*c, on_vector, 3)
+        project(*last, on_vector, 6)

@@ -24,14 +24,31 @@ IDENTITY = mybir.ActivationFunctionType.Identity
 P = 128
 PASSES = K // 512
 PLANES = H // P
-SCALE_WINDOW = 2048
-FIRST_SLOTS = 512
-LATER_GATHERS = [
-    (2, 0, 512), (0, 512, 512), (1, 512, 512), (2, 512, 512),
-    (0, 1024, 512), (1, 1024, 512), (2, 1024, 256), (2, 1280, 256),
-]
 BLOCKS = T // P
+PAIR = 2 * C
+PLANE_BYTES = 2 * P
 TINY = 2.0**-60
+
+SCALE_WINDOW = 2048
+
+LATER_GATHERS = (
+    [(PASSES - 1, 0, PAIR)]
+    + [(s, PAIR, PAIR) for s in range(PASSES)]
+    + [(s, 2 * PAIR, PAIR) for s in range(PASSES - 1)]
+    + [(PASSES - 1, e * C, C) for e in (E - 2, E - 1)]
+)
+
+W1_PARTS = ((0, 0, 4), (1, 0, 2), (2, 0, 2), (1, 2, 2), (2, 2, 2))
+
+CHUNKS = ((0, 256), (256, 256), (512, P), (640, P))
+SPLIT = 512
+
+W1_FIRST_AT = 0
+SCALE_WINDOW_AT = 17408
+LATER_WORDS_AT = SCALE_WINDOW_AT + SCALE_WINDOW // 2
+SIDE_AT = SCALE_WINDOW_AT + SCALE_WINDOW
+W1_HALF_BYTES = 2 * PASSES * 2 * PLANE_BYTES
+W1_HALVES_AT = 37888
 
 
 def tile_moe_sdn_lin_relu_kernel(
@@ -50,8 +67,8 @@ def tile_moe_sdn_lin_relu_kernel(
         offs_sb = lists.tile([P, S // 16], U16, name="offs_sb")
         pos_sb = [lists.tile([P, T // 16], U16, name="pos%d_sb" % r) for r in range(2)]
 
-        x_scale_win = shared.tile([P, SCALE_WINDOW], U8, name="x_scale_win", align_bytes=64, offset=17408)
-        w1_scale = keep.tile([P, E * PASSES, H], U8, name="w1_scale", align_bytes=64)
+        x_scale_win = shared.tile([P, SCALE_WINDOW], U8, name="x_scale_win", align_bytes=64, offset=SCALE_WINDOW_AT)
+        w_scale = keep.tile([P, E * PASSES, H], U8, name="w_scale", align_bytes=64)
         slot_scale = [keep.tile([P, S], U8, name="slot_scale%d" % s, align_bytes=64) for s in range(PASSES)]
         zero_in = keep.tile([P, 1], F32, name="zero_in")
         gate_rows = keep.tile([P, P], F32, name="gate_rows")
@@ -59,7 +76,7 @@ def tile_moe_sdn_lin_relu_kernel(
         win_i = x_scale_win[:].bitcast(I32)
         nc.gpsimd.memset(win_i[:, : T // 4], 0)
         nc.gpsimd.memset(zero_in[:], 0.0)
-        nc.vector.memset(w1_scale[:].rearrange("p g n -> p (g n)").bitcast(I32), 0)
+        nc.vector.memset(w_scale[:].rearrange("p g n -> p (g n)").bitcast(I32), 0)
         nc.vector.memset(win_i[:, T // 4 :], 0)
         nc.gpsimd.memset(gate_rows[:], 0.0)
         make_identity(nc, ident[:])
@@ -68,23 +85,25 @@ def tile_moe_sdn_lin_relu_kernel(
         w1_words_i = w1_words.bitcast(I32).rearrange("e s p n -> p (e s) n")
         x_first = keep.tile([P, T], I32, name="x_first", align_bytes=64)
         x_rest = keep.tile([P, PASSES - 1, T], I32, name="x_rest", align_bytes=64)
-        parts = ((0, 0, 3), (1, 0, 2), (2, 0, 2), (1, 2, 2), (2, 2, 2))
-        w1_part = {}
-        for k, (pair, plane, planes) in enumerate(parts):
-            w1_part[pair, plane] = shared.tile(
-                [P, 2 * PASSES, 2 * P * planes], U8, name="w1_part%d%d" % (pair, plane), align_bytes=64,
-                offset=34816 + 3072 * k if k else 0,
-            )
+        x_win = [x_first[:]] + [x_rest[:, s, :] for s in range(PASSES - 1)]
 
-        w1_last_early = keep.tile([P, 2, 2 * P], U8, name="w1_last_early", align_bytes=64)
-        w1_last_late = [keep.tile([P, PASSES - 1, 2 * P], U8, name="w1_last_late%d" % e, align_bytes=64) for e in range(2)]
+        w1_at = {part[:2]: W1_HALVES_AT + W1_HALF_BYTES * k for k, part in enumerate(W1_PARTS[1:])}
+        w1_at[0, 0] = W1_FIRST_AT
+        w1_part = {
+            (pair, plane): shared.tile(
+                [P, 2 * PASSES, PLANE_BYTES * planes],
+                U8,
+                name="w1_part%d%d" % (pair, plane),
+                align_bytes=64,
+                offset=w1_at[pair, plane],
+            )
+            for pair, plane, planes in W1_PARTS
+        }
 
         def load_part(pair, plane, planes):
-            src = w1_words_i[:, 2 * PASSES * pair : 2 * PASSES * (pair + 1), 64 * plane : 64 * (plane + planes)]
-            nc.sync.dma_start(w1_part[pair, plane][:].bitcast(I32), src)
-
-        zero_bias = keep.tile([P, 1], F32, name="zero_bias")
-        x_win = [x_first[:]] + [x_rest[:, s, :] for s in range(PASSES - 1)]
+            rows = slice(2 * PASSES * pair, 2 * PASSES * (pair + 1))
+            words = slice(PLANE_BYTES // 4 * plane, PLANE_BYTES // 4 * (plane + planes))
+            nc.sync.dma_start(w1_part[pair, plane][:].bitcast(I32), w1_words_i[:, rows, words])
 
         nc.sync.dma_start(offs_sb[:], offs)
         nc.sync.dma_start(x_first[:], x_words_i[:, 0, :])
@@ -94,61 +113,56 @@ def tile_moe_sdn_lin_relu_kernel(
         for q in range(2, 4):
             nc.scalar.dma_start(win_i[32 * q : 32 * q + 4, : T // 4], x_scales_i[0, 4 * q : 4 * q + 4, :])
             nc.scalar.dma_start(win_i[32 * q - 8 : 32 * q, : T // 4], x_scales_i[1:, 4 * q : 4 * q + 4, :])
+        zero_bias = keep.tile([P, 1], F32, name="zero_bias")
         nc.scalar.activation(zero_bias[:], zero_in[:], RELU)
         w1_scales_i = w1_scales.bitcast(I32).rearrange("e s (q r) n -> r q (e s) n", r=4)
         nc.sync.dma_start(x_rest[:], x_words_i[:, 1:, :])
         nc.sync.dma_start(gate_rows[: 2 * BLOCKS, :], gate[:, 0, :].rearrange("r (b m) -> r b m", m=P))
-        load_part(*parts[0])
-        nc.sync.dma_start(w1_last_early[:].bitcast(I32), w1_words_i[:, 0 : 2 * PASSES : PASSES, 192:])
+        load_part(*W1_PARTS[0])
         for r in range(4):
-            nc.sync.dma_start(w1_scale[r:P:32, : 2 * PASSES, :].bitcast(I32), w1_scales_i[r][:, : 2 * PASSES])
+            nc.sync.dma_start(w_scale[r:P:32, : 2 * PASSES, :].bitcast(I32), w1_scales_i[r][:, : 2 * PASSES])
         for r, pos in enumerate((pos1, pos2)):
             nc.sync.dma_start(pos_sb[r][:], pos)
 
         slot_words = {}
 
-        def gather_words(g, s, first, n):
+        def gather_words(dst, s, first, n):
             offsets = offs_sb[:, first // 16 : (first + n) // 16]
-            nc.vector.tensor_copy(g, x_win[s].bitcast(U32).indirect(offsets))
+            nc.vector.tensor_copy(dst, x_win[s].bitcast(U32).indirect(offsets))
             for col in range(0, n, C):
-                slot_words[s, (first + col) // C] = g[:, col : col + C]
+                slot_words[s, (first + col) // C] = dst[:, col : col + C]
 
-        first_words = [
-            shared.tile([P, C], U32, name="first_words%d" % e, align_bytes=64, offset=6144 + 4 * C * e) for e in range(2)
-        ]
-        for e in range(2):
-            gather_words(first_words[e][:], 0, e * C, C)
+        first_words = keep.tile([P, PAIR], U32, name="first_words", align_bytes=64)
+        gather_words(first_words[:], 0, 0, PAIR)
         nc.vector.tensor_copy(slot_scale[0][:], x_scale_win[:].indirect(offs_sb[:]))
         for s in range(1, PASSES):
-            for row, first in ((0, 4 * s), (64, 52 + 4 * s)):
+            for row, source in ((0, 4 * s), (64, 64 - 12 + 4 * s)):
                 nc.sync.dma_start(
-                    slot_scale[s][row : row + 64, :].bitcast(I32), slot_scale[0][first : first + 64, :].bitcast(I32)
+                    slot_scale[s][row : row + 64, :].bitcast(I32), slot_scale[0][source : source + 64, :].bitcast(I32)
                 )
         for r in range(4):
-            nc.sync.dma_start(w1_scale[r:P:32, 2 * PASSES :, :].bitcast(I32), w1_scales_i[r][:, 2 * PASSES :])
-        for part in parts[1:]:
+            nc.sync.dma_start(w_scale[r:P:32, 2 * PASSES :, :].bitcast(I32), w1_scales_i[r][:, 2 * PASSES :])
+        for part in W1_PARTS[1:]:
             load_part(*part)
-        for e in range(2):
-            nc.sync.dma_start(w1_last_late[e][:].bitcast(I32), w1_words_i[:, PASSES * e + 1 : PASSES * (e + 1), 192:])
 
         gate_cols = bank(6, [P, P], "gate_cols")
         nc.tensor.transpose(gate_cols[:], gate_rows[:], ident[:])
         gates = keep.tile([P, 2, BLOCKS], F32, name="gates")
-        side = shared.tile([P, BLOCKS], F32, name="side", align_bytes=64, offset=19456)
+        side = shared.tile([P, BLOCKS], F32, name="side", align_bytes=64, offset=SIDE_AT)
         pivot = keep.tile([P, BLOCKS], F32, name="pivot")
         inverse = keep.tile([P, BLOCKS], F32, name="inverse")
-        ratio_cols = shared.tile([P, BLOCKS], F32, name="ratio_cols", align_bytes=64, offset=6144)
+        ratio_cols = keep.tile([P, BLOCKS], F32, name="ratio_cols")
         nc.scalar.copy(gates[:].rearrange("p r b -> p (r b)"), gate_cols[:, : 2 * BLOCKS])
         nc.scalar.activation(side[:], gate_cols[:, BLOCKS : 2 * BLOCKS], SIGN, bias=TINY / 2)
         for b in range(BLOCKS):
             nc.scalar.activation(pivot[:, b : b + 1], side[:, b : b + 1], IDENTITY, bias=gates[:, 1, b : b + 1], scale=TINY)
-        second_words = keep.tile([P, FIRST_SLOTS], U32, name="second_words", align_bytes=64)
-        gather_words(second_words[:], 1, 0, FIRST_SLOTS)
+        second_words = keep.tile([P, PAIR], U32, name="second_words", align_bytes=64)
+        gather_words(second_words[:], 1, 0, PAIR)
         nc.vector.reciprocal(inverse[:], pivot[:])
         for b in range(BLOCKS):
             nc.scalar.activation(ratio_cols[:, b : b + 1], gates[:, 0, b : b + 1], COPY, scale=inverse[:, b : b + 1])
 
-        later_words = shared.tile([P, PASSES * S - 2 * FIRST_SLOTS], U32, name="later_words", align_bytes=64, offset=18432)
+        later_words = shared.tile([P, PASSES * S - 2 * PAIR], U32, name="later_words", align_bytes=64, offset=LATER_WORDS_AT)
         col = 0
         for s, first, n in LATER_GATHERS:
             gather_words(later_words[:, col : col + n], s, first, n)
@@ -158,14 +172,11 @@ def tile_moe_sdn_lin_relu_kernel(
 
         def mx_pass(acc, j, e, s, start, stop):
             plane = max(first for pair, first in w1_part if pair == e // 2 and first <= j)
-            if e < 2 and j == 3:
-                words = w1_last_late[e][:, s - 1, :] if s else w1_last_early[:, e, :]
-            else:
-                words = w1_part[e // 2, plane][:, (e % 2) * PASSES + s, 2 * P * (j - plane) : 2 * P * (j - plane + 1)]
+            at = PLANE_BYTES * (j - plane)
             nc.tensor.matmul_mx(
                 out=acc,
-                lhsT=words.bitcast(FP4X4),
-                lhsT_scale=w1_scale[:, e * PASSES + s, P * j : P * (j + 1)],
+                lhsT=w1_part[e // 2, plane][:, (e % 2) * PASSES + s, at : at + PLANE_BYTES].bitcast(FP4X4),
+                lhsT_scale=w_scale[:, e * PASSES + s, P * j : P * (j + 1)],
                 rhs=slot_words[s, e].bitcast(FP8X4),
                 rhs_scale=slot_scale[s][:, e * C : (e + 1) * C],
                 start=start,
@@ -175,110 +186,111 @@ def tile_moe_sdn_lin_relu_kernel(
         def relu(j, e, acc):
             nc.scalar.activation(hidden[j][:, e * C : e * C + acc.shape[1]], acc, RELU, bias=zero_bias[:])
 
-        def relu_on_vector(j, e, acc):
-            nc.vector.tensor_scalar_max(hidden[j][:, e * C : e * C + acc.shape[1]], acc, 0.0)
-
-        def pair_plane(j, pair, k, between=lambda: None):
-            acc = bank(k, [P, 2 * C], "acc")
+        def pair_sums(j, pair, k):
+            acc = bank(k, [P, PAIR], "acc")
             for h in range(2):
                 for s in range(PASSES):
                     mx_pass(acc[:, h * C : (h + 1) * C], j, 2 * pair + h, s, s == 0, s == PASSES - 1)
-            between()
-            relu(j, 2 * pair, acc[:])
+            return acc[:]
 
-        first_acc = [bank(j, [P, 2 * C], "acc") for j in range(PLANES)]
+        first_acc = [bank(j, [P, PAIR], "acc") for j in range(PLANES)]
         for e in range(2):
             for j in range(PLANES):
                 mx_pass(first_acc[j][:, e * C : (e + 1) * C], j, e, 0, e == 0, False)
-        ratio = keep.tile([P, T], F32, name="ratio")
-        for first in range(0, BLOCKS, 3):
-            spread = bank(4 + first // 3, [P, 3, P], "spread")
-            for b in range(3):
-                nc.tensor.transpose(spread[:, b, :], ratio_cols[:, first + b : first + b + 1].to_broadcast([P, P]), ident[:])
-            nc.scalar.copy(ratio[:, first * P : (first + 3) * P], spread[:].rearrange("p b t -> p (b t)"))
-
-        def finish_first(j, empty):
+        for j in range(PLANES):
             for s in range(1, PASSES):
                 for e in range(2):
                     mx_pass(first_acc[j][:, e * C : (e + 1) * C], j, e, s, False, s == PASSES - 1 and e == 1)
-            empty(j, 0, first_acc[j][:])
+            relu(j, 0, first_acc[j][:])
 
-        for j in range(3):
-            finish_first(j, relu)
+        ratio = keep.tile([P, T], F32, name="ratio")
+        half = BLOCKS // 2
+        for k in range(2):
+            spread = bank(k, [P, half, P], "spread")
+            for b in range(half):
+                column = ratio_cols[:, half * k + b : half * k + b + 1]
+                nc.tensor.transpose(spread[:, b, :], column.to_broadcast([P, P]), ident[:])
+            nc.scalar.copy(ratio[:, half * k * P : half * (k + 1) * P], spread[:].rearrange("p b t -> p (b t)"))
+
         for j, k in ((0, 7), (1, 6)):
-            pair_plane(j, 1, k)
+            relu(j, 2, pair_sums(j, 1, k))
         last_acc = {(j, e): bank(k, [P, C], "acc") for j, e, k in ((0, 4, 4), (1, 4, 0), (0, 5, 5), (1, 5, 1))}
-        for units in (((0, 4), (1, 4), (0, 5)), ((1, 5),)):
-            for s in range(PASSES):
-                for j, e in units:
-                    mx_pass(last_acc[j, e][:], j, e, s, s == 0, s == PASSES - 1)
-        for e in (4, 5):
+        for s in range(PASSES):
+            for j, e in last_acc:
+                mx_pass(last_acc[j, e][:], j, e, s, s == 0, s == PASSES - 1)
+        for e in (E - 2, E - 1):
             relu(0, e, last_acc[0, e][:])
-            relu_on_vector(1, e, last_acc[1, e][:])
+            nc.vector.tensor_scalar_max(hidden[1][:, e * C : (e + 1) * C], last_acc[1, e][:], 0.0)
 
-        a, b, c, last = (0, 256), (256, 256), (512, 128), (640, 128)
         scaled = {(j, 0): keep.tile([P, T], F32, name="scaled%d" % j) for j in range(2)}
         for j in (2, 3):
-            for first, n in ((0, 512), (512, 256)):
+            for first, n in ((0, SPLIT), (SPLIT, T - SPLIT)):
                 scaled[j, first] = keep.tile([P, n], F32, name="scaled%d_%d" % (j, first))
         plain = [
             keep.tile([P, T], F32, name="plain0"),
-            shared.tile([P, T], F32, name="plain1", align_bytes=64, offset=34816 + 3072 * 3),
-            shared.tile([P, 512], F32, name="plain2", align_bytes=64, offset=34816 + 3072 * 4),
+            shared.tile([P, T], F32, name="plain1", align_bytes=64, offset=w1_at[1, 2]),
+            shared.tile([P, SPLIT], F32, name="plain2", align_bytes=64, offset=w1_at[2, 2]),
         ]
-        sum2 = keep.tile([P, T], F32, name="sum2")
-        sum3 = keep.tile([P, T], F32, name="sum3")
+        summed2 = keep.tile([P, T - SPLIT], F32, name="summed2")
+        summed3 = keep.tile([P, T], F32, name="summed3")
 
-        def gather_scaled(dst, j, first):
+        def window(j, r, first, n):
+            return hidden[j][:].indirect(pos_sb[r][:, first // 16 : (first + n) // 16])
+
+        def gather_scaled(j, first):
+            dst = scaled[j, first][:]
             n = dst.shape[1]
-            offsets = pos_sb[0][:, first // 16 : (first + n) // 16]
-            nc.vector.tensor_tensor(dst, hidden[j][:].indirect(offsets), ratio[:, first : first + n], ALU.mult)
+            nc.vector.tensor_tensor(dst, window(j, 0, first, n), ratio[:, first : first + n], ALU.mult)
 
-        def gather_plain(dst, j, first):
-            offsets = pos_sb[1][:, first // 16 : (first + dst.shape[1]) // 16]
-            nc.scalar.activation(dst, hidden[j][:].indirect(offsets), COPY)
+        def gather_plain(j, first, n):
+            nc.scalar.activation(plain[j][:, first : first + n], window(j, 1, first, n), COPY)
 
         def gather_sum(dst, j, first, other):
-            offsets = pos_sb[1][:, first // 16 : (first + other.shape[1]) // 16]
-            nc.vector.tensor_tensor(dst[:, first : first + other.shape[1]], hidden[j][:].indirect(offsets), other, ALU.add)
+            nc.vector.tensor_tensor(dst, window(j, 1, first, other.shape[1]), other, ALU.add)
 
-        gather_scaled(scaled[0, 0][:], 0, 0)
-        gather_plain(plain[0][:], 0, 0)
-        pair_plane(2, 1, 2)
-        pair_plane(2, 2, 7)
-        gather_scaled(scaled[1, 0][:], 1, 0)
-        finish_first(3, relu_on_vector)
-        pair_plane(3, 1, 6, between=lambda: gather_plain(plain[1][:], 1, 0))
+        gather_scaled(0, 0)
+        gather_plain(0, 0, T)
+        relu(2, 2, pair_sums(2, 1, 2))
+        relu(2, 4, pair_sums(2, 2, 7))
+        gather_scaled(1, 0)
+        second_pair_plane3 = pair_sums(3, 1, 6)
+        gather_plain(1, 0, T)
+        relu(3, 2, second_pair_plane3)
+
         w2_scales_i = w2_scales.bitcast(I32).rearrange("s (q r) n -> r q (s n)", r=4)
         for r in range(4):
-            nc.sync.dma_start(w1_scale[4 + r : P : 32, 0, :N].bitcast(I32), w2_scales_i[r])
-        w2_sb = shared.tile([P, N], I32, name="w2_sb", align_bytes=64, offset=0)
+            nc.sync.dma_start(w_scale[4 + r : P : 32, 0, :N].bitcast(I32), w2_scales_i[r])
+        w2_sb = shared.tile([P, N], I32, name="w2_sb", align_bytes=64, offset=W1_FIRST_AT)
         nc.sync.dma_start(w2_sb[:], w2_words[0].rearrange("p n d -> p (n d)").bitcast(I32))
 
         c_tok = [keep.tile([P, 2, P, 2], BF16, name="c_tok%d" % block, align_bytes=64) for block in range(BLOCKS)]
 
-        low = [bank(k, [P, 2, 2, P], "low") for k in (5, 0, 1)]
-        high = []
+        turned = {}
 
-        def pair_of_planes(block, j):
-            if j < 2:
-                return low[block // 2][:, block % 2, :, :]
-            return high[block // 2][:, block % 2, :, :] if block < 4 else high[block - 2][:, 0, :, :]
+        def open_turned(j, first, n, k):
+            tile = bank(k, [P, n // P, 2, P], "turned")
+            for b in range(n // P):
+                turned[first // P + b, j] = tile[:, b, :, :]
 
         def turn(j, block, terms):
+            dst = turned[block, j - j % 2][:, j % 2, :]
             for k, term in enumerate(terms):
-                nc.tensor.matmul(pair_of_planes(block, j)[:, j % 2, :], term, ident[:], start=k == 0, stop=k == len(terms) - 1, is_transpose=True)
+                nc.tensor.matmul(dst, term, ident[:], start=k == 0, stop=k == len(terms) - 1, is_transpose=True)
 
-        def cols(tile, block, base=0):
-            return tile[:, block * P - base : (block + 1) * P - base]
+        def block_of(tile, block):
+            return tile[:, block * P : (block + 1) * P]
 
-        def round_out(block, j, on_vector=False):
-            dst = c_tok[block][:, :, 32 * j : 32 * (j + 2), :]
-            src = pair_of_planes(block, j).rearrange("p k (m u v) -> p u (k m) v", u=2, v=2)
-            if on_vector:
-                nc.vector.tensor_scalar_mul(dst, src, pivot[:, block : block + 1])
-            else:
-                nc.scalar.activation(dst, src, COPY, scale=pivot[:, block : block + 1])
+        def round_views(block, j):
+            return (
+                c_tok[block][:, :, 32 * j : 32 * (j + 2), :],
+                turned[block, j].rearrange("p k (m u v) -> p u (k m) v", u=2, v=2),
+            )
+
+        def round_on_scalar(block, j):
+            nc.scalar.activation(*round_views(block, j), COPY, scale=pivot[:, block : block + 1])
+
+        def round_on_vector(block, j):
+            nc.vector.tensor_scalar_mul(*round_views(block, j), pivot[:, block : block + 1])
 
         grouped, c_words, c_scale = {}, {}, {}
 
@@ -286,8 +298,8 @@ def tile_moe_sdn_lin_relu_kernel(
             back = bank(k, [P, n // P, 2, P], "back")
             for b in range(n // P):
                 for u in range(2):
-                    pairs = c_tok[first // P + b][:, u, :, :].rearrange("p m v -> p (m v)").bitcast(F32)
-                    nc.tensor.transpose(back[:, b, u, :], pairs, ident[:])
+                    words = c_tok[first // P + b][:, u, :, :].rearrange("p m v -> p (m v)").bitcast(F32)
+                    nc.tensor.transpose(back[:, b, u, :], words, ident[:])
             grouped[first] = keep.tile([P, 4 * n], BF16, name="grouped%d" % first, align_bytes=64)
             copy(
                 grouped[first][:].bitcast(F32).rearrange("p (b t u) -> p b t u", t=P, u=2),
@@ -304,7 +316,7 @@ def tile_moe_sdn_lin_relu_kernel(
             nc.tensor.matmul_mx(
                 out=projected[:],
                 lhsT=w2_sb[:].bitcast(FP8X4),
-                lhsT_scale=w1_scale[4:P, 0, :N],
+                lhsT_scale=w_scale[4:P, 0, :N],
                 rhs=c_words[first][:].bitcast(FP8X4),
                 rhs_scale=c_scale[first][:],
                 start=True,
@@ -314,42 +326,44 @@ def tile_moe_sdn_lin_relu_kernel(
             copy(res[:], projected[:])
             nc.sync.dma_start(out[:, first : first + n], res[:])
 
+        for first, k in ((0, 5), (256, 0), (512, 1)):
+            open_turned(0, first, 256, k)
+        for block in range(BLOCKS):
+            turn(0, block, [block_of(scaled[0, 0], block), block_of(plain[0], block)])
+        relu(3, 4, pair_sums(3, 2, 4))
+        for (first, n), k in zip(CHUNKS, (2, 7, 3, 6)):
+            open_turned(2, first, n, k)
+        gather_scaled(2, SPLIT)
+        gather_scaled(2, 0)
+        gather_sum(summed2[:], 2, SPLIT, scaled[2, SPLIT][:])
+        for chunk in CHUNKS[:2]:
+            gather_plain(2, *chunk)
+        gather_scaled(3, 0)
+        gather_scaled(3, SPLIT)
+        for first, n in CHUNKS:
+            base = SPLIT * (first // SPLIT)
+            gather_sum(summed3[:, first : first + n], 3, first, scaled[3, base][:, first - base : first - base + n])
+        for block in range(BLOCKS):
+            turn(1, block, [block_of(scaled[1, 0], block), block_of(plain[1], block)])
+        for block in range(SPLIT // P, BLOCKS):
+            turn(2, block, [block_of(summed2, block - SPLIT // P)])
+        for block in range(SPLIT // P):
+            turn(2, block, [block_of(scaled[2, 0], block), block_of(plain[2], block)])
+        for block in range(BLOCKS):
+            round_on_scalar(block, 0)
+        for block in range(BLOCKS):
+            turn(3, block, [block_of(summed3, block)])
+
+        for k, (first, n) in enumerate(CHUNKS):
+            for block in range(first // P, (first + n) // P):
+                (round_on_vector if k == 1 else round_on_scalar)(block, 2)
         on_scalar, on_vector = nc.scalar.copy, nc.vector.tensor_copy
-        for block in range(BLOCKS):
-            turn(0, block, [cols(scaled[0, 0], block), cols(plain[0], block)])
-        pair_plane(3, 2, 4)
-        high.extend(bank(k, [P, n // P, 2, P], "high") for k, (first, n) in zip((2, 7, 3, 6), (a, b, c, last)))
-        gather_scaled(scaled[2, 512][:], 2, 512)
-        gather_scaled(scaled[2, 0][:], 2, 0)
-        gather_sum(sum2, 2, 512, scaled[2, 512][:])
-        for first in (0, 256):
-            gather_plain(plain[2][:, first : first + 256], 2, first)
-        gather_scaled(scaled[3, 0][:], 3, 0)
-        gather_scaled(scaled[3, 512][:], 3, 512)
-        for first, n in (a, b, c, last):
-            base = 512 * (first // 512)
-            gather_sum(sum3, 3, first, scaled[3, base][:, first - base : first - base + n])
-        for block in range(BLOCKS):
-            turn(1, block, [cols(scaled[1, 0], block), cols(plain[1], block)])
-        for block in (4, 5):
-            turn(2, block, [cols(sum2, block)])
-        for block in range(4):
-            turn(2, block, [cols(scaled[2, 0], block), cols(plain[2], block)])
-        for block in range(BLOCKS):
-            round_out(block, 0)
-        for block in range(BLOCKS):
-            turn(3, block, [cols(sum3, block)])
-        for block in range(BLOCKS):
-            round_out(block, 2, on_vector=block in (2, 3))
-        turn_back(*a, on_vector, 4)
-        turn_back(*b, on_scalar, 5)
-        quantize(*a)
-        turn_back(*c, on_vector, 0)
-        turn_back(*last, on_scalar, 1)
-        quantize(*b)
-        quantize(*c)
-        quantize(*last)
-        project(*a, on_scalar, 2)
-        project(*b, on_scalar, 7)
-        project(*c, on_vector, 3)
-        project(*last, on_vector, 6)
+        turn_back(*CHUNKS[0], on_vector, 4)
+        turn_back(*CHUNKS[1], on_scalar, 5)
+        quantize(*CHUNKS[0])
+        turn_back(*CHUNKS[2], on_vector, 0)
+        turn_back(*CHUNKS[3], on_scalar, 1)
+        for chunk in CHUNKS[1:]:
+            quantize(*chunk)
+        for chunk, copy, k in zip(CHUNKS, (on_scalar, on_scalar, on_vector, on_vector), (2, 7, 3, 6)):
+            project(*chunk, copy, k)

@@ -29,26 +29,31 @@ PAIR = 2 * C
 PLANE_BYTES = 2 * P
 TINY = 2.0**-60
 
-SCALE_WINDOW = 2048
+BYTE_GATHER = 512
+PAIR_ROWS = (80, 112)
+ZEROS = 64
 
-LATER_GATHERS = (
-    [(PASSES - 1, 0, PAIR)]
-    + [(s, PAIR, PAIR) for s in range(PASSES)]
-    + [(s, 2 * PAIR, PAIR) for s in range(PASSES - 1)]
-    + [(PASSES - 1, e * C, C) for e in (E - 2, E - 1)]
+WORD_GATHERS = (
+    ((0, 0, C), 0),
+    ((0, C, C), 1024),
+    ((0, PAIR, PAIR), 2048),
+    ((1, 0, PAIR), 4096),
+    ((2, 0, PAIR), 6144),
+    ((1, PAIR, PAIR), 8192),
+    ((2, PAIR, PAIR), 10240),
+    ((1, 2 * PAIR, PAIR), 12288),
+    ((2, 2 * PAIR, PAIR), 14336),
+    ((0, 4 * C, C), 4096),
+    ((0, 5 * C, C), 5120),
 )
 
-W1_PARTS = ((0, 0, 4), (1, 0, 2), (2, 0, 2), (1, 2, 2), (2, 2, 2))
+W1_PARTS = ((0, 4, 0, 4), (4, 2, 0, 4), (6, 6, 0, 2), (12, 6, 0, 2), (6, 6, 2, 2), (12, 6, 2, 2))
 
 CHUNKS = ((0, 256), (256, 256), (512, P), (640, P))
 SPLIT = 512
 
-W1_FIRST_AT = 0
-SCALE_WINDOW_AT = 17408
-LATER_WORDS_AT = SCALE_WINDOW_AT + SCALE_WINDOW // 2
-SIDE_AT = SCALE_WINDOW_AT + SCALE_WINDOW
-W1_HALF_BYTES = 2 * PASSES * 2 * PLANE_BYTES
-W1_HALVES_AT = 37888
+W1_AT = (0, 4096, 6144, 9216, 12288, 15360)
+WORDS_AT = 20480
 
 
 def tile_moe_sdn_lin_relu_kernel(
@@ -67,118 +72,121 @@ def tile_moe_sdn_lin_relu_kernel(
         offs_sb = lists.tile([P, S // 16], U16, name="offs_sb")
         pos_sb = [lists.tile([P, T // 16], U16, name="pos%d_sb" % r) for r in range(2)]
 
-        x_scale_win = shared.tile([P, SCALE_WINDOW], U8, name="x_scale_win", align_bytes=64, offset=SCALE_WINDOW_AT)
-        w_scale = keep.tile([P, E * PASSES, H], U8, name="w_scale", align_bytes=64)
-        slot_scale = [keep.tile([P, S], U8, name="slot_scale%d" % s, align_bytes=64) for s in range(PASSES)]
+        scale_win = keep.tile([P, T], U8, name="scale_win", align_bytes=64)
+        w_scale = [keep.tile([P, rows, H], U8, name="w_scale%d" % rows, align_bytes=64) for rows in (2 * PASSES, 4 * PASSES)]
+        slot_scale = keep.tile([P, S], U8, name="slot_scale", align_bytes=64)
+        moved_scale = keep.tile([P, PASSES - 1, S], U8, name="moved_scale", align_bytes=64)
         zero_in = keep.tile([P, 1], F32, name="zero_in")
-        gate_rows = keep.tile([P, P], F32, name="gate_rows")
+        zeros = keep.tile([P, ZEROS], I32, name="zeros")
+        gate_rows = keep.tile([P, T // 2], F32, name="gate_rows")
         ident = keep.tile([P, P], F32, name="ident")
-        win_i = x_scale_win[:].bitcast(I32)
-        nc.gpsimd.memset(win_i[:, : T // 4], 0)
+        win_i = scale_win[:].bitcast(I32)
+        for first, last in ((0, 80), (96, 112)):
+            nc.gpsimd.memset(win_i[first:last, :], 0)
         nc.gpsimd.memset(zero_in[:], 0.0)
-        nc.vector.memset(w_scale[:].rearrange("p g n -> p (g n)").bitcast(I32), 0)
-        nc.vector.memset(win_i[:, T // 4 :], 0)
+        nc.vector.memset(zeros[:], 0)
+        nc.vector.memset(w_scale[0][:].rearrange("p g n -> p (g n)").bitcast(I32), 0)
+        nc.vector.memset(moved_scale[:].rearrange("p s n -> p (s n)").bitcast(I32), 0)
         nc.gpsimd.memset(gate_rows[:], 0.0)
         make_identity(nc, ident[:])
+        later_scales = w_scale[1][:].rearrange("p g n -> p (g n)").bitcast(U32).rearrange("p (a b) -> p a b", b=ZEROS)
+        nc.scalar.copy(later_scales, zeros[:].bitcast(U32).unsqueeze(1).to_broadcast(later_scales.shape))
 
         x_words_i = x_words.rearrange("s p t d -> p s (t d)").bitcast(I32)
+        x_scales_i = x_scales.bitcast(I32)
         w1_words_i = w1_words.bitcast(I32).rearrange("e s p n -> p (e s) n")
+        w1_scales_i = w1_scales.bitcast(I32).rearrange("e s (q r) n -> r q (e s) n", r=4)
         x_first = keep.tile([P, T], I32, name="x_first", align_bytes=64)
         x_rest = keep.tile([P, PASSES - 1, T], I32, name="x_rest", align_bytes=64)
         x_win = [x_first[:]] + [x_rest[:, s, :] for s in range(PASSES - 1)]
+        w1_part = [
+            shared.tile([P, rows, PLANE_BYTES * planes], U8, name="w1_part%d" % k, align_bytes=64, offset=W1_AT[k])
+            for k, (row, rows, plane, planes) in enumerate(W1_PARTS)
+        ]
 
-        w1_at = {part[:2]: W1_HALVES_AT + W1_HALF_BYTES * k for k, part in enumerate(W1_PARTS[1:])}
-        w1_at[0, 0] = W1_FIRST_AT
-        w1_part = {
-            (pair, plane): shared.tile(
-                [P, 2 * PASSES, PLANE_BYTES * planes],
-                U8,
-                name="w1_part%d%d" % (pair, plane),
-                align_bytes=64,
-                offset=w1_at[pair, plane],
-            )
-            for pair, plane, planes in W1_PARTS
-        }
-
-        def load_part(pair, plane, planes):
-            rows = slice(2 * PASSES * pair, 2 * PASSES * (pair + 1))
+        def load_part(k):
+            row, rows, plane, planes = W1_PARTS[k]
             words = slice(PLANE_BYTES // 4 * plane, PLANE_BYTES // 4 * (plane + planes))
-            nc.sync.dma_start(w1_part[pair, plane][:].bitcast(I32), w1_words_i[:, rows, words])
+            nc.sync.dma_start(w1_part[k][:].bitcast(I32), w1_words_i[:, row : row + rows, words])
+
+        def load_scales(tile, row):
+            for r in range(4):
+                nc.sync.dma_start(tile[r:P:32].bitcast(I32), w1_scales_i[r][:, row : row + tile.shape[1]])
 
         nc.sync.dma_start(offs_sb[:], offs)
+        for h, row in enumerate(PAIR_ROWS):
+            nc.sync.dma_start(win_i[row : row + 16, :], x_scales_i[1:, 8 * h : 8 * h + 8, :].rearrange("s b n -> b s n"))
+        for q in range(4):
+            nc.sync.dma_start(win_i[32 * q : 32 * q + 4, :], x_scales_i[0, 4 * q : 4 * q + 4, :])
         nc.sync.dma_start(x_first[:], x_words_i[:, 0, :])
-        x_scales_i = x_scales.bitcast(I32)
-        for q in range(2):
-            nc.sync.dma_start(win_i[32 * q : 32 * q + 12, : T // 4], x_scales_i[:, 4 * q : 4 * q + 4, :])
-        for q in range(2, 4):
-            nc.scalar.dma_start(win_i[32 * q : 32 * q + 4, : T // 4], x_scales_i[0, 4 * q : 4 * q + 4, :])
-            nc.scalar.dma_start(win_i[32 * q - 8 : 32 * q, : T // 4], x_scales_i[1:, 4 * q : 4 * q + 4, :])
         zero_bias = keep.tile([P, 1], F32, name="zero_bias")
         nc.scalar.activation(zero_bias[:], zero_in[:], RELU)
-        w1_scales_i = w1_scales.bitcast(I32).rearrange("e s (q r) n -> r q (e s) n", r=4)
+        nc.sync.dma_start(gate_rows[:4, :], gate[:, 0, :].rearrange("r (h n) -> r h n", h=2))
+        load_scales(w_scale[0], 0)
+        load_part(0)
         nc.sync.dma_start(x_rest[:], x_words_i[:, 1:, :])
-        nc.sync.dma_start(gate_rows[: 2 * BLOCKS, :], gate[:, 0, :].rearrange("r (b m) -> r b m", m=P))
-        load_part(*W1_PARTS[0])
-        for r in range(4):
-            nc.sync.dma_start(w_scale[r:P:32, : 2 * PASSES, :].bitcast(I32), w1_scales_i[r][:, : 2 * PASSES])
-        for r, pos in enumerate((pos1, pos2)):
-            nc.sync.dma_start(pos_sb[r][:], pos)
 
         slot_words = {}
 
-        def gather_words(dst, s, first, n):
+        def gather_bytes(first):
+            offsets = offs_sb[:, first // 16 : (first + BYTE_GATHER) // 16]
+            nc.vector.tensor_copy(slot_scale[:, first : first + BYTE_GATHER], scale_win[:].indirect(offsets))
+
+        def gather_words(k):
+            (s, first, n), at = WORD_GATHERS[k]
+            dst = shared.tile([P, n], U32, name="words%d" % k, align_bytes=64, offset=WORDS_AT + at)
             offsets = offs_sb[:, first // 16 : (first + n) // 16]
-            nc.vector.tensor_copy(dst, x_win[s].bitcast(U32).indirect(offsets))
+            nc.vector.tensor_copy(dst[:], x_win[s].bitcast(U32).indirect(offsets))
             for col in range(0, n, C):
                 slot_words[s, (first + col) // C] = dst[:, col : col + C]
 
-        first_words = keep.tile([P, PAIR], U32, name="first_words", align_bytes=64)
-        gather_words(first_words[:], 0, 0, PAIR)
-        nc.vector.tensor_copy(slot_scale[0][:], x_scale_win[:].indirect(offs_sb[:]))
-        for s in range(1, PASSES):
-            for row, source in ((0, 4 * s), (64, 64 - 12 + 4 * s)):
-                nc.sync.dma_start(
-                    slot_scale[s][row : row + 64, :].bitcast(I32), slot_scale[0][source : source + 64, :].bitcast(I32)
-                )
-        for r in range(4):
-            nc.sync.dma_start(w_scale[r:P:32, 2 * PASSES :, :].bitcast(I32), w1_scales_i[r][:, 2 * PASSES :])
-        for part in W1_PARTS[1:]:
-            load_part(*part)
+        gather_bytes(0)
+        gather_bytes(BYTE_GATHER)
+        gather_words(0)
+        gather_bytes(2 * BYTE_GATHER)
+        gather_words(1)
+        for q in range(4):
+            row = PAIR_ROWS[q // 2] + 8 * (q % 2)
+            nc.sync.dma_start(moved_scale[32 * q : 32 * q + 4].bitcast(I32), slot_scale[row : row + 8, :].bitcast(I32))
+        load_part(1)
+        load_scales(w_scale[1], 2 * PASSES)
+        load_part(2)
+        load_part(3)
+        for r, pos in enumerate((pos1, pos2)):
+            nc.sync.dma_start(pos_sb[r][:], pos)
+        load_part(4)
+        load_part(5)
 
-        gate_cols = bank(6, [P, P], "gate_cols")
-        nc.tensor.transpose(gate_cols[:], gate_rows[:], ident[:])
+        half = BLOCKS // 2
+        gate_cols = bank(6, [P, half, P], "gate_cols")
+        for b in range(half):
+            nc.tensor.transpose(gate_cols[:, b, :], gate_rows[:, b * P : (b + 1) * P], ident[:])
         gates = keep.tile([P, 2, BLOCKS], F32, name="gates")
-        side = shared.tile([P, BLOCKS], F32, name="side", align_bytes=64, offset=SIDE_AT)
+        side = shared.tile([P, BLOCKS], F32, name="side", align_bytes=64, offset=WORDS_AT + WORD_GATHERS[2][1])
         pivot = keep.tile([P, BLOCKS], F32, name="pivot")
         inverse = keep.tile([P, BLOCKS], F32, name="inverse")
-        ratio_cols = keep.tile([P, BLOCKS], F32, name="ratio_cols")
-        nc.scalar.copy(gates[:].rearrange("p r b -> p (r b)"), gate_cols[:, : 2 * BLOCKS])
-        nc.scalar.activation(side[:], gate_cols[:, BLOCKS : 2 * BLOCKS], SIGN, bias=TINY / 2)
+        nc.scalar.copy(gates[:].rearrange("p r (h b) -> p (r h) b", h=2), gate_cols[:, :, :4].rearrange("p b k -> p k b"))
+        nc.scalar.activation(side[:], gates[:, 1, :], SIGN, bias=TINY / 2)
         for b in range(BLOCKS):
             nc.scalar.activation(pivot[:, b : b + 1], side[:, b : b + 1], IDENTITY, bias=gates[:, 1, b : b + 1], scale=TINY)
-        second_words = keep.tile([P, PAIR], U32, name="second_words", align_bytes=64)
-        gather_words(second_words[:], 1, 0, PAIR)
         nc.vector.reciprocal(inverse[:], pivot[:])
-        for b in range(BLOCKS):
-            nc.scalar.activation(ratio_cols[:, b : b + 1], gates[:, 0, b : b + 1], COPY, scale=inverse[:, b : b + 1])
-
-        later_words = shared.tile([P, PASSES * S - 2 * PAIR], U32, name="later_words", align_bytes=64, offset=LATER_WORDS_AT)
-        col = 0
-        for s, first, n in LATER_GATHERS:
-            gather_words(later_words[:, col : col + n], s, first, n)
-            col += n
+        for k in range(2, 7):
+            gather_words(k)
 
         hidden = [keep.tile([P, S], F32, name="hidden%d" % j) for j in range(PLANES)]
 
         def mx_pass(acc, j, e, s, start, stop):
-            plane = max(first for pair, first in w1_part if pair == e // 2 and first <= j)
-            at = PLANE_BYTES * (j - plane)
+            row = PASSES * e + s
+            k = max(k for k, part in enumerate(W1_PARTS) if part[0] <= row < part[0] + part[1] and part[2] <= j)
+            at = PLANE_BYTES * (j - W1_PARTS[k][2])
+            w_rows = w_scale[0][:, row, :] if row < 2 * PASSES else w_scale[1][:, row - 2 * PASSES, :]
+            x_rows = slot_scale[:] if s == 0 else moved_scale[:, s - 1, :]
             nc.tensor.matmul_mx(
                 out=acc,
-                lhsT=w1_part[e // 2, plane][:, (e % 2) * PASSES + s, at : at + PLANE_BYTES].bitcast(FP4X4),
-                lhsT_scale=w_scale[:, e * PASSES + s, P * j : P * (j + 1)],
+                lhsT=w1_part[k][:, row - W1_PARTS[k][0], at : at + PLANE_BYTES].bitcast(FP4X4),
+                lhsT_scale=w_rows[:, P * j : P * (j + 1)],
                 rhs=slot_words[s, e].bitcast(FP8X4),
-                rhs_scale=slot_scale[s][:, e * C : (e + 1) * C],
+                rhs_scale=x_rows[:, e * C : (e + 1) * C],
                 start=start,
                 stop=stop,
             )
@@ -194,42 +202,47 @@ def tile_moe_sdn_lin_relu_kernel(
             return acc[:]
 
         first_acc = [bank(j, [P, PAIR], "acc") for j in range(PLANES)]
-        for e in range(2):
-            for j in range(PLANES):
-                mx_pass(first_acc[j][:, e * C : (e + 1) * C], j, e, 0, e == 0, False)
-        for j in range(PLANES):
-            for s in range(1, PASSES):
-                for e in range(2):
-                    mx_pass(first_acc[j][:, e * C : (e + 1) * C], j, e, s, False, s == PASSES - 1 and e == 1)
-            relu(j, 0, first_acc[j][:])
+        def first_pair_pass(s):
+            for e in range(2):
+                for j in range(PLANES):
+                    mx_pass(first_acc[j][:, e * C : (e + 1) * C], j, e, s, s == 0 and e == 0, False)
 
+        first_pair_pass(0)
+        ratio_cols = shared.tile([P, BLOCKS], F32, name="ratio_cols", align_bytes=64, offset=WORDS_AT)
+        for b in range(BLOCKS):
+            nc.scalar.activation(ratio_cols[:, b : b + 1], gates[:, 0, b : b + 1], COPY, scale=inverse[:, b : b + 1])
         ratio = keep.tile([P, T], F32, name="ratio")
-        half = BLOCKS // 2
         for k in range(2):
-            spread = bank(k, [P, half, P], "spread")
+            spread = bank(4 + k, [P, half, P], "spread")
             for b in range(half):
                 column = ratio_cols[:, half * k + b : half * k + b + 1]
                 nc.tensor.transpose(spread[:, b, :], column.to_broadcast([P, P]), ident[:])
             nc.scalar.copy(ratio[:, half * k * P : half * (k + 1) * P], spread[:].rearrange("p b t -> p (b t)"))
+        first_pair_pass(1)
+        for k in range(7, len(WORD_GATHERS)):
+            gather_words(k)
+        for j in range(PLANES):
+            for e in range(2):
+                mx_pass(first_acc[j][:, e * C : (e + 1) * C], j, e, PASSES - 1, False, e == 1)
+            relu(j, 0, first_acc[j][:])
 
         for j, k in ((0, 7), (1, 6)):
             relu(j, 2, pair_sums(j, 1, k))
         last_acc = {(j, e): bank(k, [P, C], "acc") for j, e, k in ((0, 4, 4), (1, 4, 0), (0, 5, 5), (1, 5, 1))}
-        for s in range(PASSES):
+        for s in (1, 2, 0):
             for j, e in last_acc:
-                mx_pass(last_acc[j, e][:], j, e, s, s == 0, s == PASSES - 1)
+                mx_pass(last_acc[j, e][:], j, e, s, s == 1, s == 0)
         for e in (E - 2, E - 1):
             relu(0, e, last_acc[0, e][:])
             nc.vector.tensor_scalar_max(hidden[1][:, e * C : (e + 1) * C], last_acc[1, e][:], 0.0)
-
         scaled = {(j, 0): keep.tile([P, T], F32, name="scaled%d" % j) for j in range(2)}
         for j in (2, 3):
             for first, n in ((0, SPLIT), (SPLIT, T - SPLIT)):
                 scaled[j, first] = keep.tile([P, n], F32, name="scaled%d_%d" % (j, first))
         plain = [
             keep.tile([P, T], F32, name="plain0"),
-            shared.tile([P, T], F32, name="plain1", align_bytes=64, offset=w1_at[1, 2]),
-            shared.tile([P, SPLIT], F32, name="plain2", align_bytes=64, offset=w1_at[2, 2]),
+            shared.tile([P, T], F32, name="plain1", align_bytes=64, offset=W1_AT[4]),
+            shared.tile([P, SPLIT], F32, name="plain2", align_bytes=64, offset=W1_AT[5]),
         ]
         summed2 = keep.tile([P, T - SPLIT], F32, name="summed2")
         summed3 = keep.tile([P, T], F32, name="summed3")
@@ -259,8 +272,8 @@ def tile_moe_sdn_lin_relu_kernel(
 
         w2_scales_i = w2_scales.bitcast(I32).rearrange("s (q r) n -> r q (s n)", r=4)
         for r in range(4):
-            nc.sync.dma_start(w_scale[4 + r : P : 32, 0, :N].bitcast(I32), w2_scales_i[r])
-        w2_sb = shared.tile([P, N], I32, name="w2_sb", align_bytes=64, offset=W1_FIRST_AT)
+            nc.sync.dma_start(w_scale[0][4 + r : P : 32, 0, :N].bitcast(I32), w2_scales_i[r])
+        w2_sb = shared.tile([P, N], I32, name="w2_sb", align_bytes=64, offset=W1_AT[0])
         nc.sync.dma_start(w2_sb[:], w2_words[0].rearrange("p n d -> p (n d)").bitcast(I32))
 
         c_tok = [keep.tile([P, 2, P, 2], BF16, name="c_tok%d" % block, align_bytes=64) for block in range(BLOCKS)]
@@ -316,7 +329,7 @@ def tile_moe_sdn_lin_relu_kernel(
             nc.tensor.matmul_mx(
                 out=projected[:],
                 lhsT=w2_sb[:].bitcast(FP8X4),
-                lhsT_scale=w_scale[4:P, 0, :N],
+                lhsT_scale=w_scale[0][4:P, 0, :N],
                 rhs=c_words[first][:].bitcast(FP8X4),
                 rhs_scale=c_scale[first][:],
                 start=True,

@@ -49,7 +49,7 @@ WORD_GATHERS = (
 
 W1_PARTS = ((0, 4, 0, 4), (4, 2, 0, 4), (6, 6, 0, 2), (12, 6, 0, 2), (6, 6, 2, 2), (12, 6, 2, 2))
 
-CHUNKS = ((0, 256), (256, 256), (512, P), (640, P))
+CHUNKS = ((0, 256), (512, 256), (256, P), (384, P))
 SPLIT = 512
 
 W1_AT = (0, 4096, 6144, 9216, 12288, 15360)
@@ -89,8 +89,6 @@ def tile_moe_sdn_lin_relu_kernel(
         nc.vector.memset(moved_scale[:].rearrange("p s n -> p (s n)").bitcast(I32), 0)
         nc.gpsimd.memset(gate_rows[:], 0.0)
         make_identity(nc, ident[:])
-        later_scales = w_scale[1][:].rearrange("p g n -> p (g n)").bitcast(U32).rearrange("p (a b) -> p a b", b=ZEROS)
-        nc.scalar.copy(later_scales, zeros[:].bitcast(U32).unsqueeze(1).to_broadcast(later_scales.shape))
 
         x_words_i = x_words.rearrange("s p t d -> p s (t d)").bitcast(I32)
         x_scales_i = x_scales.bitcast(I32)
@@ -115,10 +113,12 @@ def tile_moe_sdn_lin_relu_kernel(
 
         nc.sync.dma_start(offs_sb[:], offs)
         for h, row in enumerate(PAIR_ROWS):
-            nc.sync.dma_start(win_i[row : row + 16, :], x_scales_i[1:, 8 * h : 8 * h + 8, :].rearrange("s b n -> b s n"))
+            nc.scalar.dma_start(win_i[row : row + 16, :], x_scales_i[1:, 8 * h : 8 * h + 8, :].rearrange("s b n -> b s n"))
         for q in range(4):
-            nc.sync.dma_start(win_i[32 * q : 32 * q + 4, :], x_scales_i[0, 4 * q : 4 * q + 4, :])
+            (nc.sync if q < 2 else nc.scalar).dma_start(win_i[32 * q : 32 * q + 4, :], x_scales_i[0, 4 * q : 4 * q + 4, :])
         nc.sync.dma_start(x_first[:], x_words_i[:, 0, :])
+        later_scales = w_scale[1][:].rearrange("p g n -> p (g n)").bitcast(U32).rearrange("p (a b) -> p a b", b=ZEROS)
+        nc.scalar.copy(later_scales, zeros[:].bitcast(U32).unsqueeze(1).to_broadcast(later_scales.shape))
         zero_bias = keep.tile([P, 1], F32, name="zero_bias")
         nc.scalar.activation(zero_bias[:], zero_in[:], RELU)
         nc.sync.dma_start(gate_rows[:4, :], gate[:, 0, :].rearrange("r (h n) -> r h n", h=2))
@@ -235,17 +235,17 @@ def tile_moe_sdn_lin_relu_kernel(
         for e in (E - 2, E - 1):
             relu(0, e, last_acc[0, e][:])
             nc.vector.tensor_scalar_max(hidden[1][:, e * C : (e + 1) * C], last_acc[1, e][:], 0.0)
-        scaled = {(j, 0): keep.tile([P, T], F32, name="scaled%d" % j) for j in range(2)}
-        for j in (2, 3):
-            for first, n in ((0, SPLIT), (SPLIT, T - SPLIT)):
-                scaled[j, first] = keep.tile([P, n], F32, name="scaled%d_%d" % (j, first))
+        spans = {0: ((0, T),), 1: ((0, T),), 2: ((SPLIT, T - SPLIT), (0, SPLIT)), 3: ((SPLIT, T - SPLIT), (0, 256), (256, 256))}
+        scaled = {
+            (j, first): keep.tile([P, n], F32, name="scaled%d_%d" % (j, first)) for j in spans for first, n in spans[j]
+        }
         plain = [
             keep.tile([P, T], F32, name="plain0"),
             shared.tile([P, T], F32, name="plain1", align_bytes=64, offset=W1_AT[4]),
             shared.tile([P, SPLIT], F32, name="plain2", align_bytes=64, offset=W1_AT[5]),
+            keep.tile([P, 256], F32, name="plain3"),
         ]
-        summed2 = keep.tile([P, T - SPLIT], F32, name="summed2")
-        summed3 = keep.tile([P, T], F32, name="summed3")
+        summed = {j: keep.tile([P, T], F32, name="summed%d" % j) for j in (2, 3)}
 
         def window(j, r, first, n):
             return hidden[j][:].indirect(pos_sb[r][:, first // 16 : (first + n) // 16])
@@ -266,7 +266,7 @@ def tile_moe_sdn_lin_relu_kernel(
         relu(2, 2, pair_sums(2, 1, 2))
         relu(2, 4, pair_sums(2, 2, 7))
         gather_scaled(1, 0)
-        second_pair_plane3 = pair_sums(3, 1, 6)
+        second_pair_plane3 = pair_sums(3, 1, 3)
         gather_plain(1, 0, T)
         relu(3, 2, second_pair_plane3)
 
@@ -278,32 +278,28 @@ def tile_moe_sdn_lin_relu_kernel(
 
         c_tok = [keep.tile([P, 2, P, 2], BF16, name="c_tok%d" % block, align_bytes=64) for block in range(BLOCKS)]
 
-        turned = {}
-
-        def open_turned(j, first, n, k):
-            tile = bank(k, [P, n // P, 2, P], "turned")
-            for b in range(n // P):
-                turned[first // P + b, j] = tile[:, b, :, :]
+        turned = [bank(k, [P, PLANES, P], "turned") for k in (0, 1, 4, 5, 6, 3)]
 
         def turn(j, block, terms):
-            dst = turned[block, j - j % 2][:, j % 2, :]
             for k, term in enumerate(terms):
-                nc.tensor.matmul(dst, term, ident[:], start=k == 0, stop=k == len(terms) - 1, is_transpose=True)
+                nc.tensor.matmul(turned[block][:, j, :], term, ident[:], start=k == 0, stop=k == len(terms) - 1, is_transpose=True)
 
-        def block_of(tile, block):
-            return tile[:, block * P : (block + 1) * P]
+        def turn_both(j, block):
+            first = max(first for first, n in spans[j] if first <= block * P)
+            terms = [scaled[j, first][:, block * P - first : (block + 1) * P - first], plain[j][:, block * P : (block + 1) * P]]
+            turn(j, block, terms)
 
-        def round_views(block, j):
-            return (
-                c_tok[block][:, :, 32 * j : 32 * (j + 2), :],
-                turned[block, j].rearrange("p k (m u v) -> p u (k m) v", u=2, v=2),
-            )
+        def turn_summed(j, block):
+            turn(j, block, [summed[j][:, block * P : (block + 1) * P]])
 
-        def round_on_scalar(block, j):
-            nc.scalar.activation(*round_views(block, j), COPY, scale=pivot[:, block : block + 1])
+        def round_views(block):
+            return c_tok[block][:], turned[block][:].rearrange("p j (m u v) -> p u (j m) v", u=2, v=2)
 
-        def round_on_vector(block, j):
-            nc.vector.tensor_scalar_mul(*round_views(block, j), pivot[:, block : block + 1])
+        def round_on_scalar(block):
+            nc.scalar.activation(*round_views(block), COPY, scale=pivot[:, block : block + 1])
+
+        def round_on_vector(block):
+            nc.vector.tensor_scalar_mul(*round_views(block), pivot[:, block : block + 1])
 
         grouped, c_words, c_scale = {}, {}, {}
 
@@ -339,44 +335,41 @@ def tile_moe_sdn_lin_relu_kernel(
             copy(res[:], projected[:])
             nc.sync.dma_start(out[:, first : first + n], res[:])
 
-        for first, k in ((0, 5), (256, 0), (512, 1)):
-            open_turned(0, first, 256, k)
+        for block in range(BLOCKS - 1):
+            turn_both(0, block)
+        relu(3, 4, pair_sums(3, 2, 2))
+        turn_both(0, BLOCKS - 1)
         for block in range(BLOCKS):
-            turn(0, block, [block_of(scaled[0, 0], block), block_of(plain[0], block)])
-        relu(3, 4, pair_sums(3, 2, 4))
-        for (first, n), k in zip(CHUNKS, (2, 7, 3, 6)):
-            open_turned(2, first, n, k)
+            turn_both(1, block)
         gather_scaled(2, SPLIT)
         gather_scaled(2, 0)
-        gather_sum(summed2[:], 2, SPLIT, scaled[2, SPLIT][:])
-        for chunk in CHUNKS[:2]:
-            gather_plain(2, *chunk)
+        gather_sum(summed[2][:, SPLIT:], 2, SPLIT, scaled[2, SPLIT][:])
         gather_scaled(3, 0)
         gather_scaled(3, SPLIT)
-        for first, n in CHUNKS:
-            base = SPLIT * (first // SPLIT)
-            gather_sum(summed3[:, first : first + n], 3, first, scaled[3, base][:, first - base : first - base + n])
-        for block in range(BLOCKS):
-            turn(1, block, [block_of(scaled[1, 0], block), block_of(plain[1], block)])
-        for block in range(SPLIT // P, BLOCKS):
-            turn(2, block, [block_of(summed2, block - SPLIT // P)])
-        for block in range(SPLIT // P):
-            turn(2, block, [block_of(scaled[2, 0], block), block_of(plain[2], block)])
-        for block in range(BLOCKS):
-            round_on_scalar(block, 0)
-        for block in range(BLOCKS):
-            turn(3, block, [block_of(summed3, block)])
+        gather_scaled(3, 256)
+        for j, first in ((2, 0), (3, 0), (2, 256)):
+            gather_plain(j, first, 256)
+        gather_sum(summed[3][:, SPLIT:], 3, SPLIT, scaled[3, SPLIT][:])
+        for first in (256, 384):
+            gather_sum(summed[3][:, first : first + P], 3, first, scaled[3, 256][:, first - 256 : first - 256 + P])
+        for block in (4, 5):
+            turn_summed(2, block)
+        for j, blocks in ((2, (0, 1)), (3, (0, 1)), (2, (2, 3))):
+            for block in blocks:
+                turn_both(j, block)
+        for block in (4, 5, 2, 3):
+            turn_summed(3, block)
 
-        for k, (first, n) in enumerate(CHUNKS):
-            for block in range(first // P, (first + n) // P):
-                (round_on_vector if k == 1 else round_on_scalar)(block, 2)
         on_scalar, on_vector = nc.scalar.copy, nc.vector.tensor_copy
-        turn_back(*CHUNKS[0], on_vector, 4)
-        turn_back(*CHUNKS[1], on_scalar, 5)
-        quantize(*CHUNKS[0])
+        for block in (0, 1, 4, 3):
+            round_on_scalar(block)
+        for block in (5, 2):
+            round_on_vector(block)
+        turn_back(*CHUNKS[0], on_vector, 7)
+        turn_back(*CHUNKS[1], on_scalar, 2)
         turn_back(*CHUNKS[2], on_vector, 0)
         turn_back(*CHUNKS[3], on_scalar, 1)
-        for chunk in CHUNKS[1:]:
+        for chunk in CHUNKS:
             quantize(*chunk)
-        for chunk, copy, k in zip(CHUNKS, (on_scalar, on_scalar, on_vector, on_vector), (2, 7, 3, 6)):
+        for chunk, copy, k in zip(CHUNKS, (on_scalar, on_scalar, on_vector, on_vector), (6, 3, 4, 5)):
             project(*chunk, copy, k)

@@ -47,12 +47,12 @@ WORD_GATHERS = (
     ((0, 5 * C, C), 5120),
 )
 
-W1_PARTS = ((0, 4, 0, 4), (4, 2, 0, 4), (6, 6, 0, 2), (12, 6, 0, 2), (6, 6, 2, 2), (12, 6, 2, 2))
+W1_PARTS = ((0, 4, 0, 4), (4, 2, 0, 4), (6, 6, 0, 3), (12, 6, 0, 2), (6, 6, 3, 1), (12, 6, 2, 2))
 
-CHUNKS = ((0, 256), (512, 256), (256, P), (384, P))
+CHUNKS = ((0, 256), (256, 256), (512, P), (640, P))
 SPLIT = 512
 
-W1_AT = (0, 4096, 6144, 9216, 12288, 15360)
+W1_AT = (0, 4096, 6144, 10752, 13824, 16896)
 WORDS_AT = 20480
 
 
@@ -73,7 +73,7 @@ def tile_moe_sdn_lin_relu_kernel(
         pos_sb = [lists.tile([P, T // 16], U16, name="pos%d_sb" % r) for r in range(2)]
 
         scale_win = keep.tile([P, T], U8, name="scale_win", align_bytes=64)
-        w_scale = [keep.tile([P, rows, H], U8, name="w_scale%d" % rows, align_bytes=64) for rows in (2 * PASSES, 4 * PASSES)]
+        w_scale = [keep.tile([P, 2 * PASSES, H], U8, name="w_scale%d" % pair, align_bytes=64) for pair in range(E // 2)]
         slot_scale = keep.tile([P, S], U8, name="slot_scale", align_bytes=64)
         moved_scale = keep.tile([P, PASSES - 1, S], U8, name="moved_scale", align_bytes=64)
         zero_in = keep.tile([P, 1], F32, name="zero_in")
@@ -117,8 +117,9 @@ def tile_moe_sdn_lin_relu_kernel(
         for q in range(4):
             (nc.sync if q < 2 else nc.scalar).dma_start(win_i[32 * q : 32 * q + 4, :], x_scales_i[0, 4 * q : 4 * q + 4, :])
         nc.sync.dma_start(x_first[:], x_words_i[:, 0, :])
-        later_scales = w_scale[1][:].rearrange("p g n -> p (g n)").bitcast(U32).rearrange("p (a b) -> p a b", b=ZEROS)
-        nc.scalar.copy(later_scales, zeros[:].bitcast(U32).unsqueeze(1).to_broadcast(later_scales.shape))
+        for tile in w_scale[1:]:
+            later_scales = tile[:].rearrange("p g n -> p (g n)").bitcast(U32).rearrange("p (a b) -> p a b", b=ZEROS)
+            nc.scalar.copy(later_scales, zeros[:].bitcast(U32).unsqueeze(1).to_broadcast(later_scales.shape))
         zero_bias = keep.tile([P, 1], F32, name="zero_bias")
         nc.scalar.activation(zero_bias[:], zero_in[:], RELU)
         nc.sync.dma_start(gate_rows[:4, :], gate[:, 0, :].rearrange("r (h n) -> r h n", h=2))
@@ -149,13 +150,13 @@ def tile_moe_sdn_lin_relu_kernel(
             row = PAIR_ROWS[q // 2] + 8 * (q % 2)
             nc.sync.dma_start(moved_scale[32 * q : 32 * q + 4].bitcast(I32), slot_scale[row : row + 8, :].bitcast(I32))
         load_part(1)
-        load_scales(w_scale[1], 2 * PASSES)
-        load_part(2)
-        load_part(3)
+        for pair in (1, 2):
+            load_part(pair + 1)
+            load_scales(w_scale[pair], 2 * PASSES * pair)
         for r, pos in enumerate((pos1, pos2)):
             nc.sync.dma_start(pos_sb[r][:], pos)
-        load_part(4)
         load_part(5)
+        load_part(4)
 
         half = BLOCKS // 2
         gate_cols = bank(6, [P, half, P], "gate_cols")
@@ -179,7 +180,7 @@ def tile_moe_sdn_lin_relu_kernel(
             row = PASSES * e + s
             k = max(k for k, part in enumerate(W1_PARTS) if part[0] <= row < part[0] + part[1] and part[2] <= j)
             at = PLANE_BYTES * (j - W1_PARTS[k][2])
-            w_rows = w_scale[0][:, row, :] if row < 2 * PASSES else w_scale[1][:, row - 2 * PASSES, :]
+            w_rows = w_scale[e // 2][:, row % (2 * PASSES), :]
             x_rows = slot_scale[:] if s == 0 else moved_scale[:, s - 1, :]
             nc.tensor.matmul_mx(
                 out=acc,
@@ -226,7 +227,7 @@ def tile_moe_sdn_lin_relu_kernel(
                 mx_pass(first_acc[j][:, e * C : (e + 1) * C], j, e, PASSES - 1, False, e == 1)
             relu(j, 0, first_acc[j][:])
 
-        for j, k in ((0, 7), (1, 6)):
+        for j, k in ((0, 7), (1, 6), (2, 2)):
             relu(j, 2, pair_sums(j, 1, k))
         last_acc = {(j, e): bank(k, [P, C], "acc") for j, e, k in ((0, 4, 4), (1, 4, 0), (0, 5, 5), (1, 5, 1))}
         for s in (1, 2, 0):
@@ -243,7 +244,7 @@ def tile_moe_sdn_lin_relu_kernel(
             keep.tile([P, T], F32, name="plain0"),
             shared.tile([P, T], F32, name="plain1", align_bytes=64, offset=W1_AT[4]),
             shared.tile([P, SPLIT], F32, name="plain2", align_bytes=64, offset=W1_AT[5]),
-            keep.tile([P, 256], F32, name="plain3"),
+            keep.tile([P, SPLIT], F32, name="plain3"),
         ]
         summed = {j: keep.tile([P, T], F32, name="summed%d" % j) for j in (2, 3)}
 
@@ -263,7 +264,6 @@ def tile_moe_sdn_lin_relu_kernel(
 
         gather_scaled(0, 0)
         gather_plain(0, 0, T)
-        relu(2, 2, pair_sums(2, 1, 2))
         relu(2, 4, pair_sums(2, 2, 7))
         gather_scaled(1, 0)
         second_pair_plane3 = pair_sums(3, 1, 3)
@@ -347,23 +347,22 @@ def tile_moe_sdn_lin_relu_kernel(
         gather_scaled(3, 0)
         gather_scaled(3, SPLIT)
         gather_scaled(3, 256)
-        for j, first in ((2, 0), (3, 0), (2, 256)):
+        for j, first in ((2, 0), (3, 0), (2, 256), (3, 256)):
             gather_plain(j, first, 256)
-        gather_sum(summed[3][:, SPLIT:], 3, SPLIT, scaled[3, SPLIT][:])
-        for first in (256, 384):
-            gather_sum(summed[3][:, first : first + P], 3, first, scaled[3, 256][:, first - 256 : first - 256 + P])
+        for first in (512, 640):
+            gather_sum(summed[3][:, first : first + P], 3, first, scaled[3, SPLIT][:, first - SPLIT : first - SPLIT + P])
         for block in (4, 5):
             turn_summed(2, block)
-        for j, blocks in ((2, (0, 1)), (3, (0, 1)), (2, (2, 3))):
+        for j, blocks in ((2, (0, 1)), (3, (0, 1)), (2, (2, 3)), (3, (2, 3))):
             for block in blocks:
                 turn_both(j, block)
-        for block in (4, 5, 2, 3):
+        for block in (4, 5):
             turn_summed(3, block)
 
         on_scalar, on_vector = nc.scalar.copy, nc.vector.tensor_copy
-        for block in (0, 1, 4, 3):
+        for block in (0, 1, 2, 5):
             round_on_scalar(block)
-        for block in (5, 2):
+        for block in (3, 4):
             round_on_vector(block)
         turn_back(*CHUNKS[0], on_vector, 7)
         turn_back(*CHUNKS[1], on_scalar, 2)
@@ -371,5 +370,5 @@ def tile_moe_sdn_lin_relu_kernel(
         turn_back(*CHUNKS[3], on_scalar, 1)
         for chunk in CHUNKS:
             quantize(*chunk)
-        for chunk, copy, k in zip(CHUNKS, (on_scalar, on_scalar, on_vector, on_vector), (6, 3, 4, 5)):
+        for chunk, copy, k in zip(CHUNKS, (on_scalar, on_scalar, on_vector, on_vector), (4, 5, 6, 3)):
             project(*chunk, copy, k)

@@ -86,7 +86,6 @@ def tile_moe_sdn_lin_relu_kernel(
         nc.gpsimd.memset(zero_in[:], 0.0)
         nc.vector.memset(zeros[:], 0)
         nc.vector.memset(w_scale[0][:].rearrange("p g n -> p (g n)").bitcast(I32), 0)
-        nc.vector.memset(moved_scale[:].rearrange("p s n -> p (s n)").bitcast(I32), 0)
         nc.gpsimd.memset(gate_rows[:], 0.0)
         make_identity(nc, ident[:])
 
@@ -117,7 +116,7 @@ def tile_moe_sdn_lin_relu_kernel(
         for q in range(4):
             (nc.sync if q < 2 else nc.scalar).dma_start(win_i[32 * q : 32 * q + 4, :], x_scales_i[0, 4 * q : 4 * q + 4, :])
         nc.sync.dma_start(x_first[:], x_words_i[:, 0, :])
-        for tile in w_scale[1:]:
+        for tile in [moved_scale] + w_scale[1:]:
             later_scales = tile[:].rearrange("p g n -> p (g n)").bitcast(U32).rearrange("p (a b) -> p a b", b=ZEROS)
             nc.scalar.copy(later_scales, zeros[:].bitcast(U32).unsqueeze(1).to_broadcast(later_scales.shape))
         zero_bias = keep.tile([P, 1], F32, name="zero_bias")

@@ -140,11 +140,10 @@ def tile_moe_sdn_lin_relu_kernel(
             for col in range(0, n, C):
                 slot_words[s, (first + col) // C] = dst[:, col : col + C]
 
-        gather_bytes(0)
-        gather_bytes(BYTE_GATHER)
-        gather_words(0)
-        gather_bytes(2 * BYTE_GATHER)
-        gather_words(1)
+        for first in range(0, S, BYTE_GATHER):
+            gather_bytes(first)
+        for k in range(2):
+            gather_words(k)
         for q in range(4):
             row = PAIR_ROWS[q // 2] + 8 * (q % 2)
             nc.sync.dma_start(moved_scale[32 * q : 32 * q + 4].bitcast(I32), slot_scale[row : row + 8, :].bitcast(I32))

from contextlib import ExitStack

import concourse.mybir as mybir
from concourse.masks import make_identity

K, T, E, C, H, N = 1536, 768, 6, 256, 512, 128
S = E * C
FLOPS = 2 * K * H * S + 2 * H * N * T

F32 = mybir.dt.float32
BF16 = mybir.dt.bfloat16
I32 = mybir.dt.int32
U32 = mybir.dt.uint32
U16 = mybir.dt.uint16
U8 = mybir.dt.uint8
FP8X4 = mybir.dt.float8_e4m3fn_x4
FP4X4 = mybir.dt.float4_e2m1fn_x4
ALU = mybir.AluOpType
COPY = mybir.ActivationFunctionType.Copy
RELU = mybir.ActivationFunctionType.Relu
SIGN = mybir.ActivationFunctionType.Sign
IDENTITY = mybir.ActivationFunctionType.Identity

P = 128
PASSES = K // 512
PLANES = H // P
BLOCKS = T // P
PAIR = 2 * C
PLANE_BYTES = 2 * P
TINY = 2.0**-60

BYTE_GATHER = 512
PAIR_ROWS = (80, 112)
ZEROS = 64

WORD_GATHERS = (
    ((0, 0, C), 0),
    ((0, C, C), 1024),
    ((0, PAIR, PAIR), 2048),
    ((1, 0, PAIR), 4096),
    ((2, 0, PAIR), 6144),
    ((1, PAIR, PAIR), 8192),
    ((2, PAIR, PAIR), 10240),
    ((1, 2 * PAIR, PAIR), 12288),
    ((2, 2 * PAIR, PAIR), 14336),
    ((0, 4 * C, C), 4096),
    ((0, 5 * C, C), 5120),
)

W1_PARTS = ((0, 4, 0, 4), (4, 2, 0, 4), (6, 6, 0, 3), (12, 6, 0, 2), (6, 6, 3, 1), (12, 6, 2, 2))

CHUNKS = ((0, 256), (256, 256), (512, P), (640, P))
SPLIT = 512

W1_AT = (0, 4096, 6144, 10752, 13824, 16896)
WORDS_AT = 20480


def tile_moe_sdn_lin_relu_kernel(
    tc, x_words, x_scales, w1_words, w1_scales, w2_words, w2_scales, gate, offs, pos1, pos2, out
):
    nc = tc.nc
    with ExitStack() as ctx:
        lists = ctx.enter_context(tc.tile_pool(name="lists", bufs=1))
        keep = ctx.enter_context(tc.tile_pool(name="keep", bufs=1))
        shared = ctx.enter_context(tc.tile_pool(name="shared", bufs=1))
        psum = ctx.enter_context(tc.psum_pool(name="psum", bufs=1))

        def bank(k, shape, name):
            return psum.tile(shape, F32, name=name, tag="bank%d" % k)

        offs_sb = lists.tile([P, S // 16], U16, name="offs_sb")
        pos_sb = [lists.tile([P, T // 16], U16, name="pos%d_sb" % r) for r in range(2)]

        scale_win = keep.tile([P, T], U8, name="scale_win", align_bytes=64)
        w_scale = [keep.tile([P, 2 * PASSES, H], U8, name="w_scale%d" % pair, align_bytes=64) for pair in range(E // 2)]
        slot_scale = keep.tile([P, S], U8, name="slot_scale", align_bytes=64)
        moved_scale = keep.tile([P, PASSES - 1, S], U8, name="moved_scale", align_bytes=64)
        zero_in = keep.tile([P, 1], F32, name="zero_in")
        zeros = keep.tile([P, ZEROS], I32, name="zeros")
        gate_rows = keep.tile([P, T // 2], F32, name="gate_rows")
        ident = keep.tile([P, P], F32, name="ident")
        win_i = scale_win[:].bitcast(I32)
        for first, last in ((0, 80), (96, 112)):
            nc.gpsimd.memset(win_i[first:last, :], 0)
        nc.gpsimd.memset(zero_in[:], 0.0)
        nc.vector.memset(zeros[:], 0)
        nc.vector.memset(w_scale[0][:].rearrange("p g n -> p (g n)").bitcast(I32), 0)
        nc.gpsimd.memset(gate_rows[:], 0.0)
        make_identity(nc, ident[:])

        x_words_i = x_words.rearrange("s p t d -> p s (t d)").bitcast(I32)
        x_scales_i = x_scales.bitcast(I32)
        w1_words_i = w1_words.bitcast(I32).rearrange("e s p n -> p (e s) n")
        w1_scales_i = w1_scales.bitcast(I32).rearrange("e s (q r) n -> r q (e s) n", r=4)
        x_first = keep.tile([P, T], I32, name="x_first", align_bytes=64)
        x_rest = keep.tile([P, PASSES - 1, T], I32, name="x_rest", align_bytes=64)
        x_win = [x_first[:]] + [x_rest[:, s, :] for s in range(PASSES - 1)]
        w1_part = [
            shared.tile([P, rows, PLANE_BYTES * planes], U8, name="w1_part%d" % k, align_bytes=64, offset=W1_AT[k])
            for k, (row, rows, plane, planes) in enumerate(W1_PARTS)
        ]

        def load_part(k):
            row, rows, plane, planes = W1_PARTS[k]
            words = slice(PLANE_BYTES // 4 * plane, PLANE_BYTES // 4 * (plane + planes))
            nc.sync.dma_start(w1_part[k][:].bitcast(I32), w1_words_i[:, row : row + rows, words])

        def load_scales(tile, row):
            for r in range(4):
                nc.sync.dma_start(tile[r:P:32].bitcast(I32), w1_scales_i[r][:, row : row + tile.shape[1]])

        nc.sync.dma_start(offs_sb[:], offs)
        for h, row in enumerate(PAIR_ROWS):
            nc.scalar.dma_start(win_i[row : row + 16, :], x_scales_i[1:, 8 * h : 8 * h + 8, :].rearrange("s b n -> b s n"))
        for q in range(4):
            (nc.sync if q < 2 else nc.scalar).dma_start(win_i[32 * q : 32 * q + 4, :], x_scales_i[0, 4 * q : 4 * q + 4, :])
        nc.sync.dma_start(x_first[:], x_words_i[:, 0, :])
        for tile in [moved_scale] + w_scale[1:]:
            later_scales = tile[:].rearrange("p g n -> p (g n)").bitcast(U32).rearrange("p (a b) -> p a b", b=ZEROS)
            nc.scalar.copy(later_scales, zeros[:].bitcast(U32).unsqueeze(1).to_broadcast(later_scales.shape))
        zero_bias = keep.tile([P, 1], F32, name="zero_bias")
        nc.scalar.activation(zero_bias[:], zero_in[:], RELU)
        nc.sync.dma_start(gate_rows[:4, :], gate[:, 0, :].rearrange("r (h n) -> r h n", h=2))
        load_scales(w_scale[0], 0)
        load_part(0)
        nc.sync.dma_start(x_rest[:], x_words_i[:, 1:, :])

        slot_words = {}

        def gather_bytes(first):
            offsets = offs_sb[:, first // 16 : (first + BYTE_GATHER) // 16]
            nc.vector.tensor_copy(slot_scale[:, first : first + BYTE_GATHER], scale_win[:].indirect(offsets))

        def gather_words(k):
            (s, first, n), at = WORD_GATHERS[k]
            dst = shared.tile([P, n], U32, name="words%d" % k, align_bytes=64, offset=WORDS_AT + at)
            offsets = offs_sb[:, first // 16 : (first + n) // 16]
            nc.vector.tensor_copy(dst[:], x_win[s].bitcast(U32).indirect(offsets))
            for col in range(0, n, C):
                slot_words[s, (first + col) // C] = dst[:, col : col + C]

        for first in range(0, S, BYTE_GATHER):
            gather_bytes(first)
        for k in range(2):
            gather_words(k)
        for q in range(4):
            row = PAIR_ROWS[q // 2] + 8 * (q % 2)
            nc.sync.dma_start(moved_scale[32 * q : 32 * q + 4].bitcast(I32), slot_scale[row : row + 8, :].bitcast(I32))
        load_part(1)
        for pair in (1, 2):
            load_part(pair + 1)
            load_scales(w_scale[pair], 2 * PASSES * pair)
        for r, pos in enumerate((pos1, pos2)):
            nc.sync.dma_start(pos_sb[r][:], pos)
        load_part(5)
        load_part(4)

        half = BLOCKS // 2
        gate_cols = bank(6, [P, half, P], "gate_cols")
        for b in range(half):
            nc.tensor.transpose(gate_cols[:, b, :], gate_rows[:, b * P : (b + 1) * P], ident[:])
        gates = keep.tile([P, 2, BLOCKS], F32, name="gates")
        side = shared.tile([P, BLOCKS], F32, name="side", align_bytes=64, offset=WORDS_AT + WORD_GATHERS[2][1])
        pivot = keep.tile([P, BLOCKS], F32, name="pivot")
        inverse = keep.tile([P, BLOCKS], F32, name="inverse")
        nc.scalar.copy(gates[:].rearrange("p r (h b) -> p (r h) b", h=2), gate_cols[:, :, :4].rearrange("p b k -> p k b"))
        nc.scalar.activation(side[:], gates[:, 1, :], SIGN, bias=TINY / 2)
        for b in range(BLOCKS):
            nc.scalar.activation(pivot[:, b : b + 1], side[:, b : b + 1], IDENTITY, bias=gates[:, 1, b : b + 1], scale=TINY)
        nc.vector.reciprocal(inverse[:], pivot[:])
        for k in range(2, 7):
            gather_words(k)

        hidden = [keep.tile([P, S], F32, name="hidden%d" % j) for j in range(PLANES)]

        def mx_pass(acc, j, e, s, start, stop):
            row = PASSES * e + s
            k = max(k for k, part in enumerate(W1_PARTS) if part[0] <= row < part[0] + part[1] and part[2] <= j)
            at = PLANE_BYTES * (j - W1_PARTS[k][2])
            w_rows = w_scale[e // 2][:, row % (2 * PASSES), :]
            x_rows = slot_scale[:] if s == 0 else moved_scale[:, s - 1, :]
            nc.tensor.matmul_mx(
                out=acc,
                lhsT=w1_part[k][:, row - W1_PARTS[k][0], at : at + PLANE_BYTES].bitcast(FP4X4),
                lhsT_scale=w_rows[:, P * j : P * (j + 1)],
                rhs=slot_words[s, e].bitcast(FP8X4),
                rhs_scale=x_rows[:, e * C : (e + 1) * C],
                start=start,
                stop=stop,
            )

        def relu(j, e, acc):
            nc.scalar.activation(hidden[j][:, e * C : e * C + acc.shape[1]], acc, RELU, bias=zero_bias[:])

        def pair_sums(j, pair, k):
            acc = bank(k, [P, PAIR], "acc")
            for h in range(2):
                for s in range(PASSES):
                    mx_pass(acc[:, h * C : (h + 1) * C], j, 2 * pair + h, s, s == 0, s == PASSES - 1)
            return acc[:]

        first_acc = [bank(j, [P, PAIR], "acc") for j in range(PLANES)]
        def first_pair_pass(s):
            for e in range(2):
                for j in range(PLANES):
                    mx_pass(first_acc[j][:, e * C : (e + 1) * C], j, e, s, s == 0 and e == 0, False)

        first_pair_pass(0)
        ratio_cols = shared.tile([P, BLOCKS], F32, name="ratio_cols", align_bytes=64, offset=WORDS_AT)
        for b in range(BLOCKS):
            nc.scalar.activation(ratio_cols[:, b : b + 1], gates[:, 0, b : b + 1], COPY, scale=inverse[:, b : b + 1])
        ratio = keep.tile([P, T], F32, name="ratio")
        for k in range(2):
            spread = bank(4 + k, [P, half, P], "spread")
            for b in range(half):
                column = ratio_cols[:, half * k + b : half * k + b + 1]
                nc.tensor.transpose(spread[:, b, :], column.to_broadcast([P, P]), ident[:])
            nc.scalar.copy(ratio[:, half * k * P : half * (k + 1) * P], spread[:].rearrange("p b t -> p (b t)"))
        first_pair_pass(1)
        for k in range(7, len(WORD_GATHERS)):
            gather_words(k)
        for j in range(PLANES):
            for e in range(2):
                mx_pass(first_acc[j][:, e * C : (e + 1) * C], j, e, PASSES - 1, False, e == 1)
            relu(j, 0, first_acc[j][:])

        for j, k in ((0, 7), (1, 6), (2, 2)):
            relu(j, 2, pair_sums(j, 1, k))
        last_acc = {(j, e): bank(k, [P, C], "acc") for j, e, k in ((0, 4, 4), (1, 4, 0), (0, 5, 5), (1, 5, 1))}
        for s in (1, 2, 0):
            for j, e in last_acc:
                mx_pass(last_acc[j, e][:], j, e, s, s == 1, s == 0)
        for e in (E - 2, E - 1):
            relu(0, e, last_acc[0, e][:])
            nc.vector.tensor_scalar_max(hidden[1][:, e * C : (e + 1) * C], last_acc[1, e][:], 0.0)
        spans = {0: ((0, T),), 1: ((0, T),), 2: ((SPLIT, T - SPLIT), (0, SPLIT)), 3: ((SPLIT, T - SPLIT), (0, 256), (256, 256))}
        scaled = {
            (j, first): keep.tile([P, n], F32, name="scaled%d_%d" % (j, first)) for j in spans for first, n in spans[j]
        }
        plain = [
            keep.tile([P, T], F32, name="plain0"),
            shared.tile([P, T], F32, name="plain1", align_bytes=64, offset=W1_AT[4]),
            shared.tile([P, SPLIT], F32, name="plain2", align_bytes=64, offset=W1_AT[5]),
            keep.tile([P, SPLIT], F32, name="plain3"),
        ]
        summed = {j: keep.tile([P, T], F32, name="summed%d" % j) for j in (2, 3)}

        def window(j, r, first, n):
            return hidden[j][:].indirect(pos_sb[r][:, first // 16 : (first + n) // 16])

        def gather_scaled(j, first):
            dst = scaled[j, first][:]
            n = dst.shape[1]
            nc.vector.tensor_tensor(dst, window(j, 0, first, n), ratio[:, first : first + n], ALU.mult)

        def gather_plain(j, first, n):
            nc.scalar.activation(plain[j][:, first : first + n], window(j, 1, first, n), COPY)

        def gather_sum(dst, j, first, other):
            nc.vector.tensor_tensor(dst, window(j, 1, first, other.shape[1]), other, ALU.add)

        gather_scaled(0, 0)
        gather_plain(0, 0, T)
        relu(2, 4, pair_sums(2, 2, 7))
        gather_scaled(1, 0)
        second_pair_plane3 = pair_sums(3, 1, 3)
        gather_plain(1, 0, T)
        relu(3, 2, second_pair_plane3)

        w2_scales_i = w2_scales.bitcast(I32).rearrange("s (q r) n -> r q (s n)", r=4)
        for r in range(4):
            nc.sync.dma_start(w_scale[0][4 + r : P : 32, 0, :N].bitcast(I32), w2_scales_i[r])
        w2_sb = shared.tile([P, N], I32, name="w2_sb", align_bytes=64, offset=W1_AT[0])
        nc.sync.dma_start(w2_sb[:], w2_words[0].rearrange("p n d -> p (n d)").bitcast(I32))

        c_tok = [keep.tile([P, 2, P, 2], BF16, name="c_tok%d" % block, align_bytes=64) for block in range(BLOCKS)]

        turned = [bank(k, [P, PLANES, P], "turned") for k in (0, 1, 4, 5, 6, 3)]

        def turn(j, block, terms):
            for k, term in enumerate(terms):
                nc.tensor.matmul(turned[block][:, j, :], term, ident[:], start=k == 0, stop=k == len(terms) - 1, is_transpose=True)

        def turn_both(j, block):
            first = max(first for first, n in spans[j] if first <= block * P)
            terms = [scaled[j, first][:, block * P - first : (block + 1) * P - first], plain[j][:, block * P : (block + 1) * P]]
            turn(j, block, terms)

        def turn_summed(j, block):
            turn(j, block, [summed[j][:, block * P : (block + 1) * P]])

        def round_views(block):
            return c_tok[block][:], turned[block][:].rearrange("p j (m u v) -> p u (j m) v", u=2, v=2)

        def round_on_scalar(block):
            nc.scalar.activation(*round_views(block), COPY, scale=pivot[:, block : block + 1])

        def round_on_vector(block):
            nc.vector.tensor_scalar_mul(*round_views(block), pivot[:, block : block + 1])

        grouped, c_words, c_scale = {}, {}, {}

        def turn_back(first, n, copy, k):
            back = bank(k, [P, n // P, 2, P], "back")
            for b in range(n // P):
                for u in range(2):
                    words = c_tok[first // P + b][:, u, :, :].rearrange("p m v -> p (m v)").bitcast(F32)
                    nc.tensor.transpose(back[:, b, u, :], words, ident[:])
            grouped[first] = keep.tile([P, 4 * n], BF16, name="grouped%d" % first, align_bytes=64)
            copy(
                grouped[first][:].bitcast(F32).rearrange("p (b t u) -> p b t u", t=P, u=2),
                back[:].rearrange("p b u t -> p b t u"),
            )

        def quantize(first, n):
            c_words[first] = keep.tile([P, n], U32, name="c_words%d" % first, align_bytes=64)
            c_scale[first] = keep.tile([P, n], U8, name="c_scale%d" % first, align_bytes=64)
            nc.vector.quantize_mx(out=c_words[first][:].bitcast(FP8X4), scales=c_scale[first][:], in_=grouped[first][:])

        def project(first, n, copy, k):
            projected = bank(k, [P, n], "projected")
            nc.tensor.matmul_mx(
                out=projected[:],
                lhsT=w2_sb[:].bitcast(FP8X4),
                lhsT_scale=w_scale[0][4:P, 0, :N],
                rhs=c_words[first][:].bitcast(FP8X4),
                rhs_scale=c_scale[first][:],
                start=True,
                stop=True,
            )
            res = keep.tile([P, n], F32, name="res%d" % first)
            copy(res[:], projected[:])
            nc.sync.dma_start(out[:, first : first + n], res[:])

        for block in range(BLOCKS - 1):
            turn_both(0, block)
        relu(3, 4, pair_sums(3, 2, 2))
        turn_both(0, BLOCKS - 1)
        for block in range(BLOCKS):
            turn_both(1, block)
        gather_scaled(2, SPLIT)
        gather_scaled(2, 0)
        gather_sum(summed[2][:, SPLIT:], 2, SPLIT, scaled[2, SPLIT][:])
        gather_scaled(3, 0)
        gather_scaled(3, SPLIT)
        gather_scaled(3, 256)
        for j, first in ((2, 0), (3, 0), (2, 256), (3, 256)):
            gather_plain(j, first, 256)
        for first in (512, 640):
            gather_sum(summed[3][:, first : first + P], 3, first, scaled[3, SPLIT][:, first - SPLIT : first - SPLIT + P])
        for block in (4, 5):
            turn_summed(2, block)
        for j, blocks in ((2, (0, 1)), (3, (0, 1)), (2, (2, 3)), (3, (2, 3))):
            for block in blocks:
                turn_both(j, block)
        for block in (4, 5):
            turn_summed(3, block)

        on_scalar, on_vector = nc.scalar.copy, nc.vector.tensor_copy
        for block in (0, 1, 2, 5):
            round_on_scalar(block)
        for block in (3, 4):
            round_on_vector(block)
        turn_back(*CHUNKS[0], on_vector, 7)
        turn_back(*CHUNKS[1], on_scalar, 2)
        turn_back(*CHUNKS[2], on_vector, 0)
        turn_back(*CHUNKS[3], on_scalar, 1)
        for chunk in CHUNKS:
            quantize(*chunk)
        for chunk, copy, k in zip(CHUNKS, (on_scalar, on_scalar, on_vector, on_vector), (4, 5, 6, 3)):
            project(*chunk, copy, k)
